import numpy as np, ml_dtypes
CORES = [113,118,241,246]
N = 4
BF = ml_dtypes.bfloat16
def gentries(a):
    return np.ascontiguousarray(a.reshape(8, 16, -1).transpose(0, 2, 1)).reshape(8, -1)
def gtable(e):
    e = np.asarray(e); return np.ascontiguousarray(e.reshape(8, -1, 16).transpose(0, 2, 1)).reshape(128, -1).astype(np.int32)
M, MB, Q, BASE, L, LA, T, C = 2048, 11, 1152, 1024, 256, 64, 4, 12
def boxes(rng):
    c = rng.integers(-255, 256, (2, N, 8, 8, M))
    return np.concatenate([np.minimum(c[0], c[1]), -np.maximum(c[0], c[1])], axis=2)
def tags(rng):
    u = rng.integers(0, 20, (N, 8, 16, BASE))
    return (u >= 8).astype(np.int64) + (u >= 15)
def grow(rng, fill):
    tag = tags(rng); name = np.where(tag == 0, rng.integers(1, M, tag.shape), rng.integers(1, BASE, tag.shape))
    return np.where(rng.random(tag.shape) < fill, name + M * tag, 0)
def starts(rng):
    v = rng.integers(1, BASE, (N, 8, T, L)); few = rng.integers(1, BASE, (N, 8, T, 12))
    return np.where(rng.random(v.shape) < 0.3, np.take_along_axis(few, rng.integers(0, 12, v.shape), 3), v)
def pack(R, e, x, v):
    return {"rg": R.reshape(N, 128, M).astype(np.float32).astype(BF), "nd": np.ascontiguousarray(e.reshape(N, 128, BASE)).astype(np.int32),
            "z": np.concatenate([x, -x], axis=2).reshape(N, 128, L).astype(np.float32).astype(BF), "vs": np.stack([gtable(a.reshape(8, -1)) for a in v])}
def setup_inputs(rng):
    fill = rng.choice(np.array([0.0, 0.3, 0.5, 0.7, 0.85, 0.85, 0.95, 1.0]), (N, 8, 1, BASE))
    return pack(boxes(rng), grow(rng, fill), rng.integers(-255, 256, (N, 8, 8, L)), starts(rng))
def setup_inputs_spread(rng):
    R = np.floor(511 * rng.random((N, 8, 16, M)) ** rng.choice(np.array([0.5, 1.0, 2.0, 4.0, 4.0]), (N, 8, 1, M))).astype(np.int64) - 255
    x = np.floor(511 * rng.random((N, 8, 8, L)) ** rng.choice(np.array([0.5, 1.0, 2.0]), (N, 8, 1, L))).astype(np.int64) - 255
    tag = tags(rng); u = rng.random(tag.shape)
    name = 1 + np.where(tag == 0, np.floor((M - 1) * u ** 3), np.floor((BASE - 1) * u ** 2)).astype(np.int64)
    e = np.where(rng.random(tag.shape) < rng.choice(np.array([0.2, 0.5, 0.8, 0.95, 1.0]), (N, 8, 1, BASE)), name + M * tag, 0)
    return pack(R, e, x, 1 + np.floor((BASE - 1) * rng.random((N, 8, T, L)) ** 2).astype(np.int64))
def setup_inputs_ties(rng):
    c = rng.integers(-200, 201, (2, 8, 8, 5)); lo = np.minimum(c[0], c[1]); hi = np.maximum(c[0], c[1])
    tm = np.broadcast_to(np.concatenate([lo, -hi], axis=1), (N, 8, 16, 5))
    R = np.take_along_axis(tm, rng.integers(0, 5, (N, 8, 1, M)), 3)
    R = R + rng.integers(-1, 2, R.shape) * (rng.random(R.shape) < 0.02)
    k = rng.integers(0, 5, (N, 8, 1, L))
    x = np.where(rng.random((N, 8, 8, L)) < 0.5, np.take_along_axis(np.broadcast_to(lo, (N, 8, 8, 5)), k, 3), np.take_along_axis(np.broadcast_to(hi, (N, 8, 8, 5)), k, 3))
    x = x + rng.integers(-1, 2, x.shape)
    return pack(R, grow(rng, rng.choice(np.array([0.3, 0.6, 0.85, 1.0]), (N, 8, 1, BASE))), x, starts(rng))
def setup_inputs_ends(rng):
    F = np.array([1, 2, M - 2, M - 1]); B = np.array([3, 6, M - 5, M - 10]); B3 = (B[:, None] + np.arange(3)).reshape(-1)
    kind = rng.choice(np.array([0, 0, 1, 1, 2, 2, 3, 4, 4]), (N, 8, M)); u = rng.integers(15 - C, 18 - C, (N, 8, M))
    off = rng.random((N, 8, M)) < 0.25; off[:, :, F] = False; u[:, :, F] = 16 - C
    kind[:, :, B3] = 0; off[:, :, B3] = False
    for g in range(8):
        kind[:, g, F] = 1 + (g & 1)
        if (g >> 1) & 1 == 0: off[:, g, 1:3] = True
    few = np.where((np.arange(8)[:, None] + rng.integers(0, 8, (N, 8, 1, M))) % 8 < u[:, :, None, :], 255, -255); k = kind[:, :, None, :]
    any_ = np.where(rng.random((N, 8, 16, M)) < 0.6, -255, 255)
    low = np.where(k == 0, -255, np.where(k == 2, few, np.where(k == 4, any_[:, :, :8], 255)))
    neg = np.where(k == 0, -255, np.where(k == 1, few, np.where(k == 4, any_[:, :, 8:], 255)))
    R = np.concatenate([low, neg], axis=2)
    at = np.where(kind == 2, 8, 0) + rng.integers(0, 8, (N, 8, M))
    off[:, :, B3] = False
    R = np.where((np.arange(16)[:, None] == at[:, :, None, :]) & off[:, :, None, :], R - np.sign(R), R)
    w = rng.choice(np.array([0, 0, 0, 1, 1, 1, 2, 3]), (N, 8, 1, L)); w[..., 0] = 1; w[..., 1] = 0; w[..., L - 2] = 1; w[..., L - 1] = 0
    r = np.where(rng.random((N, 8, 8, L)) < 0.5, -255, 255); one = np.where(np.arange(8)[:, None] == rng.integers(0, 8, (N, 8, 1, L)), -255, 255)
    x = np.where(w == 0, 255, np.where(w == 1, -255, np.where(w == 2, r, one)))
    tag = tags(rng); e1 = rng.choice(F, tag.shape); e2 = rng.choice(np.array([1, 2, BASE - 2, BASE - 1]), tag.shape); h = rng.random(tag.shape) < 0.5
    name = np.where(tag == 0, np.where(h, e1, rng.integers(1, M, tag.shape)), np.where(h, e2, rng.integers(1, BASE, tag.shape)))
    p = rng.random(tag.shape); e = np.where(p < 0.42, 0, np.where(p < 0.66, 2 * M + BASE - 1, name + M * tag))
    for c in (1, BASE - 1):
        for i, n in ((0, M - 1), (1, M - 2), (2, M + BASE - 2), (13, M + 2), (14, 2), (15, 1)): e[:, :, i, c] = n
    few_nodes = np.array([3, 4, BASE - 4, BASE - 3])
    for j in range(4):
        e[:, :, :, few_nodes[j]] = 0
        for i, n in ((0, B[j] + 2), (7, B[j] + 1), (15, B[j])): e[:, :, i, few_nodes[j]] = n
    p = rng.random((N, 8, T, L)); v = np.where(p < 0.33, 1, np.where(p < 0.66, BASE - 1, rng.integers(1, BASE, p.shape)))
    v[..., 0] = 1; v[..., 1] = BASE - 1; v[..., L - 2] = 1; v[..., L - 1] = BASE - 1
    v[..., L - 10:L - 2] = np.tile(few_nodes, 2)
    return pack(R, e, x, v)
def pairs(rng, mode, P):
    if mode in (0, 1):
        a = np.full(LA, P[0]); b = np.full(LA, P[1])
        if mode == 1: j = int(rng.choice(np.array([0, LA - 1, rng.integers(0, LA)]))); a[j] = P[2]; b[j] = P[3]
        return a, b
    a = P[:LA].copy(); b = P[LA:].copy()
    if mode == 3: b[:] = P[LA]
    if mode == 4: b = P[1:LA + 1].copy()
    if mode == 5: a[LA - 1] = a[0]; b[LA - 1] = b[0]
    return a, b
def staged(rng, mode, tight, fill):
    R = boxes(rng); e = grow(rng, fill); x = rng.integers(-255, 256, (N, 8, 8, L)); v = starts(rng); P0 = BASE - 2 * T * LA
    for g in range(8):
        if mode[0, g] < 0: continue
        x[:, g] = rng.integers(-100, 101, (N, 8, L))
        for t in range(T):
            R[:, g, :, P0 + 2 * t * LA:P0 + 2 * (t + 1) * LA] = 40 * t - 255; R[:, g, :, M - (t + 1) * LA:M - t * LA] = 40 * t - 255
        R[:, g, :, Q:Q + 16] = 255; R[:, g, :8, Q + 8:Q + 16] = -255
        for q in range(N):
            for t in range(T):
                P = P0 + 2 * t * LA + rng.permutation(2 * LA); a, b = pairs(rng, int(mode[q, g]), P); sh = (16, LA); pad = Q + rng.integers(0, 16, sh)
                vals = np.zeros(sh, np.int64); nf = rng.choice(np.array([0, 1, 2, 5, 13]), LA) if tight and t % 2 == 0 else np.full(LA, 13)
                vals[0] = M + b
                if t % 2 == 0:
                    vals[2] = np.where(rng.random(LA) < 0.5, M + P0 + 2 * (t + 1) * LA - 1, 0); ty = rng.integers(0, 6, (1, LA))
                    if mode[q, g] == 2: vals[2, 0] = 0; nf[0] = 13; ty[0, 0] = 2
                    row = np.where(ty == 5, rng.integers(0, 5, sh), ty)
                    bf = np.where(row == 0, 0, np.where(row == 1, rng.integers(1, BASE, sh) + M * rng.integers(1, 3, sh), np.where(row == 2, M + P[rng.integers(0, 2 * LA, sh)],
                         np.where(row == 3, Q + rng.integers(0, 8, sh), Q + 8 + rng.integers(0, 8, sh)))))
                else:
                    c = M - 1 - np.arange(LA) - t * LA; vals[1] = c; vals[2] = np.where(rng.random(LA) < 0.5, c, 0)
                    room = rng.choice(np.array([0, 1, 2, 16]) if tight else np.array([1, 2, 9, 16]), (1, LA))
                    bf = np.where(np.argsort(rng.random(sh), axis=0) < room, 0, pad)
                vals[3:] = np.where(np.arange(3, 16)[:, None] < 16 - nf, pad[3:], 0)
                if t % 2 == 1: vals[3:5] = np.where(rng.random(LA) < 0.3, c, 0)
                ac = np.take_along_axis(vals, np.argsort(rng.random(sh), axis=0), 0)
                ev = e[q, g]; ev[:, b] = bf; ev[:, a] = ac
                v[(q - t) % N, g, t, :LA] = a
    return pack(R, e, x, v)
def setup_inputs_crowd(rng):
    mode = rng.integers(0, 6, (N, 8)); mode[0] = rng.permutation(np.array([0, 0, 1, 1, 2, 3, 4, 5])); mode[1] = 2; mode[1, rng.integers(0, 8)] = 5; mode[N - 1] = 2
    return staged(rng, mode, False, 0.6)
def setup_inputs_corners(rng):
    mode = rng.integers(0, 6, (N, 8)); mode[0] = rng.permutation(np.array([0, 1, 2, 2, 3, 4, 4, 5])); mode[:, rng.permutation(8)[:2]] = -1
    return staged(rng, mode, True, rng.choice(np.array([0.0, 0.06, 0.5, 0.94, 0.94, 1.0]), (N, 8, 1, BASE)))
def check_inputs(d):
    bad = []
    for k, lo, hi in (("rg", -255, 255), ("z", -255, 255), ("nd", 0, 2 * M + BASE - 1), ("vs", 1, BASE - 1)):
        a = np.asarray(d[k]).astype(np.float64)
        if not np.all((a >= lo) & (a <= hi)): bad.append("range of " + k)
        elif np.any(a != np.floor(a)): bad.append("whole numbers of " + k)
    a = np.asarray(d["nd"]).astype(np.int64); n = a & (M - 1)
    if np.any((a >= M) & ((n < 1) | (n >= BASE))): bad.append("names of nd")
    a = np.asarray(d["z"]).astype(np.float32).reshape(-1, 2, 8, L)
    if np.any(a[:, 0] != -a[:, 1]): bad.append("halves of z")
    return bad
def take(a, i):
    return np.take_along_axis(a, i[:, :, None, :], 3)
def pick(a, i):
    return np.take_along_axis(a, i.reshape(N, 8, -1), 2).reshape(i.shape)
def reference(rg, nd, z, vs):
    R = rg.astype(np.float32).astype(np.int16).reshape(N, 8, 16, M); X = z.astype(np.float32).astype(np.int16).reshape(N, 8, 16, L)
    W = np.stack([gentries(a) for a in vs]).astype(np.int64).reshape(N, 8, T, L)
    D = np.zeros((N, 8, 16, Q), np.int64); D[..., :BASE] = nd.reshape(N, 8, 16, BASE)
    G = np.zeros((N, 8, 3, L), np.int64); A = np.zeros(N, np.int64); LOW = -2 ** 40
    for t in range(T):
        home = (np.arange(N) - t) % N
        x = X[home]; g = G[home]; need = (C - (A[home] & 1)).reshape(N, 1, 1, 1); S = np.add.reduce(R, axis=2, dtype=np.int64)
        n = np.stack([np.add.reduce(x >= take(R, g[:, :, k]), axis=2, dtype=np.int64) for k in range(3)], axis=2)
        keep = (g > 0) & (n >= need); g = np.where(keep, g, 0); gs = np.where(keep, pick(S, g), -2 ** 20)
        h = np.zeros_like(g); v = W[home][:, :, t]
        for s in (2, 1, 0):
            e = take(D, v); nm = e & (M - 1); tg = e >> MB
            n = np.add.reduce(x[:, :, :, None, :] >= take(R, nm.reshape(N, 8, 16 * L)).reshape(N, 8, 16, 16, L), axis=2, dtype=np.int64)
            ok = (e > 0) & (n >= need); score = pick(S, nm)
            for k in range(s + 1):
                best = np.max(np.where(ok & (tg == k), score * M + (M - 1 - nm), LOW), axis=2)
                new = (best > LOW) & ((best >> MB) > gs[:, :, k])
                g[:, :, k] = np.where(new, M - 1 - (best & (M - 1)), g[:, :, k]); gs[:, :, k] = np.where(new, best >> MB, gs[:, :, k]); h[:, :, k] = np.where(new, v, h[:, :, k])
            if s > 0: v = np.where(g[:, :, s] > 0, g[:, :, s], v)
        even = t % 2 == 0
        a = h[:, :, 1 if even else 0, :LA]; b = g[:, :, 1, :LA] if even else v[:, :, :LA]
        ea = take(D, a); eb = take(D, b)
        ask = (a > 0) & (a != b) & np.any((ea if even else eb) == 0, axis=2)
        a1 = a[:, :, :, None]; b1 = b[:, :, :, None]; a2 = a[:, :, None, :]; b2 = b[:, :, None, :]
        meet = ((a1 == a2) | (a1 == b2) | (b1 == a2) | (b1 == b2)) & ask[:, :, None, :] & np.tri(LA, LA, -1, dtype=bool)
        act = ask & ~np.any(meet, axis=3); A[home] = np.add.reduce(act, axis=(1, 2), dtype=np.int64)
        q, p, l = np.nonzero(act); al = a[q, p, l]; bl = b[q, p, l]
        if even:
            nb = eb & (M - 1); full = eb > 0
            go = full & (pick(R[:, :, t], nb) >= x[:, :, t, None, :LA]); stay = full & ~go & (pick(R[:, :, 8 + t], nb) >= x[:, :, 8 + t, None, :LA])
            strad = full & ~go & ~stay; number = np.add.accumulate(strad, axis=2, dtype=np.int64)
            free = ea == 0; place = np.add.accumulate(free, axis=2, dtype=np.int64) - free
            put = strad & (number < np.add.reduce(free, axis=2, dtype=np.int64)[:, :, None, :])
            new = BASE + LA * (t >> 1) + np.arange(LA)
            ya = np.where(free & (place == 0), M + new, ea)
            for j in range(16):
                ya = np.where(free & put[:, :, j:j + 1] & (place == number[:, :, j:j + 1]), eb[:, :, j:j + 1], ya)
            yb = np.where(go | put, 0, eb); yw = np.where(go, eb, 0)
            D[q, p, :, new[l]] = yw[q, p, :, l]
            cut = R[q, p, :, bl]; half = cut.copy(); half[:, t] = x[q, p, t, l]; cut[:, 8 + t] = x[q, p, 8 + t, l]
            R[q, p, :, new[l]] = half; R[q, p, :, bl] = cut
        else:
            e0 = g[:, :, 0, None, :LA]; free = eb == 0; place = np.add.accumulate(free, axis=2, dtype=np.int64) - free
            ya = np.where(ea == e0, 0, ea); yb = np.where(free & (place == 0), e0, eb)
        D[q, p, :, al] = ya[q, p, :, l]; D[q, p, :, bl] = yb[q, p, :, l]
        G[home] = g
    return {"yn": D.reshape(N, 128, Q).astype(np.float32), "yr": R[..., :Q].reshape(N, 128, Q).astype(np.float32).astype(BF), "yg": g.reshape(N, 8, 3 * L).astype(np.float32)}

@@ -1,0 +1,694 @@
+from concourse.mybir import AluOpType, AxisListType, ActivationFunctionType
+
+ALU, ACT = AluOpType, ActivationFunctionType
+
+NR, NT = 4, 4
+B = float(2 ** 24)
+NONE = -4094.0 * 2048.0
+RND = 1.5 * 2.0 ** 34
+RND2 = 1.5 * 2.0 ** 24
+S3 = ((0, 1024, "S"), (1024, 1536, "S"), (1536, 2048, "S"))
+S4 = tuple((512 * j, 512 * j + 512, "S") for j in range(4))
+E1 = (S4[0], (512, 1024, "E")) + S4[2:]
+OPT = dict(chunks=(S4, S4), sign=((), (1, 3)), en="H", yc="E", war=True, eng=8)
+COST = dict(c=1.04, g=1.56, sc=3.8, pe=0.52, lat=70.0, look=0.0, rem=2500.0, lean=200.0)
+
+URGE = {2: 50, 3: 60, 4: -130, 5: 50, 6: -5, 7: 15, 8: -15, 12: -45, 13: 20, 14: 5, 16: 35, 17: 20, 18: -5, 19: 5, 20: 90, 23: -5, 24: 110, 25: -50,
+        26: 15, 28: 10, 29: -115, 30: 120, 31: 5, 32: 45, 33: 25, 34: 30, 35: 15, 36: -100, 37: 40, 38: 65, 39: -10, 40: -10, 41: 10, 42: -10,
+        43: 95, 44: 35, 45: 5, 47: 20, 48: 20, 49: 30, 50: 5, 52: -20, 55: 35, 56: 5, 57: 35, 58: 45, 61: -20, 62: -15, 63: 60, 64: -20, 65: 5,
+        66: 20, 67: -5, 68: -150, 69: 65, 70: -40, 71: -15, 72: -15, 73: 10, 74: 40, 76: 30, 77: -10, 78: -20, 79: 5, 80: -35, 81: -15, 82: -15,
+        83: -5, 84: -25}
+f32, b16, f16, i32, u16 = "float32", "bfloat16", "float16", "int32", "uint16"
+TILE = {}
+
+
+def _decl(where, dtype, halves=False, **kw):
+    for k, n in kw.items():
+        for x in (("0", "1") if halves else ("",)):
+            TILE[k + x] = (where, [128, n], dtype)
+
+
+ZERO = dict(YV=512, Y0=128, Y1=128, YC0=128, YC1=128, VM0=32, VM1=32, HM=16)
+ZERO2 = dict(YG0=256, YG1=256, YGC0=256, YGC1=256, YA=128, YAC=128, NM0=32, NM1=32, NZ0=32, NZ1=32, MN=16, BASE=32, GN0=32, ABM=16,
+             SG00=64, SG01=64, SG10=64, SG11=64, SG20=64, SG21=64, SK0=16, SK1=16, SK2=16, RST8=512)
+_decl("sbuf", f32, **ZERO)
+_decl("sbuf", f32, **ZERO2)
+_decl("psum", f32, pX0=512, pX1=512, pB=512, pV0=512, pV1=512, pM0=512, pM1=512, pA=512)
+_decl("sbuf", b16, True, RG=2048, CM=2048, RGG=384, CMG=384, U=128, W=128, PEN=128, PENG=32)
+_decl("sbuf", b16, R0=5248, R1=5248, R2=5248, XX0=512, XX1=512, XX2=512, XX3=512, ONE=512, REP=2048, BJ=2048, ID=128, NID=128, BO=128,
+      BO24=32, UW=256, CST=384, CG=32, TRI=128, NTRI=128, TP=128, TN=128, DG=160, SL0=160, SL8=160, SL2=160, SL10=160, MASK=640, R16B=128,
+      CSEL=256, FR=64, NGS=128, STR=64, NB=64, PL=64, EHI=64, ELO=64, ACB=16, RC=64, RH=64, XC=64, XH=64)
+_decl("sbuf", f16, True, EH=384)
+_decl("sbuf", f16, OTH=256, OWN=256, G0X=128)
+_decl("sbuf", f32, True, SC=384, EN=128, K=32, KH=32, HI=32, NW=32, DF=32, FX=16, LO=32)
+_decl("sbuf", f32, D0=1344, D1=1344, D2=1344, D3=1344, D4=1344, ID32=128, R16=128, RST=384, DV=16, KC=16,
+      YVC=512, VS32=64, VL=64, VV0=48, VV1=48, VV2=48, VV3=48, SV1=48, SV2=48, SV3=48,
+      GM10=64, GM11=64, GM20=64, GM21=64, GM30=64, GM31=64, KA0=4, KA1=4, KA2=4, KA3=4, GN1=32, YO=256, COL=16, COLI=32,
+      EA=64, EB=64, AB=16, Q1=16, Q2=16, ACR=32, ADD0=32, ADD2=32, DUM=32, XD=32, OF=32,
+      AS=16, EBN=64, PUT=64, EP=64, P0=64, NE=64, NV=128, ZA=1024, ZS=1024, RES=64, RM=64, KEEP=16)
+_decl("sbuf", i32, ND=1024, VS=64, PI=16, IT=128, IT2=128)
+_decl("sbuf", u16, True, EU=128, VO=16, GU=32)
+_decl("sbuf", u16, VS16=64, AO=16, SO=4, GO=4, EX=16, RA=2, OU=32)
+
+MSGS = ["xx%d" % t for t in (1, 2, 3)] + ["vv%d" % t for t in (1, 2, 3)] + ["gm%d%d" % (t, h) for t in (1, 2, 3) for h in (0, 1)] + \
+       ["ka%d" % t for t in (1, 2, 3)]
+SEMAPHORES = ["eV", "eS", "eP", "eG", "sent", "ldz", "ldv", "ldn0", "ldn1", "ldr0", "ldr1", "out", "cd1", "cd2", "cd3", "cd4", "cr1", "cr2"] + MSGS
+WIDE = {f32: 4, i32: 4, b16: 2, u16: 2, f16: 2}
+PLACE, SCRATCH = {}, {}
+for _k, (_w, _s, _d) in TILE.items():
+    _b = _k if _w == "psum" else "all_" + _d
+    _at = SCRATCH[_b][1][1] if _b in SCRATCH else 0
+    PLACE[_k] = (_b, _at)
+    SCRATCH[_b] = (_w, [128, _at + -(-_s[1] // 16) * 16], _d)
+
+
+def A(name, c0=0, c1=None, step=1, p0=0, p1=128):
+    if c1 is None:
+        c1 = TILE[name][1][1]
+    return ("ap", name, c0, c1, step, p0, p1)
+
+
+def IND(win, off):
+    return ("ind", win, off)
+
+
+def _n(x):
+    return (x[2][3] - x[2][2]) * 16 if x[0] == "ind" else len(range(x[2], x[3], x[4]))
+
+
+def _isv(x):
+    return isinstance(x, tuple) and x[0] in ("ap", "ind")
+
+
+def program():
+    ops, part = [], [0]
+    C, O = COST, OPT
+
+    def add(eng, calls, cost, w, r, **kw):
+        ops.append(dict(eng=eng, calls=calls, cost=cost, w=w, r=r, part=part[0], **kw))
+
+    def comp(eng, meth, args, kw=None):
+        w, r = [], []
+        for i, x in enumerate(list(args) + list((kw or {}).values())):
+            if _isv(x):
+                (w if i == 0 else r).append(x[1] if x[0] == "ind" else x)
+                if x[0] == "ind":
+                    r.append(x[2])
+        vs = [x for x in args if _isv(x)]
+        n = max(_n(x) for x in vs)
+        if eng == "G":
+            cost = 170 + 2 * n * C["c"]
+        elif args[0][0] == "ind":
+            cost = 50 + n * C["sc"] * C["c"]
+        elif any(x[0] == "ind" for x in vs):
+            cost = (50 if eng == "V" else 65) + n * C["g"] * C["c"]
+        elif eng == "S":
+            cost = 65 + n * C["c"]
+        else:
+            f = 0.5 if all(WIDE[TILE[x[1]][2]] == 2 for x in vs if _n(x) > 1) else 1.0
+            if meth == "tensor_tensor" and all(TILE[x[1]][0] == "sbuf" for x in vs[1:]):
+                f = 2.0
+            cost = 20 + max(64, n * f) * C["c"]
+        add(eng, [(meth, args, kw or {})], cost, w, r)
+
+    def ts(out, in0, s1, op0, s2=None, op1=None):
+        comp("V", "tensor_scalar", [out, in0, s1, s2, op0] + ([op1] if op1 is not None else []))
+
+    def tt(out, a, b, op):
+        comp("V", "tensor_tensor", [out, a, b, op])
+
+    def either(func, a, kw):
+        first = ops.pop()
+        comp("S", "activation", [first["calls"][0][1][0], a, func], kw)
+        other = ops.pop()
+        first["r"] = first["r"] + [x for x in other["r"] if x not in first["r"]]
+        first["alt"] = {"V": (first["calls"], first["cost"]), "S": (other["calls"], other["cost"])}
+        ops.append(first)
+
+    def cp(out, a, eng="V"):
+        if eng != "S":
+            comp("V", "tensor_copy", [out, a])
+        if eng == "E":
+            either(ACT.Copy, a, {})
+        if eng == "S":
+            comp("S", "activation", [out, a, ACT.Copy])
+
+    def aff(out, a, scale, bias=None):
+        if bias is None:
+            ts(out, a, scale, ALU.mult)
+            either(ACT.Copy, a, {"scale": scale})
+        else:
+            ts(out, a, scale, ALU.mult, bias, ALU.add)
+            either(ACT.Identity, a, {"scale": scale, "bias": bias})
+
+    def ms(out, v, free=True):
+        comp("V", "memset", [out, v])
+        if free and _n(out) <= 512:
+            either(ACT.Copy, A("ONE", 0, _n(out), 1, out[5], out[6]), {"scale": v})
+
+    def iota(out, pat, base, cm):
+        kw = {} if TILE[out[1]][2] == i32 else {"allow_small_or_imprecise_dtypes": True}
+        comp("G", "iota", [out, pat, base, cm], kw)
+
+    def fill(out, v):
+        iota(out, [[0, _n(out)]], v, 0)
+
+    def sel(out, a, pat, op, base, cm, other=0.0):
+        comp("G", "affine_select", [out, a, pat, op, other, base, cm])
+
+    def mm(lst):
+        w, r, cost = [], [], 0.0
+        for o, l, x, _, _ in lst:
+            w.append(o)
+            r += [l, x]
+            cost += max(min(64, _n(l)), _n(x)) * (4 if TILE[x[1]][2] == f32 else 1) * C["pe"]
+        add("P", [("matmul", list(m), {}) for m in lst], cost + 30, w, r)
+
+    def dma(q, out, in_, sem, lat):
+        add(q, [("dma_start", [out, in_], {})], 60.0, [out] if out[0] == "ap" else [], [in_] if in_[0] == "ap" else [], sem=sem, lat=lat)
+
+    def send(src, dst, hop, sem, more=0.0):
+        add("G", [("remote", [dst, src, hop, sem], {})], 800.0, [], [src], sem="sent", lat=C["rem"] + more)
+        add("R", [], 0.0, [dst], [], sem=sem, lat=C["rem"], after=len(ops) - 1)
+
+    def turn(y, yc, nq, k, out, ps, plus=0.0):
+        mm([(A(ps, 0, 64 * nq), A("R16"), A(y, 0, 64 * nq), True, True)])
+        cp(A(yc, 0, 64 * nq), A(ps, 0, 64 * nq), O["yc"])
+        if plus:
+            ts(out, IND(A(yc, 0, 128 * k), A("GO", 0, k)), plus, ALU.add)
+        else:
+            cp(out, IND(A(yc, 0, 128 * k), A("GO", 0, k)), "E" if TILE[out[1]][2] == f32 else "V")
+
+    dma("Y", A("VS"), ("hbm", "vs", None), "ldv", 1800)
+    dma("Y", A("XX0", 0, 256), ("hbm", "z", None), "ldz", 1900)
+    dma("S", A("ND", 0, 512), ("hbm", "nd", (0, 512)), "ldn0", 3000)
+    dma("Y", A("ND", 512, 1024), ("hbm", "nd", (512, 1024)), "ldn1", 3200)
+    dma("S", A("R0", 0, 1152), ("hbm", "rg", (0, 1152)), "ldr0", 3800)
+    dma("Y", A("R0", 1152, 2048), ("hbm", "rg", (1152, 2048)), "ldr1", 4300)
+    ms(A("ONE"), 1.0, False)
+    iota(A("PI", 0, 1), [[0, 1]], 0, 1)
+    iota(A("IT"), [[-1, 128]], 128, 1)
+    iota(A("COLI"), [[1, 32]], 0, 0)
+    sel(A("ID"), A("ONE", 0, 128), [[-1, 128]], ALU.is_equal, 0, 1)
+    sel(A("BO"), A("ONE", 0, 128), [[-16, 8], [0, 16]], ALU.is_ge, 0, 1)
+    sel(A("BO"), A("BO"), [[16, 8], [0, 16]], ALU.is_ge, 15, -1)
+    for j in range(4):
+        sel(A("REP", 512 * j, 512 * j + 512), A("ONE"), [[-1, 32], [0, 16]], ALU.is_equal, -32 * j, 1)
+    ts(A("IT2"), A("IT"), 15, ALU.bitwise_and)
+    ts(A("R16"), A("IT2"), 0.0, ALU.is_equal)
+    cp(A("ID32"), A("ID"), "E")
+    aff(A("UW", 0, 128), A("ID"), -B)
+    aff(A("UW", 128, 256), A("ID"), B)
+    aff(A("NID"), A("ID"), -1.0)
+    for k in range(3):
+        aff(A("BO24", 8 * k, 8 * k + 8), A("BO", 0, 128, 16), 2048.0)
+    cp(A("BO24", 24, 32), A("BO", 0, 128, 16), "E")
+    ms(A("CST", 0, 128), 0.0)
+    ms(A("CST", 128, 384), -B / 128)
+    ms(A("RST"), 0.0)
+    ms(A("RST", 0, 384, 16), -4 * B)
+    for i, (v, o) in enumerate(((4, ALU.arith_shift_right), (15, ALU.bitwise_and), (8, ALU.bitwise_and), (7, ALU.bitwise_and), (3, ALU.bitwise_and))):
+        ts(A("PI", 1 + i, 2 + i), A("PI", 0, 1), v, o)
+    cp(A("COL", 0, 5), A("PI", 1, 6))
+    ts(A("COL", 5, 6), A("COL", 1, 2), 8.0, ALU.mult, A("COL", 0, 1), ALU.add)
+    ts(A("COL", 6, 7), A("COL", 0, 1), A("COL", 2, 3), ALU.add, 8.0, ALU.mult)
+    ts(A("COL", 6, 7), A("COL", 6, 7), A("COL", 3, 4), ALU.add)
+    ts(A("SO"), A("COLI", 0, 4), 128.0, ALU.mult, A("COL", 5, 6), ALU.add)
+    ts(A("GO"), A("COLI", 0, 4), 128.0, ALU.mult, A("COL", 6, 7), ALU.add)
+    cp(A("EX"), A("COLI", 0, 16))
+    ts(A("RA"), A("COLI", 0, 2), 0.0, ALU.mult, A("COL", 4, 5), ALU.add)
+    ms(A("YV", 0, sum(ZERO.values())), 0.0)
+    ops[-1]["w"] = [A(n) for n in ZERO]
+    ms(A("KA0"), 12.0)
+    ms(A("D0", 1024, 1152), 0.0)
+    ms(A("R0", 3200, 4096), 0.0)
+    ms(A("COL", 7, 8), 1023.5)
+    ms(A("COL", 8, 9), 0.5)
+    ms(A("COL", 9, 11), 1.0)
+    ms(A("COL", 11, 13), 0.0)
+    for h in (0, 1):
+        for j in O["sign"][h]:
+            ms(A("COL", 9 + h, 10 + h, 1, 32 * j, 32 * j + 32), 2.0)
+            ms(A("COL", 11 + h, 12 + h, 1, 32 * j, 32 * j + 32), -16.0)
+    cp(A("D0", 0, 512), A("ND", 0, 512))
+    cp(A("D0", 512, 1024), A("ND", 512, 1024))
+    cp(A("R0", 2048, 3200), A("R0", 0, 1152))
+    cp(A("R0", 4096, 4672), A("R0", 0, 576))
+    cp(A("R0", 4672, 5248), A("R0", 576, 1152), "S")
+    ms(A("R0", 0, 1), 256.0)
+    mm([(A("pM0", 128 * h, 128 * h + 128), A("XX0", 128 * h, 128 * h + 128), A("ID"), True, True) for h in (0, 1)])
+    cp(A("XX0", 256, 512), A("pM0", 0, 256), "S")
+    cp(A("VS32"), A("VS"))
+    cp(IND(A("YV"), A("SO", 0, 4)), A("VS32"))
+    turn("YV", "YVC", 8, 4, A("VL"), "pA")
+    for t in range(NT):
+        n = "VV0" if t == 0 else "SV%d" % t
+        aff(A(n, 0, 16), A("VL", 16 * t, 16 * t + 16), 1.0, -1023.5)
+        aff(A(n, 16, 32), A("VL", 16 * t, 16 * t + 16), -1.0, NONE + 1023.5)
+        if t:
+            cp(A(n, 32, 48), A("VS32", 16 * t, 16 * t + 16), "E")
+    for t in (1, 2, 3):
+        send(A("XX0"), A("XX%d" % t), t, "xx%d" % t, 12000.0)
+        send(A("SV%d" % t), A("VV%d" % t), t, "vv%d" % t, 8000.0)
+    at, names = 0, list(ZERO2)
+    for some in (names[:2], names[2:4], names[4:14], names[14:-1], names[-1:]):
+        ms(A(names[0], at, at + sum(ZERO2[n] for n in some)), 0.0)
+        ops[-1]["w"] = [A(n) for n in some]
+        at += sum(ZERO2[n] for n in some)
+    ms(A("RST8", 0, 512, 8), 4 * B)
+    for k in range(3):
+        fill(A("CG", 8 * k, 8 * k + 8), -16 * k if O["en"] == "S" else 0)
+    sel(A("TRI"), A("BO"), [[1, 128]], ALU.is_ge, 0, -1)
+    sel(A("TP"), A("TRI"), [[-1, 128]], ALU.not_equal, 0, 1, 64.0)
+    sel(A("TN"), A("TRI"), [[-1, 128]], ALU.not_equal, 0, 1, -31.0)
+    aff(A("NTRI"), A("TRI"), -1.0)
+    sel(A("DG"), A("ONE", 0, 160), [[-1, 160]], ALU.is_equal, 16, 1)
+    for t in (0, 8, 2, 10):
+        sel(A("SL%d" % t), A("DG"), [[0, 10], [1, 16]], ALU.is_equal, -t, 0)
+    for j in range(4):
+        sel(A("BJ", 512 * j, 512 * j + 512), A("ONE"), [[-1, 4], [-16, 8], [0, 16]], ALU.is_equal, -4 * j, 1)
+    off = [0, 64, 192, 384, 640]
+    fill(A("MASK", 0, 640, 1, 0, 16), 4096)
+    for c in range(4):
+        x = A("MASK", off[c], off[c + 1], 1, 0, 16)
+        sel(x, x, [[-1, 2], [0, 2], [1, 16 * c + 16]], ALU.is_ge, -16 * c, -1)
+    sel(A("R16B", 0, 128, 1, 0, 16), A("ONE", 0, 128, 1, 0, 16), [[0, 8], [-1, 16]], ALU.is_equal, 0, 1)
+    sel(A("CSEL"), A("ONE", 0, 256), [[-16, 4], [0, 64]], ALU.is_ge, 0, 1)
+    sel(A("CSEL"), A("CSEL"), [[16, 4], [0, 64]], ALU.is_ge, 15, -1)
+    iota(A("NV"), [[1, 128]], 2048 + 1024, 0)
+    aff(A("KEEP"), A("R16", 0, 16), -1.0, 1.0)
+    iota(A("DUM", 0, 12), [[16, 12]], 1152, 0)
+    iota(A("DUM", 12, 32), [[16, 20]], 3200, 0)
+    ts(A("DUM"), A("DUM"), A("COL", 1, 2), ALU.add)
+    for t in (0, 2):
+        n = "ADD%d" % t
+        iota(A(n, 0, 8), [[-16, 8]], -1152, 0)
+        fill(A(n, 8, 12), 1024 + 32 * t - 1152 - 128)
+        iota(A(n, 12, 24), [[2048 - 64, 3], [-16, 4]], -3200, 0)
+        iota(A(n, 24, 32), [[2048 - 64, 2], [0, 4]], 1024 + 32 * t - 3200 - 192, 0)
+        ts(A(n, 0, 8), A(n, 0, 8), A("COL", 1, 2), ALU.subtract)
+        ts(A(n, 12, 24), A(n, 12, 24), A("COL", 1, 2), ALU.subtract)
+    nx = [0]
+
+    def xbank(h):
+        nx[0] += 1
+        return ("pX%d" if nx[0] % 2 else "pM%d") % h
+
+    def nodes(t):
+        return A("D%d" % t, 0, 1152)
+
+    def recs(t):
+        return A("R%d" % ((t + 1) // 2))
+
+    def pen(out, cnt, need):
+        ts(out, cnt, need, ALU.is_lt)
+        either(ACT.Relu, cnt, {"bias": need, "scale": -1.0})
+        return A("UW", 0, 128)
+
+    def guards(t, h):
+        H = str(h)
+        K, KH, gu, rg, cm, pn, pM = [x + H for x in ("K", "KH", "GU", "RGG", "CMG", "PENG", "pM")]
+        xt, init = A("XX%d" % t, 256 + 128 * h, 384 + 128 * h), A("VV%d" % t, 16 + 8 * h, 24 + 8 * h)
+        if t == 0:
+            ms(A(K), NONE - 1023.5)
+            cp(A(K, 16, 24), init)
+            ms(A(KH), NONE)
+            return
+        gm = "GM%d%d" % (t, h)
+        cp(A(gu, 0, 24), A(gm, 32, 56))
+        cp(A(rg), IND(recs(t), A(gu, 0, 24)), "S")
+        mm([(A(pM, 128 * k, 128 * k + 128), xt, A("ID"), True, True) for k in range(3)])
+        tt(A(cm), A(rg), A(pM, 0, 384), ALU.is_le)
+        mm([(A(pM, 8 * k, 8 * k + 8), A(cm, 128 * k, 128 * k + 128), A("BO24", 24, 32), True, True) for k in range(3)] +
+           [(A(pM, 32, 56), A("ONE", 0, 128), A("CG", 0, 24), True, False), (A(pM, 32, 56), A("ID32"), A(gm, 0, 24), False, False)] +
+           [(A(pM, 32 + 8 * k, 40 + 8 * k), A(rg, 128 * k, 128 * k + 128), A("BO24", 0, 8), False, k == 2) for k in range(3)])
+        ts(A("DF" + H, 0, 24), A(pM, 0, 24), A("KA%d" % t, 0, 1), ALU.is_lt, -B, ALU.mult)
+        tt(A("DF" + H, 0, 24), A("DF" + H, 0, 24), A(pM, 32, 56), ALU.add)
+        ts(A(K, 0, 16), A("DF" + H, 0, 16), NONE - 1023.5, ALU.max)
+        tt(A(K, 16, 24), A("DF" + H, 16, 24), init, ALU.max)
+        ts(A(KH, 0, 24), A(K, 0, 24), RND, ALU.add, RND, ALU.subtract)
+
+    def gather(t, h, s):
+        H = str(h)
+        vo = A("VS16", 16 * t + 8 * h, 16 * t + 8 * h + 8) if s == 2 else A("VO" + H, 0, 8)
+        cp(A("EU" + H), IND(nodes(t), vo))
+        for c0, c1, e in O["chunks"][h]:
+            cp(A("RG" + H, c0, c1), IND(recs(t), A("EU" + H, c0 // 16, c1 // 16)), e)
+        if O["en"] == "S":
+            comp("S", "activation", [A("EN" + H), IND(nodes(t), vo), ACT.Identity], {"bias": A("COL", 7, 8), "scale": -1.0})
+
+    def level(t, h, s):
+        n = s + 1
+        H = str(h)
+        EU, RG, CM, pV, pM, SC, K, KH, HI, NW, DF, VM = [x + H for x in ("EU", "RG", "CM", "pV", "pM", "SC", "K", "KH", "HI", "NW", "DF", "VM")]
+        xt = A("XX%d" % t, 256 + 128 * h, 384 + 128 * h)
+        vm = A("VV%d" % t, 8 * h, 8 * h + 8) if s == 2 else A(VM, 16 * s, 16 * s + 8)
+        ts(A("U" + H), A(EU), 2048.0, ALU.is_ge)
+        if s:
+            ts(A("W" + H), A(EU), 4096.0, ALU.is_ge)
+            mm([(A(pV, 0, 128 * n), A("ONE", 0, 128), A("CST", 0, 128 * n), True, False),
+                (A(pV, 0, 256), A("U" + H), A("UW"), False, False),
+                (A(pV, 128, 128 * n), A("W" + H), A("UW", 0, 128 * s), False, False)])
+        else:
+            mm([(A(pV, 0, 128), A("U" + H), A("UW", 0, 128), True, False)])
+        for k in range(n):
+            if O["en"] == "S":
+                mm([(A(pV, 128 * k, 128 * k + 128), A("EN" + H), A("ID32"), False, False)])
+            else:
+                ts(A("EH" + H, 128 * k, 128 * k + 128), A(EU), -1.0, ALU.mult, 1023.5 + 2048 * k, ALU.add)
+                mm([(A(pV, 128 * k, 128 * k + 128), A("EH" + H, 128 * k, 128 * k + 128), A("ID"), False, False)])
+        for j in range(4):
+            px = xbank(h)
+            cm, rg = A(CM, 512 * j, 512 * j + 512), A(RG, 512 * j, 512 * j + 512)
+            mm([(A(px), xt, A("REP", 512 * j, 512 * j + 512), True, j not in O["sign"][h])])
+            if j in O["sign"][h]:
+                mm([(A(px), A("NID"), rg, False, True)])
+                comp("S", "activation", [cm, A(px), ACT.Sign], {"bias": A("COL", 8, 9)})
+            else:
+                tt(cm, rg, A(px), ALU.is_le)
+        for q in (0, 8):
+            mm([(A(pV, i, 128 * n, 16), A(RG, i, 2048, 16), A("BO24", 0, 8 * n), False, False) for i in range(q, q + 8)])
+
+    def choose(t, h, s):
+        n = s + 1
+        H = str(h)
+        CM, pV, pM, SC, K, KH, HI, NW, DF, VM = [x + H for x in ("CM", "pV", "pM", "SC", "K", "KH", "HI", "NW", "DF", "VM")]
+        vm = A("VV%d" % t, 8 * h, 8 * h + 8) if s == 2 else A(VM, 16 * s, 16 * s + 8)
+        mm([(A(pM, i, 128, 16), A(CM, i, 2048, 16), A("BO24", 24, 32), True, True) for i in range(16)])
+        big = pen(A("PEN" + H), A(pM, 0, 128), A("KC", 2 * t + h, 2 * t + h + 1))
+        mm([(A(pV, 128 * k, 128 * k + 128), big, A("PEN" + H), False, k == s) for k in range(n)])
+        comp("V", "tensor_tensor_scan", [A(SC, 0, 128 * n), A("RST", 0, 128 * n), A(pV, 0, 128 * n), -4 * B, ALU.add, ALU.max])
+        if s == 2:
+            guards(t, h)
+        best, m = A(SC, 15, 128 * n, 16), 8 * n
+        ts(A(HI, 0, m), best, RND, ALU.add, RND, ALU.subtract)
+        tt(A(DF, 0, m), best, A(K, 0, m), ALU.subtract)
+        tt(A(NW, 0, m), A(HI, 0, m), A(KH, 0, m), ALU.is_gt)
+        tt(A(DF, 0, m), A(DF, 0, m), A(NW, 0, m), ALU.mult)
+        tt(A(KH, 0, m), A(KH, 0, m), A(HI, 0, m), ALU.max)
+        tt(A(K, 0, m), A(K, 0, m), A(DF, 0, m), ALU.add)
+        if s:
+            v2 = A(VM, 16 * s - 16, 16 * s - 8)
+            tt(IND(A("Y" + H), A("SO", 0, 1)), A(KH, 8 * s, 8 * s + 16), A(K, 8 * s, 8 * s + 16), ALU.subtract)
+            turn("Y" + H, "YC" + H, 1, 1, A("VO" + H), pM, 1023.5)
+            if s == 2 or h == 0:
+                tt(v2, A(KH, 8 * s, m), A(K, 8 * s, m), ALU.subtract)
+            if s == 2:
+                aff(A("FX" + H, 0, 8), v2, -1.0, NONE)
+                tt(A(K, 8, 16), A(K, 8, 16), A("FX" + H, 0, 8), ALU.max)
+        k = 1 - t % 2
+        if h == 0 and s >= k:
+            nw = A(NW, 8 * k, 8 * k + 8)
+            if s == 2:
+                aff(A("DV", 0, 8), vm, 1.0, 1023.5)
+                tt(A("HM", 0, 8), A("DV", 0, 8), nw, ALU.mult)
+            else:
+                aff(A("AB", 8, 16), vm, 1.0, 1023.5)
+                tt(A("DV", 0, 8), A("AB", 8, 16), A("HM", 0, 8), ALU.subtract)
+                tt(A("DV", 0, 8), A("DV", 0, 8), nw, ALU.mult)
+                tt(A("HM", 0, 8), A("HM", 0, 8), A("DV", 0, 8), ALU.add)
+
+    def handon(t, h):
+        H = str(h)
+        K, KH, GN, NM, NZ, pM = [x + H for x in ("K", "KH", "GN", "NM", "NZ", "pM")]
+        low = A("SG%d%d" % (t, h), 0, 24) if t < 3 else A("LO" + H, 0, 24)
+        tt(low, A(K, 0, 24), A(KH, 0, 24), ALU.subtract)
+        aff(A(NM, 0, 24), low, -1.0, 1023.5)
+        ts(A(NZ, 0, 24), A(KH, 0, 24), NONE, ALU.is_gt)
+        if t == 3 or (h == 0 and t % 2):
+            tt(A(GN, 0, 24), A(NM, 0, 24), A(NZ, 0, 24), ALU.mult)
+        if t < 3:
+            tt(IND(A("YG" + H), A("SO", 0, 2)), A(NM), A(NZ), ALU.mult)
+            turn("YG" + H, "YGC" + H, 3, 2, A(low[1], 32, 64), pM)
+            send(A(low[1]), A("GM%d%d" % (t + 1, h)), 1, "gm%d%d" % (t + 1, h))
+        else:
+            mm([(A(pM, 0, 128, 1, 0, 24), A(GN, 0, 24), A("ID32"), True, True)])
+            cp(A("YO", 128 * h, 128 * h + 128, 1, 0, 24), A(pM, 0, 128, 1, 0, 24), "E")
+            for k in range(3):
+                dma("Y", ("hbm", "yg", (256 * k + 128 * h, 256 * k + 128 * h + 128)), A("YO", 128 * h, 128 * h + 128, 1, 8 * k, 8 * k + 8), "out", 2000)
+
+    def decide(t):
+        even = t % 2 == 0
+        X, m, low = "XX%d" % t, 32 if even else 16, (1, 0, 64)
+        cp(A("EB"), A("EU0", 0, 64))
+        cp(IND(A("YA"), A("SO", 0, 1)), A("HM"))
+        turn("YA", "YAC", 1, 1, A("AO"), "pA" if even else "pB")
+        cp(A("EA"), IND(nodes(t), A("AO", 0, 4)), "E")
+        ts(A("FR"), A("EA" if even else "EB"), 0.0, ALU.is_equal)
+        either(ACT.Relu, A("EA" if even else "EB"), {"scale": -1.0, "bias": 1.0})
+        mm([(A("pA", 64, 72, *low), A("FR"), A("BO24", 24, 32), True, True)])
+        if even:
+            aff(A("AB", 8, 16), A("VM0", 0, 8), 1.0, 1023.5)
+        tt(A("Q1", 0, 8), A("HM", 0, 8), A("AB", 8, 16), ALU.not_equal)
+        tt(A("Q2", 0, 8, *low), A("pA", 64, 72, *low), A("HM", 0, 8, *low), ALU.min)
+        tt(A("Q2", 0, 8, *low), A("Q2", 0, 8, *low), A("Q1", 0, 8, *low), ALU.min)
+        tt(A("ABM", 0, 8, *low), A("HM", 0, 8, *low), A("Q2", 0, 8, *low), ALU.mult)
+        tt(A("ABM", 8, 16, *low), A("AB", 8, 16, *low), A("Q2", 0, 8, *low), ALU.mult)
+        cp(A("OTH"), IND(A("ABM"), A("EX")))
+        tt(A("OWN", 0, 128), IND(A("ABM"), A("EX", 0, 8)), A("R16"), ALU.mult)
+        tt(A("OWN", 128, 256), IND(A("ABM"), A("EX", 8, 16)), A("R16"), ALU.mult)
+        for cs in ((0, 1, 2), (3,)):
+            o0 = off[cs[0]]
+            mm([(A("pA", 0, off[cs[-1] + 1] - o0), A("R16B", 0, 128, 1, 0, 16), A("MASK", o0, off[cs[-1] + 1], 1, 0, 16), True, False)])
+            for c in cs:
+                w, lst = 16 * c + 16, []
+                for b, (o, o2) in enumerate(((0, 0), (1, 1), (0, 1), (1, 0))):
+                    out = A("pA", off[c] - o0 + b * w, off[c] - o0 + b * w + w)
+                    lst.append((out, A("OWN", 128 * o, 128 * o + 128, *low), A("CSEL", 64 * c, 64 * c + w, *low), False, False))
+                    lst.append((out, A("OTH", 128 * o2, 128 * o2 + 128, *low), A("NID", 0, w, *low), False, c == cs[-1] and b == 3))
+                mm(lst)
+            for c in cs:
+                comp("V", "tensor_reduce", [A("MN", c, c + 1), A("pA", off[c] - o0, off[c + 1] - o0), AxisListType.X, ALU.min],
+                     {"apply_absolute_value": True})
+        ts(A("ACR", 0, m), IND(A("MN"), A("RA", 0, m // 16)), 0.0, ALU.is_gt)
+        if t < 3:
+            ts(A("ACB", 0, 4), A("MN", 0, 4), 0.0, ALU.is_gt)
+            mm([(A("pA", 0, 4), A("ONE", 0, 128), A("ACB", 0, 4), True, True)])
+            comp("V", "tensor_reduce", [A("AS", 0, 1), A("pA", 0, 4), AxisListType.X, ALU.add])
+            ts(A("AS", 1, 2), A("AS", 0, 1), -0.5, ALU.add, RND2, ALU.add)
+            ts(A("SK%d" % t, 0, 1), A("AS", 1, 2), RND2 - 12.0, ALU.subtract, A("AS", 0, 1), ALU.subtract)
+            send(A("SK%d" % t, 0, 4), A("KA%d" % (t + 1)), 1, "ka%d" % (t + 1))
+        cp(A("BASE", 0, 4), A("AO", 0, 4))
+        for c in ((4, 12, 16, 20) if even else (4,)):
+            cp(A("BASE", c, c + 4), A("VO0", 0, 4))
+        tt(A("XD", 0, m), A("BASE", 0, m), A("ADD%d" % (t & 2), 0, m), ALU.add)
+        tt(A("OF", 0, m), A("XD", 0, m), A("ACR", 0, m), ALU.mult)
+        tt(A("OF", 0, m), A("OF", 0, m), A("DUM", 0, m), ALU.add)
+        cp(A("OU", 0, m), A("OF", 0, m))
+        new = A("D%d" % (t + 1))
+        if not even:
+            cp(A("G0X"), IND(A("GN0"), A("EX", 0, 8)))
+            mm([(A("pB", 0, 64), A("G0X", 0, 128, *low), A("ID", 0, 64, *low), True, True),
+                (A("pB", 64, 128), A("TP"), A("FR"), True, True)])
+            tt(A("NE"), A("EA"), A("pB", 0, 64), ALU.not_equal)
+            ts(A("P0"), A("pB", 64, 128), 64.0, ALU.is_equal)
+            tt(A("P0"), A("P0"), A("pB", 0, 64), ALU.mult)
+            tt(IND(new, A("OU", 0, 4)), A("EA"), A("NE"), ALU.mult)
+            tt(IND(new, A("OU", 4, 8)), A("EB"), A("P0"), ALU.add)
+            return
+        for o, x, r in (("RC", "XC", 8 + t), ("RH", "XH", t)):
+            aff(A(o), IND(recs(t), A("VO0", 0, 4)), A("KEEP", r, r + 1))
+            aff(A(x), A(X, 0, 64), A("R16", r, r + 1))
+        for j in range(5):
+            o, x = ("RC", "XC") if j < 3 else ("RH", "XH")
+            tt(IND(recs(t + 1), A("OU", 12 + 4 * j, 16 + 4 * j)), A(o), A(x), ALU.add)
+        for b, r in ((0, t), (1, 8 + t)):
+            out = A("pB", 64 * b, 64 * b + 64)
+            mm([(out, A("BJ", 128 * (r ^ 8), 128 * (r ^ 8) + 128), A(X, 0, 64), True, False)] +
+               [(out, A("SL%d" % r, r + 16 - i, r + 144 - i), A("RG0", i, 1024, 16), False, i == 15) for i in range(16)])
+        ts(A("NGS"), A("pB", 0, 128), 0.0, ALU.is_lt)
+        tt(A("STR"), A("NGS", 0, 64), A("NGS", 64, 128), ALU.mult)
+        tt(A("EBN"), A("EB"), A("NGS", 0, 64), ALU.mult)
+        cp(A("EHI"), A("EB"), "E")
+        tt(A("ELO"), A("EB"), A("EHI"), ALU.subtract)
+        mm([(A("pB", 0, 64), A("TN"), A("STR"), True, True), (A("pB", 64, 128), A("TP"), A("FR"), True, True),
+            (A("pB", 128, 192), A("BO"), A("FR"), True, False), (A("pB", 128, 192), A("NTRI"), A("STR"), False, True)])
+        aff(A("NB"), A("pB", 0, 64), 16384.0, 96.0 * 16384.0)
+        aff(A("PL"), A("pB", 64, 128), -16384.0)
+        ts(A("P0"), A("pB", 64, 128), 64.0, ALU.is_equal)
+        ts(A("PUT"), A("pB", 128, 192), 0.0, ALU.is_gt)
+        for b, ps in ((1, "pB"), (0, "pA")):
+            for q in (0, 4):
+                lst = []
+                for j in range(q, q + 4):
+                    out, bj = A(ps, j, 512, 8), A("BJ", 128 * (8 * b + j), 128 * (8 * b + j) + 128)
+                    lst += [(out, A("ID"), A("PL"), True, False), (out, bj, A("NB"), False, False), (out, bj, A("EHI"), False, False),
+                            (out, bj, A("ELO"), False, True)]
+                mm(lst)
+            comp("S", "activation", [A("ZA", 512 * b, 512 * b + 512), A(ps), ACT.Abs])
+            comp("V", "tensor_tensor_scan", [A("ZS", 512 * b, 512 * b + 512), A("RST8"), A("ZA", 512 * b, 512 * b + 512), 4 * B, ALU.add, ALU.min])
+        tt(A("P0"), A("P0"), A("NV", 32 * t, 32 * t + 64), ALU.mult)
+        tt(A("P0"), A("P0"), A("EA"), ALU.add)
+        tt(A("PUT"), A("PUT"), A("STR"), ALU.mult)
+        tt(A("EP"), A("EB"), A("PUT"), ALU.mult)
+        tt(IND(new, A("OU", 4, 8)), A("EBN"), A("EP"), ALU.subtract)
+        tt(IND(new, A("OU", 8, 12)), A("EB"), A("EBN"), ALU.subtract)
+        tt(A("RES"), A("ZS", 7, 512, 8), A("ZS", 519, 1024, 8), ALU.min)
+        ts(A("RM"), A("RES"), 8192.0, ALU.is_lt)
+        tt(A("RM"), A("RM"), A("RES"), ALU.mult)
+        tt(IND(new, A("OU", 0, 4)), A("P0"), A("RM"), ALU.add)
+
+    for t in range(NT):
+        even = t % 2 == 0
+        cp(A("VS16", 16 * t, 16 * t + 16), A("VV%d" % t, 32, 48) if t else A("VS", 0, 16))
+        dma("Y", nodes(t + 1), nodes(t), "cd%d" % (t + 1), 4000)
+        if even:
+            dma("Y", recs(t + 1), recs(t), "cr%d" % (t // 2 + 1), 7000)
+        if t == 3:
+            dma("Y", ("hbm", "yr", None), A("R2", 2048, 3200), "out", 3000)
+        for h in (0, 1):
+            aff(A("KC", 2 * t + h, 2 * t + h + 1), A("KA%d" % t, 0, 1), A("COL", 9 + h, 10 + h), A("COL", 11 + h, 12 + h))
+            steps = []
+            for s in (2, 1, 0):
+                steps += [(gather, t, h, s), (level, t, h, s)] + [(decide, t)] * (s == 0 and h == 0 and even) + [(choose, t, h, s)]
+            for step in steps + [(handon, t, h)] + [(decide, t)] * (h == 0 and not even):
+                part[0] += 1
+                step[0](*step[1:])
+    dma("Y", ("hbm", "yn", (0, 576)), A("D4", 0, 576), "out", 3000)
+    dma("S", ("hbm", "yn", (576, 1152)), A("D4", 576, 1152), "out", 3000)
+    return ops
+
+
+def inorder(ops, deps, i, j):
+    return ops[i]["eng"] == ops[j]["eng"] and "sem" not in ops[j] and (ops[i]["eng"] == "P" or not (deps[i].get(j) or OPT["war"]))
+
+
+def order(ops):
+    C = COST
+    seen, deps = {}, []
+    for i, o in enumerate(ops):
+        if "alt" in o:
+            o.update(eng="V", calls=o["alt"]["V"][0], cost=o["alt"]["V"][1])
+        d = {}
+        for x, wr in [(x, False) for x in o["r"]] + [(x, True) for x in o["w"]]:
+            ps = TILE[x[1]][0] == "psum"
+            lo, hi = (0, 512) if ps else (x[2], x[3])
+            lst = seen.setdefault(x[1], [])
+            for a, b, j, w2 in lst:
+                if j != i and a < hi and lo < b and (wr or w2 or ps):
+                    d[j] = d.get(j, False) or (w2 and not wr)
+            if (wr and x[4] == 1 and x[6] - x[5] == 128) or ps:
+                lst[:] = [e for e in lst if not (lo <= e[0] and e[1] <= hi)]
+            lst.append((lo, hi, i, wr))
+        deps.append(d)
+    n = len(ops)
+    pre = [list(deps[i]) + ([ops[i]["after"]] if "after" in ops[i] else []) for i in range(n)]
+    suc = [[] for _ in ops]
+    for i in range(n):
+        for j in pre[i]:
+            suc[j].append(i)
+    dur = [o["cost"] + (o["lat"] if "lat" in o and o["eng"] != "R" else 0.0) for o in ops]
+    rank = [0.0] * n
+    for i in range(n - 1, -1, -1):
+        rank[i] = dur[i] + max([rank[j] + C["lat"] for j in suc[i]], default=0.0)
+    rank = [rank[i] + 100.0 * URGE.get(ops[i]["part"], 0) for i in range(n)]
+    left = [len(p) for p in pre]
+    ready = {i: 0.0 for i in range(n) if not left[i]}
+    free, seq, end = {}, [], 0.0
+    while ready:
+        for i, r in ready.items():
+            if "alt" in ops[i]:
+                e = min("VS", key=lambda e: max(r, free.get(e, 0.0)) + ops[i]["alt"][e][1] + (C["lean"] if e == "V" else 0.0))
+                ops[i].update(eng=e, calls=ops[i]["alt"][e][0], cost=ops[i]["alt"][e][1])
+                dur[i] = ops[i]["cost"]
+        st = {i: max(r, free.get(ops[i]["eng"], 0.0)) for i, r in ready.items()}
+        i0 = min(st, key=lambda i: (st[i], -rank[i]))
+        i = max((j for j in st if ops[j]["eng"] == ops[i0]["eng"] and st[j] <= st[i0] + C["look"]), key=lambda j: rank[j])
+        del ready[i]
+        ops[i]["t0"] = st[i]
+        if ops[i]["eng"] != "R":
+            free[ops[i]["eng"]] = st[i] + ops[i]["cost"]
+        fin = st[i] + dur[i]
+        ops[i]["t1"] = fin
+        end = max(end, fin)
+        seq.append(i)
+        for j in suc[i]:
+            left[j] -= 1
+            if not left[j]:
+                ready[j] = max(ops[k]["t1"] + (0.0 if inorder(ops, deps, j, k) else C["lat"]) for k in pre[j])
+    return seq, deps, end
+
+
+def waits(ops, seq, deps):
+    pos, known, clock, need, cnt = {}, {}, {}, {}, {}
+    for i in seq:
+        o = ops[i]
+        key = o.get("sem") or o["eng"]
+        pos[i] = (key, cnt.get(key, 0))
+        cnt[key] = cnt.get(key, 0) + 1
+        kn = known.setdefault(o["eng"], {})
+        need[i] = []
+        if o["eng"] != "R":
+            for j in sorted(deps[i], key=lambda j: -ops[j]["t1"]):
+                if inorder(ops, deps, i, j):
+                    continue
+                k, p = pos[j]
+                if kn.get(k, -1) < p:
+                    need[i].append(j)
+                    for k2, p2 in clock[j].items():
+                        kn[k2] = max(kn.get(k2, -1), p2)
+        clock[i] = dict(kn) if o["eng"] != "R" else {}
+        clock[i][key] = pos[i][1]
+    return need
+
+
+PLAN = {}
+
+
+def rank_program(g, core, T, topo):
+    rank = T.rank_of(core)
+    if rank is None:
+        return
+    if not PLAN:
+        ops = program()
+        seq, deps, _ = order(ops)
+        PLAN.update(ops=ops, seq=seq, need=waits(ops, seq, deps))
+    ops, seq, need = PLAN["ops"], PLAN["seq"], PLAN["need"]
+    queue = {"V": g.vector, "S": g.scalar, "P": g.tensor, "G": g, "Y": g.sync}
+    call = {"V": {"tensor_scalar": g.vector.tensor_scalar, "tensor_tensor": g.vector.tensor_tensor, "tensor_copy": g.vector.tensor_copy,
+                  "memset": g.vector.memset, "tensor_tensor_scan": g.vector.tensor_tensor_scan, "tensor_reduce": g.vector.tensor_reduce},
+            "S": {"activation": g.scalar.activation, "dma_start": g.scalar.dma_start}, "P": {"matmul": g.tensor.matmul},
+            "G": {"iota": g.iota, "affine_select": g.affine_select}, "Y": {"dma_start": g.sync.dma_start}}
+
+    def view(x):
+        if not isinstance(x, tuple):
+            return x
+        if x[0] == "ind":
+            return view(x[1]).indirect(view(x[2]))
+        if x[0] == "hbm":
+            return T[x[1]][:] if x[2] is None else T[x[1]][:, x[2][0]:x[2][1]]
+        buf, at = PLACE[x[1]]
+        return T[buf][x[5]:x[6], at + x[2]:at + x[3]] if x[4] == 1 else T[buf][x[5]:x[6], at + x[2]:at + x[3]:x[4]]
+
+    def lanes(a, b):
+        return topo.engines(a, b)[:OPT["eng"]]
+
+    marked = set(j for i in seq for j in need[i])
+    total, value = {}, {}
+    for i in seq:
+        o = ops[i]
+        if o["eng"] == "R":
+            hop = ops[o["after"]]["calls"][0][1][2]
+            value[i] = (o["sem"], len(lanes(T.cores[(rank - hop) % NR], core)))
+            total[o["sem"]] = value[i][1]
+            continue
+        for j in need[i]:
+            queue[o["eng"]].wait_ge(T.sem[value[j][0]], value[j][1])
+        for meth, args, kw in o["calls"]:
+            if meth == "remote":
+                to = T.cores[(rank + args[2]) % NR]
+                rid, pid = topo.addr(to, core)
+                use = lanes(core, to)
+                g.remote_dma(view(args[0]), view(args[1]), T.sem[args[3]], T.sem["sent"], pid, rid, sum(1 << e for e in use))
+                total["sent"] = total.get("sent", 0) + len(use)
+            else:
+                ins = call[o["eng"]][meth](*[view(x) for x in args], **{k: view(x) for k, x in kw.items()})
+        if o.get("sem") == "sent":
+            continue
+        if "sem" in o or i in marked:
+            sem, n = (o["sem"], 16) if "sem" in o else ("e" + o["eng"], 1)
+            ins.then_inc(T.sem[sem], n)
+            total[sem] = total.get(sem, 0) + n
+            value[i] = (sem, total[sem])
+    for sem, n in total.items():
+        g.wait_ge(T.sem[sem], n)

@@ -10,14 +10,14 @@ RND2 = 1.5 * 2.0 ** 24
 S3 = ((0, 1024, "S"), (1024, 1536, "S"), (1536, 2048, "S"))
 S4 = tuple((512 * j, 512 * j + 512, "S") for j in range(4))
 E1 = (S4[0], (512, 1024, "E")) + S4[2:]
-OPT = dict(chunks=(S4, S4), sign=((), (1, 3)), en="H", yc="E", war=True, eng=8)
-COST = dict(c=1.04, g=1.56, sc=3.8, pe=0.52, lat=70.0, look=0.0, rem=2500.0, lean=200.0)
+OPT = dict(chunks=(E1, E1), sign=((), (1, 3)), en="H", yc="E", war=True, eng=8, t2=True)
+COST = dict(c=0.95, g=1.8, sc=3.8, pe=0.475, lat=190, look=0.0, rem=2500.0, lean=0)
 
-URGE = {2: 50, 3: 60, 4: -130, 5: 50, 6: -5, 7: 15, 8: -15, 12: -45, 13: 20, 14: 5, 16: 35, 17: 20, 18: -5, 19: 5, 20: 90, 23: -5, 24: 110, 25: -50,
-        26: 15, 28: 10, 29: -115, 30: 120, 31: 5, 32: 45, 33: 25, 34: 30, 35: 15, 36: -100, 37: 40, 38: 65, 39: -10, 40: -10, 41: 10, 42: -10,
-        43: 95, 44: 35, 45: 5, 47: 20, 48: 20, 49: 30, 50: 5, 52: -20, 55: 35, 56: 5, 57: 35, 58: 45, 61: -20, 62: -15, 63: 60, 64: -20, 65: 5,
-        66: 20, 67: -5, 68: -150, 69: 65, 70: -40, 71: -15, 72: -15, 73: 10, 74: 40, 76: 30, 77: -10, 78: -20, 79: 5, 80: -35, 81: -15, 82: -15,
-        83: -5, 84: -25}
+URGE = {2: 5, 3: 110, 4: -60, 5: 135, 6: 55, 7: -5, 8: 25, 9: -10, 10: 10, 11: -5, 12: -45, 13: -25, 14: 100, 15: -10, 16: -5, 17: 5, 18: 185, 20: -10,
+        21: 75, 22: -20, 23: 15, 24: -5, 25: 100, 26: 135, 27: 35, 28: 25, 29: 15, 30: -5, 31: 35, 32: -10, 33: 25, 34: -35, 35: 35, 36: -30, 38: -30,
+        40: 15, 41: 35, 42: -5, 43: 5, 44: -5, 45: 10, 46: -20, 48: -45, 49: 20, 50: -10, 51: -10, 52: -20, 53: -15, 54: 5, 55: -70, 57: -5, 59: 100,
+        60: -30, 61: 20, 62: 100, 63: 55, 64: 55, 66: -10, 67: 25, 68: 10, 69: 30, 70: -15, 71: -20, 72: 30, 73: -40, 74: 15, 75: -50, 76: -125,
+        80: -30, 81: -45, 82: 15, 83: -45, 84: -10}
 f32, b16, f16, i32, u16 = "float32", "bfloat16", "float16", "int32", "uint16"
 TILE = {}
 
@@ -40,7 +40,7 @@ _decl("sbuf", b16, R0=5248, R1=5248, R2=5248, XX0=512, XX1=512, XX2=512, XX3=512
       CSEL=256, FR=64, NGS=128, STR=64, NB=64, PL=64, EHI=64, ELO=64, ACB=16, RC=64, RH=64, XC=64, XH=64)
 _decl("sbuf", f16, True, EH=384)
 _decl("sbuf", f16, OTH=256, OWN=256, G0X=128)
-_decl("sbuf", f32, True, SC=384, EN=128, K=32, KH=32, HI=32, NW=32, DF=32, FX=16, LO=32)
+_decl("sbuf", f32, True, SC=384, EN=128, K=32, KH=32, HI=32, NW=32, DF=32, FX=16, LO=32, TH=32)
 _decl("sbuf", f32, D0=1344, D1=1344, D2=1344, D3=1344, D4=1344, ID32=128, R16=128, RST=384, DV=16, KC=16,
       YVC=512, VS32=64, VL=64, VV0=48, VV1=48, VV2=48, VV3=48, SV1=48, SV2=48, SV3=48,
       GM10=64, GM11=64, GM20=64, GM21=64, GM30=64, GM31=64, KA0=4, KA1=4, KA2=4, KA3=4, GN1=32, YO=256, COL=16, COLI=32,
@@ -381,9 +381,13 @@ def program():
         if s == 2:
             guards(t, h)
         best, m = A(SC, 15, 128 * n, 16), 8 * n
+        if O["t2"]:
+            aff(A("TH" + H, 0, m), A(KH, 0, m), 1.0, 1024.0)
+            tt(A(NW, 0, m), best, A("TH" + H, 0, m), ALU.is_gt)
         ts(A(HI, 0, m), best, RND, ALU.add, RND, ALU.subtract)
         tt(A(DF, 0, m), best, A(K, 0, m), ALU.subtract)
-        tt(A(NW, 0, m), A(HI, 0, m), A(KH, 0, m), ALU.is_gt)
+        if not O["t2"]:
+            tt(A(NW, 0, m), A(HI, 0, m), A(KH, 0, m), ALU.is_gt)
         tt(A(DF, 0, m), A(DF, 0, m), A(NW, 0, m), ALU.mult)
         tt(A(KH, 0, m), A(KH, 0, m), A(HI, 0, m), ALU.max)
         tt(A(K, 0, m), A(K, 0, m), A(DF, 0, m), ALU.add)
@@ -528,14 +532,20 @@ def program():
         tt(A("RM"), A("RM"), A("RES"), ALU.mult)
         tt(IND(new, A("OU", 0, 4)), A("P0"), A("RM"), ALU.add)
 
+    def copies(t):
+        last = len(ops) - 1
+        dma("Y", nodes(t + 1), nodes(t), "cd%d" % (t + 1), 3000)
+        ops[-1]["also"] = last
+        if t % 2 == 0:
+            dma("Y", recs(t + 1), recs(t), "cr%d" % (t // 2 + 1), 6000)
+            ops[-1]["also"] = last
+        if t == 3:
+            dma("Y", ("hbm", "yr", None), A("R2", 2048, 3200), "out", 3000)
+            ops[-1]["also"] = last
+
     for t in range(NT):
         even = t % 2 == 0
         cp(A("VS16", 16 * t, 16 * t + 16), A("VV%d" % t, 32, 48) if t else A("VS", 0, 16))
-        dma("Y", nodes(t + 1), nodes(t), "cd%d" % (t + 1), 4000)
-        if even:
-            dma("Y", recs(t + 1), recs(t), "cr%d" % (t // 2 + 1), 7000)
-        if t == 3:
-            dma("Y", ("hbm", "yr", None), A("R2", 2048, 3200), "out", 3000)
         for h in (0, 1):
             aff(A("KC", 2 * t + h, 2 * t + h + 1), A("KA%d" % t, 0, 1), A("COL", 9 + h, 10 + h), A("COL", 11 + h, 12 + h))
             steps = []
@@ -544,6 +554,8 @@ def program():
             for step in steps + [(handon, t, h)] + [(decide, t)] * (h == 0 and not even):
                 part[0] += 1
                 step[0](*step[1:])
+                if step == (choose, t, 0, 2):
+                    copies(t)
     dma("Y", ("hbm", "yn", (0, 576)), A("D4", 0, 576), "out", 3000)
     dma("S", ("hbm", "yn", (576, 1152)), A("D4", 576, 1152), "out", 3000)
     return ops
@@ -559,7 +571,7 @@ def order(ops):
     for i, o in enumerate(ops):
         if "alt" in o:
             o.update(eng="V", calls=o["alt"]["V"][0], cost=o["alt"]["V"][1])
-        d = {}
+        d = {o["also"]: True} if "also" in o else {}
         for x, wr in [(x, False) for x in o["r"]] + [(x, True) for x in o["w"]]:
             ps = TILE[x[1]][0] == "psum"
             lo, hi = (0, 512) if ps else (x[2], x[3])

@@ -2,22 +2,19 @@ from concourse.mybir import AluOpType, AxisListType, ActivationFunctionType
 
 ALU, ACT = AluOpType, ActivationFunctionType
 
-NR, NT = 4, 4
-B = float(2 ** 24)
-NONE = -4094.0 * 2048.0
-RND = 1.5 * 2.0 ** 34
+NR, NT, W = 4, 4, 18
+B = 2.0 ** 26
+RB = 1.5 * 2.0 ** 23 * B
+R2K = 1.5 * 2.0 ** 34
+R1K = 1.5 * 2.0 ** 33
 RND2 = 1.5 * 2.0 ** 24
-S3 = ((0, 1024, "S"), (1024, 1536, "S"), (1536, 2048, "S"))
-S4 = tuple((512 * j, 512 * j + 512, "S") for j in range(4))
-E1 = (S4[0], (512, 1024, "E")) + S4[2:]
-OPT = dict(chunks=(E1, E1), sign=((), (1, 3)), en="H", yc="E", war=True, eng=8, t2=True)
+NONE0, NONE1, THR = -4092.0 * 4096, -4088.0 * 4096, -4085.0 * 4096
+BIG = 1280.0 * 8192
+Z = 64
+COFF = {2: 0, 1: 432, 0: 720}
+OPT = dict(gath=("SSSS", "SSSS"), turn="EE", war=True, eng=8, zb=("pB", "pA"), cb=("pA", "pB"), urge=0.0, late=0.0)
 COST = dict(c=0.95, g=1.8, sc=3.8, pe=0.475, lat=190, look=0.0, rem=2500.0, lean=0)
 
-URGE = {2: 5, 3: 110, 4: -60, 5: 135, 6: 55, 7: -5, 8: 25, 9: -10, 10: 10, 11: -5, 12: -45, 13: -25, 14: 100, 15: -10, 16: -5, 17: 5, 18: 185, 20: -10,
-        21: 75, 22: -20, 23: 15, 24: -5, 25: 100, 26: 135, 27: 35, 28: 25, 29: 15, 30: -5, 31: 35, 32: -10, 33: 25, 34: -35, 35: 35, 36: -30, 38: -30,
-        40: 15, 41: 35, 42: -5, 43: 5, 44: -5, 45: 10, 46: -20, 48: -45, 49: 20, 50: -10, 51: -10, 52: -20, 53: -15, 54: 5, 55: -70, 57: -5, 59: 100,
-        60: -30, 61: 20, 62: 100, 63: 55, 64: 55, 66: -10, 67: 25, 68: 10, 69: 30, 70: -15, 71: -20, 72: 30, 73: -40, 74: 15, 75: -50, 76: -125,
-        80: -30, 81: -45, 82: 15, 83: -45, 84: -10}
 f32, b16, f16, i32, u16 = "float32", "bfloat16", "float16", "int32", "uint16"
 TILE = {}
 
@@ -28,31 +25,32 @@ def _decl(where, dtype, halves=False, **kw):
             TILE[k + x] = (where, [128, n], dtype)
 
 
-ZERO = dict(YV=512, Y0=128, Y1=128, YC0=128, YC1=128, VM0=32, VM1=32, HM=16)
-ZERO2 = dict(YG0=256, YG1=256, YGC0=256, YGC1=256, YA=128, YAC=128, NM0=32, NM1=32, NZ0=32, NZ1=32, MN=16, BASE=32, GN0=32, ABM=16,
-             SG00=64, SG01=64, SG10=64, SG11=64, SG20=64, SG21=64, SK0=16, SK1=16, SK2=16, RST8=512)
+ZERO = dict(YV=512, Y0=128, Y1=128, YC0=128, YC1=128, MN=16, AB=32)
+ZERO2 = dict(YG0=256, YG1=256, YGC0=256, YGC1=256, SG00=64, SG01=64, SG10=64, SG11=64, SG20=64, SG21=64, SG30=64, SG31=64, RST8=512)
 _decl("sbuf", f32, **ZERO)
 _decl("sbuf", f32, **ZERO2)
 _decl("psum", f32, pX0=512, pX1=512, pB=512, pV0=512, pV1=512, pM0=512, pM1=512, pA=512)
-_decl("sbuf", b16, True, RG=2048, CM=2048, RGG=384, CMG=384, U=128, W=128, PEN=128, PENG=32)
-_decl("sbuf", b16, R0=5248, R1=5248, R2=5248, XX0=512, XX1=512, XX2=512, XX3=512, ONE=512, REP=2048, BJ=2048, ID=128, NID=128, BO=128,
-      BO24=32, UW=256, CST=384, CG=32, TRI=128, NTRI=128, TP=128, TN=128, DG=160, SL0=160, SL8=160, SL2=160, SL10=160, MASK=640, R16B=128,
-      CSEL=256, FR=64, NGS=128, STR=64, NB=64, PL=64, EHI=64, ELO=64, ACB=16, RC=64, RH=64, XC=64, XH=64)
-_decl("sbuf", f16, True, EH=384)
-_decl("sbuf", f16, OTH=256, OWN=256, G0X=128)
-_decl("sbuf", f32, True, SC=384, EN=128, K=32, KH=32, HI=32, NW=32, DF=32, FX=16, LO=32, TH=32)
-_decl("sbuf", f32, D0=1344, D1=1344, D2=1344, D3=1344, D4=1344, ID32=128, R16=128, RST=384, DV=16, KC=16,
+_decl("sbuf", b16, True, RG=2048, CM=2048, RGG=384, CMG=384, U=128, W=128, NW=48)
+_decl("sbuf", b16, R0=Z + 5248, R1=Z + 5248, R2=Z + 5248, XX0=320, XX1=320, XX2=320, XX3=320, ZL=256, ONE=512, REP=2048, BJ=2048, ID=128, ID2K=128,
+      BO=128, BO1=16, BO4K=32, BOS=32, BK0=32, BK1=32, BK2=32, BK3=32, SK0=32, SK1=32, SK2=32, IW=288, UW=288, CC=864, CT=144, CG=32, L1=128, L2=128,
+      TRI=128, NTRI=128, TP=128, TN=128, TQ=128, DG=160, SL0=160, SL8=160, SL2=160, SL10=160, MASK=640, R16B=256, CSEL=512, SEA=128, SEB=128, BSB=32,
+      FR=64, NGS=128, STR=64, NBE=64, PL=64, ACB=16, RC=64, RH=64, XC=64, XH=64)
+_decl("sbuf", f16, True, E0=128, E1=128)
+_decl("sbuf", f16, OWN=256, G0X=128, TT=64, ELO=64)
+_decl("sbuf", f32, True, SC=576, KE=128, HI=32, NM=32, NZ=32, GN=32)
+_decl("sbuf", f32, D1=Z + 1152, D2=Z + 1152, D3=Z + 1152, D4=Z + 1152, ID32=128, NID32=128, R16=128, NR16=128, BSEL=16, RST=432, HM=16, DV=16,
       YVC=512, VS32=64, VL=64, VV0=48, VV1=48, VV2=48, VV3=48, SV1=48, SV2=48, SV3=48,
-      GM10=64, GM11=64, GM20=64, GM21=64, GM30=64, GM31=64, KA0=4, KA1=4, KA2=4, KA3=4, GN1=32, YO=256, COL=16, COLI=32,
-      EA=64, EB=64, AB=16, Q1=16, Q2=16, ACR=32, ADD0=32, ADD2=32, DUM=32, XD=32, OF=32,
-      AS=16, EBN=64, PUT=64, EP=64, P0=64, NE=64, NV=128, ZA=1024, ZS=1024, RES=64, RM=64, KEEP=16)
+      GM10=64, GM11=64, GM20=64, GM21=64, GM30=64, GM31=64, YO=256, COL=16, COLI=32,
+      EA=64, EB=64, Q1=16, Q2=16, ADD0=32, ADD2=32, XT=32, OF=32, AS=16, EBN=64, PUT=64, EP=64, P0=64, M1=64, NE=64, EHI=64, NV=128,
+      ZA=1024, ZS=1024, KEEP=16)
 _decl("sbuf", i32, ND=1024, VS=64, PI=16, IT=128, IT2=128)
-_decl("sbuf", u16, True, EU=128, VO=16, GU=32)
-_decl("sbuf", u16, VS16=64, AO=16, SO=4, GO=4, EX=16, RA=2, OU=32)
+_decl("sbuf", u16, True, EU=128, VO=16)
+_decl("sbuf", u16, VS16=64, AO=16, SO=4, GO=4, EX=16, EXK=16, RA=2, OU=32, GU10=32, GU11=32, GU20=32, GU21=32, GU30=32, GU31=32,
+      SU00=32, SU01=32, SU10=32, SU11=32, SU20=32, SU21=32)
 
-MSGS = ["xx%d" % t for t in (1, 2, 3)] + ["vv%d" % t for t in (1, 2, 3)] + ["gm%d%d" % (t, h) for t in (1, 2, 3) for h in (0, 1)] + \
+MSGS = ["xx%d" % t for t in (1, 2, 3)] + ["vv%d" % t for t in (1, 2, 3)] + ["g%s%d%d" % (x, t, h) for x in "mu" for t in (1, 2, 3) for h in (0, 1)] + \
        ["ka%d" % t for t in (1, 2, 3)]
-SEMAPHORES = ["eV", "eS", "eP", "eG", "sent", "ldz", "ldv", "ldn0", "ldn1", "ldr0", "ldr1", "out", "cd1", "cd2", "cd3", "cd4", "cr1", "cr2"] + MSGS
+SEMAPHORES = ["eV", "eS", "eP", "eG", "sent", "ldz", "ldx", "ldv", "ldn0", "ldn1", "ldr0", "ldr1", "out", "cd2", "cd3", "cd4", "cr1", "cr2"] + MSGS
 WIDE = {f32: 4, i32: 4, b16: 2, u16: 2, f16: 2}
 PLACE, SCRATCH = {}, {}
 for _k, (_w, _s, _d) in TILE.items():
@@ -80,8 +78,12 @@ def _isv(x):
     return isinstance(x, tuple) and x[0] in ("ap", "ind")
 
 
+def _real(x):
+    return TILE[x[1][1] if x[0] == "ind" else x[1]][2] in (f32, b16)
+
+
 def program():
-    ops, part = [], [0]
+    ops, part = [], [(0, 0, "")]
     C, O = COST, OPT
 
     def add(eng, calls, cost, w, r, **kw):
@@ -106,8 +108,8 @@ def program():
             cost = 65 + n * C["c"]
         else:
             f = 0.5 if all(WIDE[TILE[x[1]][2]] == 2 for x in vs if _n(x) > 1) else 1.0
-            if meth == "tensor_tensor" and all(TILE[x[1]][0] == "sbuf" for x in vs[1:]):
-                f = 2.0
+            if meth == "tensor_tensor":
+                f = 2.0 if all(TILE[x[1]][0] == "sbuf" for x in vs[1:]) else 1.0
             cost = 20 + max(64, n * f) * C["c"]
         add(eng, [(meth, args, kw or {})], cost, w, r)
 
@@ -118,20 +120,23 @@ def program():
         comp("V", "tensor_tensor", [out, a, b, op])
 
     def either(func, a, kw):
+        out = ops[-1]["calls"][0][1][0]
+        if not (_real(out) and _real(a)) or out[0] == "ind":
+            return
         first = ops.pop()
-        comp("S", "activation", [first["calls"][0][1][0], a, func], kw)
+        comp("S", "activation", [out, a, func], kw)
         other = ops.pop()
         first["r"] = first["r"] + [x for x in other["r"] if x not in first["r"]]
         first["alt"] = {"V": (first["calls"], first["cost"]), "S": (other["calls"], other["cost"])}
         ops.append(first)
 
-    def cp(out, a, eng="V"):
-        if eng != "S":
-            comp("V", "tensor_copy", [out, a])
-        if eng == "E":
-            either(ACT.Copy, a, {})
+    def cp(out, a, eng="E"):
         if eng == "S":
             comp("S", "activation", [out, a, ACT.Copy])
+            return
+        comp("V", "tensor_copy", [out, a])
+        if eng == "E":
+            either(ACT.Copy, a, {})
 
     def aff(out, a, scale, bias=None):
         if bias is None:
@@ -164,6 +169,9 @@ def program():
             cost += max(min(64, _n(l)), _n(x)) * (4 if TILE[x[1]][2] == f32 else 1) * C["pe"]
         add("P", [("matmul", list(m), {}) for m in lst], cost + 30, w, r)
 
+    def acc(out, l, x, start=False, stop=False):
+        return (out, l, x, start, stop)
+
     def dma(q, out, in_, sem, lat):
         add(q, [("dma_start", [out, in_], {})], 60.0, [out] if out[0] == "ap" else [], [in_] if in_[0] == "ap" else [], sem=sem, lat=lat)
 
@@ -171,42 +179,72 @@ def program():
         add("G", [("remote", [dst, src, hop, sem], {})], 800.0, [], [src], sem="sent", lat=C["rem"] + more)
         add("R", [], 0.0, [dst], [], sem=sem, lat=C["rem"], after=len(ops) - 1)
 
-    def turn(y, yc, nq, k, out, ps, plus=0.0):
-        mm([(A(ps, 0, 64 * nq), A("R16"), A(y, 0, 64 * nq), True, True)])
-        cp(A(yc, 0, 64 * nq), A(ps, 0, 64 * nq), O["yc"])
-        if plus:
-            ts(out, IND(A(yc, 0, 128 * k), A("GO", 0, k)), plus, ALU.add)
+    def zero(tiles, groups):
+        at, names = 0, list(tiles)
+        for n in groups:
+            some, names = names[:n], names[n:]
+            ms(A(some[0], 0, sum(tiles[x] for x in some)), 0.0)
+            ops[-1]["w"] = [A(x) for x in some]
+
+    def turn(y, yc, nq, k, ps, c0=0, keys=False):
+        out, src = A(ps, c0, c0 + 64 * nq), A(y, 0, 64 * nq)
+        if keys:
+            mm([acc(out, A("R16"), src, True), acc(out, A("L1"), A("CT", 0, 64)), acc(out, A("L2"), A("CT", 0, 64)), acc(out, A("NR16"), src, False, True)])
         else:
-            cp(out, IND(A(yc, 0, 128 * k), A("GO", 0, k)), "E" if TILE[out[1]][2] == f32 else "V")
+            mm([acc(out, A("R16"), src, True, True)])
+        cp(A(yc, 0, 64 * nq), out)
+        return IND(A(yc, 0, 128 * k), A("GO", 0, k))
 
     dma("Y", A("VS"), ("hbm", "vs", None), "ldv", 1800)
-    dma("Y", A("XX0", 0, 256), ("hbm", "z", None), "ldz", 1900)
-    dma("S", A("ND", 0, 512), ("hbm", "nd", (0, 512)), "ldn0", 3000)
-    dma("Y", A("ND", 512, 1024), ("hbm", "nd", (512, 1024)), "ldn1", 3200)
-    dma("S", A("R0", 0, 1152), ("hbm", "rg", (0, 1152)), "ldr0", 3800)
-    dma("Y", A("R0", 1152, 2048), ("hbm", "rg", (1152, 2048)), "ldr1", 4300)
+    dma("S", A("R0", Z, Z + 1152), ("hbm", "rg", (0, 1152)), "ldr0", 3000)
+    dma("Y", A("ND", 0, 512), ("hbm", "nd", (0, 512)), "ldn0", 3400)
+    dma("S", A("ND", 512, 1024), ("hbm", "nd", (512, 1024)), "ldn1", 3800)
+    dma("Y", A("ZL"), ("hbm", "z", None), "ldz", 3000)
+    dma("Y", A("R0", Z + 1152, Z + 2048), ("hbm", "rg", (1152, 2048)), "ldr1", 4300)
+    dma("Y", A("XX0", 256, 320), ("hbm", "z", (0, 64)), "ldx", 4300)
     ms(A("ONE"), 1.0, False)
+    sel(A("ID"), A("ONE", 0, 128), [[-1, 128]], ALU.is_equal, 0, 1)
     iota(A("PI", 0, 1), [[0, 1]], 0, 1)
     iota(A("IT"), [[-1, 128]], 128, 1)
     iota(A("COLI"), [[1, 32]], 0, 0)
-    sel(A("ID"), A("ONE", 0, 128), [[-1, 128]], ALU.is_equal, 0, 1)
     sel(A("BO"), A("ONE", 0, 128), [[-16, 8], [0, 16]], ALU.is_ge, 0, 1)
     sel(A("BO"), A("BO"), [[16, 8], [0, 16]], ALU.is_ge, 15, -1)
-    for j in range(4):
-        sel(A("REP", 512 * j, 512 * j + 512), A("ONE"), [[-1, 32], [0, 16]], ALU.is_equal, -32 * j, 1)
+    sel(A("IW"), A("ONE", 0, 288), [[0, 2], [-16, 8], [-1, W]], ALU.is_equal, 2, 1)
+    sel(A("IW"), A("IW"), [[0, 16], [1, W]], ALU.is_ge, -2, 0)
+    for i in range(16):
+        cp(A("REP", i, 2048, 16), A("ID"))
     ts(A("IT2"), A("IT"), 15, ALU.bitwise_and)
     ts(A("R16"), A("IT2"), 0.0, ALU.is_equal)
-    cp(A("ID32"), A("ID"), "E")
-    aff(A("UW", 0, 128), A("ID"), -B)
-    aff(A("UW", 128, 256), A("ID"), B)
-    aff(A("NID"), A("ID"), -1.0)
+    aff(A("NR16"), A("R16"), -1.0)
+    cp(A("ID32"), A("ID"))
+    aff(A("NID32"), A("ID"), -1.0)
+    aff(A("ID2K"), A("ID"), 2048.0)
+    aff(A("UW", 0, 144), A("IW", 0, 144), -B)
+    aff(A("UW", 144, 288), A("IW", 0, 144), B)
+    bo = A("BO", 0, 128, 16)
     for k in range(3):
-        aff(A("BO24", 8 * k, 8 * k + 8), A("BO", 0, 128, 16), 2048.0)
-    cp(A("BO24", 24, 32), A("BO", 0, 128, 16), "E")
-    ms(A("CST", 0, 128), 0.0)
-    ms(A("CST", 128, 384), -B / 128)
+        aff(A("BO4K", 8 * k, 8 * k + 8), bo, 4096.0)
+    cp(A("BO1", 0, 8), bo)
+    cp(A("BSEL", 0, 8), bo)
+    aff(A("BSEL", 8, 16), bo, -1.0)
+    aff(A("BOS", 0, 24), A("BO4K", 0, 24), 15.0 * B / 4096 / 4096)
+    aff(A("BK0", 0, 24), A("BO4K", 0, 24), 12 * 15.0 * B / 4096 / 4096)
     ms(A("RST"), 0.0)
-    ms(A("RST", 0, 384, 16), -4 * B)
+    ms(A("RST", 0, 432, W), -4 * B)
+    for n in ("L1", "L2", "CT", "CG"):
+        ms(A(n), 0.0)
+    for n, p, v in (("L1", 0, 1.0), ("L1", 32, 1.0), ("L1", 64, 11.0), ("L2", 0, -1.0), ("L2", 96, 7.0)):
+        ms(A(n, 0, 128, 1, p, p + 1), v)
+    for c0, c1, v in ((0, 64, R2K), (64, 80, 1024.0), (80, 144, 32.0 * 16384)):
+        ms(A("CT", c0, c1, 1, 0, 1), v)
+    ms(A("CG", 0, 16, 1, 0, 1), 2048.0)
+    ms(A("CC", 0, 432), 0.0)
+    ms(A("CC", 432, 864), 0.0)
+    for p, c0, c1, st, v in ((0, 0, 432, 1, RB), (0, 432, 864, 1, RB), (0, 1, 864, W, 0.0), (0, 432, 864, W, 0.0),
+                             (32, 0, 144, 1, -B), (32, 144, 432, 1, -2 * B), (32, 432, 864, 1, -B), (32, 576, 720, 1, -2 * B), (32, 0, 432, W, -B),
+                             (32, 432, 864, W, 0.0), (32, 1, 432, W, 0.0), (32, 577, 720, W, 0.0),
+                             (64, 1, 288, W, NONE0 / 11), (96, 577, 720, W, NONE1 / 7)):
+        ms(A("CC", c0, c1, st, p, p + 1), v)
     for i, (v, o) in enumerate(((4, ALU.arith_shift_right), (15, ALU.bitwise_and), (8, ALU.bitwise_and), (7, ALU.bitwise_and), (3, ALU.bitwise_and))):
         ts(A("PI", 1 + i, 2 + i), A("PI", 0, 1), v, o)
     cp(A("COL", 0, 5), A("PI", 1, 6))
@@ -216,78 +254,80 @@ def program():
     ts(A("SO"), A("COLI", 0, 4), 128.0, ALU.mult, A("COL", 5, 6), ALU.add)
     ts(A("GO"), A("COLI", 0, 4), 128.0, ALU.mult, A("COL", 6, 7), ALU.add)
     cp(A("EX"), A("COLI", 0, 16))
+    ts(A("EXK"), A("COLI", 0, 16), float(W), ALU.mult, W - 1.0, ALU.add)
     ts(A("RA"), A("COLI", 0, 2), 0.0, ALU.mult, A("COL", 4, 5), ALU.add)
-    ms(A("YV", 0, sum(ZERO.values())), 0.0)
-    ops[-1]["w"] = [A(n) for n in ZERO]
-    ms(A("KA0"), 12.0)
-    ms(A("D0", 1024, 1152), 0.0)
-    ms(A("R0", 3200, 4096), 0.0)
-    ms(A("COL", 7, 8), 1023.5)
-    ms(A("COL", 8, 9), 0.5)
-    ms(A("COL", 9, 11), 1.0)
-    ms(A("COL", 11, 13), 0.0)
-    for h in (0, 1):
-        for j in O["sign"][h]:
-            ms(A("COL", 9 + h, 10 + h, 1, 32 * j, 32 * j + 32), 2.0)
-            ms(A("COL", 11 + h, 12 + h, 1, 32 * j, 32 * j + 32), -16.0)
-    cp(A("D0", 0, 512), A("ND", 0, 512))
-    cp(A("D0", 512, 1024), A("ND", 512, 1024))
-    cp(A("R0", 2048, 3200), A("R0", 0, 1152))
-    cp(A("R0", 4096, 4672), A("R0", 0, 576))
-    cp(A("R0", 4672, 5248), A("R0", 576, 1152), "S")
-    ms(A("R0", 0, 1), 256.0)
-    mm([(A("pM0", 128 * h, 128 * h + 128), A("XX0", 128 * h, 128 * h + 128), A("ID"), True, True) for h in (0, 1)])
-    cp(A("XX0", 256, 512), A("pM0", 0, 256), "S")
+    zero(ZERO, (1, 6))
+    for h in "01":
+        ms(A("SC" + h, 432, 576), 0.0)
+    ms(A("R0", Z + 3200, Z + 4096), 256.0)
+    cp(A("R0", Z + 2048, Z + 3200), A("R0", Z, Z + 1152), "V")
+    cp(A("R0", Z + 4096, Z + 5248), A("R0", Z, Z + 1152), "V")
+    ms(A("R0", Z, Z + 2049, 2048), 256.0)
+    mm([acc(A("pM0", 128 * h, 128 * h + 128), A("ZL", 128 * h, 128 * h + 128), A("ID"), True, True) for h in (0, 1)])
+    cp(A("XX0", 0, 256), A("pM0", 0, 256))
     cp(A("VS32"), A("VS"))
     cp(IND(A("YV"), A("SO", 0, 4)), A("VS32"))
-    turn("YV", "YVC", 8, 4, A("VL"), "pA")
+    cp(A("VL"), turn("YV", "YVC", 8, 4, "pA"))
     for t in range(NT):
         n = "VV0" if t == 0 else "SV%d" % t
-        aff(A(n, 0, 16), A("VL", 16 * t, 16 * t + 16), 1.0, -1023.5)
-        aff(A(n, 16, 32), A("VL", 16 * t, 16 * t + 16), -1.0, NONE + 1023.5)
+        cp(A(n, 0, 16), A("VL", 16 * t, 16 * t + 16))
+        aff(A(n, 16, 32), A("VL", 16 * t, 16 * t + 16), -1.0, NONE0 + 1024)
         if t:
-            cp(A(n, 32, 48), A("VS32", 16 * t, 16 * t + 16), "E")
+            cp(A(n, 32, 48), A("VS32", 16 * t, 16 * t + 16))
     for t in (1, 2, 3):
         send(A("XX0"), A("XX%d" % t), t, "xx%d" % t, 12000.0)
         send(A("SV%d" % t), A("VV%d" % t), t, "vv%d" % t, 8000.0)
-    at, names = 0, list(ZERO2)
-    for some in (names[:2], names[2:4], names[4:14], names[14:-1], names[-1:]):
-        ms(A(names[0], at, at + sum(ZERO2[n] for n in some)), 0.0)
-        ops[-1]["w"] = [A(n) for n in some]
-        at += sum(ZERO2[n] for n in some)
-    ms(A("RST8", 0, 512, 8), 4 * B)
-    for k in range(3):
-        fill(A("CG", 8 * k, 8 * k + 8), -16 * k if O["en"] == "S" else 0)
+    cp(A("D1", Z, Z + 512), A("ND", 0, 512))
+    cp(A("D1", Z + 512, Z + 1024), A("ND", 512, 1024))
+    ms(A("D1", Z + 1024, Z + 1152), 0.0)
+    zero(ZERO2, (2, 2, 8, 1))
+    ms(A("RST8", 0, 512, 8), 8192.0)
+    for t in range(3):
+        fill(A("SK%d" % t, 24, 32), 0)
     sel(A("TRI"), A("BO"), [[1, 128]], ALU.is_ge, 0, -1)
     sel(A("TP"), A("TRI"), [[-1, 128]], ALU.not_equal, 0, 1, 64.0)
-    sel(A("TN"), A("TRI"), [[-1, 128]], ALU.not_equal, 0, 1, -31.0)
     aff(A("NTRI"), A("TRI"), -1.0)
+    aff(A("TN"), A("TRI"), 16384.0)
+    sel(A("TN"), A("TN"), [[-1, 128]], ALU.not_equal, 0, 1, -31.0 * 16384)
+    sel(A("TQ"), A("NTRI"), [[-1, 128]], ALU.not_equal, 0, 1, 64.0)
     sel(A("DG"), A("ONE", 0, 160), [[-1, 160]], ALU.is_equal, 16, 1)
     for t in (0, 8, 2, 10):
         sel(A("SL%d" % t), A("DG"), [[0, 10], [1, 16]], ALU.is_equal, -t, 0)
     for j in range(4):
         sel(A("BJ", 512 * j, 512 * j + 512), A("ONE"), [[-1, 4], [-16, 8], [0, 16]], ALU.is_equal, -4 * j, 1)
     off = [0, 64, 192, 384, 640]
-    fill(A("MASK", 0, 640, 1, 0, 16), 4096)
     for c in range(4):
+        iota(A("MASK", off[c], off[c + 1]), [[0, 64 * c + 64]], 16 * c - 32, 1)
+    sel(A("MASK"), A("MASK"), [[0, 640]], ALU.is_ge, -32, 1)
+    fill(A("MASK", 0, 640, 1, 0, 16), -int(BIG))
+    for c in range(4):
+        w = 16 * c + 16
         x = A("MASK", off[c], off[c + 1], 1, 0, 16)
-        sel(x, x, [[-1, 2], [0, 2], [1, 16 * c + 16]], ALU.is_ge, -16 * c, -1)
-    sel(A("R16B", 0, 128, 1, 0, 16), A("ONE", 0, 128, 1, 0, 16), [[0, 8], [-1, 16]], ALU.is_equal, 0, 1)
-    sel(A("CSEL"), A("ONE", 0, 256), [[-16, 4], [0, 64]], ALU.is_ge, 0, 1)
-    sel(A("CSEL"), A("CSEL"), [[16, 4], [0, 64]], ALU.is_ge, 15, -1)
-    iota(A("NV"), [[1, 128]], 2048 + 1024, 0)
+        sel(x, x, [[0, 4], [-1, w]], ALU.is_ge, 16 * c - 1, 1, BIG)
+        x = A("MASK", off[c], off[c] + w, 1, 0, 16)
+        sel(x, x, [[1, w]], ALU.not_equal, -16 * c, -1, 0.0)
+    for j in (0, 1):
+        cp(A("R16B", 128 * j, 128 * j + 128), A("R16"))
+    fill(A("CSEL"), 8192)
+    sel(A("CSEL"), A("CSEL"), [[-16, 4], [0, 128]], ALU.is_ge, 0, 1)
+    sel(A("CSEL"), A("CSEL"), [[16, 4], [0, 128]], ALU.is_ge, 15, -1)
+    for n, at in (("SEA", 0), ("SEB", 8)):
+        fill(A(n), 0)
+        sel(A(n), A(n), [[-1, 8], [0, 16]], ALU.not_equal, -at, 1, -8192.0)
+        sel(A(n), A(n), [[-1, 8], [0, 16]], ALU.not_equal, -16, 1, BIG)
+    fill(A("BSB"), 0)
+    for c in (4, 12, 16, 20):
+        cp(A("BSB", c, c + 4), A("BO", 0, 64, 16))
+    iota(A("NV"), [[1, 128]], 2048 + 1024 - 8192, 0)
     aff(A("KEEP"), A("R16", 0, 16), -1.0, 1.0)
-    iota(A("DUM", 0, 12), [[16, 12]], 1152, 0)
-    iota(A("DUM", 12, 32), [[16, 20]], 3200, 0)
-    ts(A("DUM"), A("DUM"), A("COL", 1, 2), ALU.add)
     for t in (0, 2):
         n = "ADD%d" % t
-        iota(A(n, 0, 8), [[-16, 8]], -1152, 0)
-        fill(A(n, 8, 12), 1024 + 32 * t - 1152 - 128)
-        iota(A(n, 12, 24), [[2048 - 64, 3], [-16, 4]], -3200, 0)
-        iota(A(n, 24, 32), [[2048 - 64, 2], [0, 4]], 1024 + 32 * t - 3200 - 192, 0)
-        ts(A(n, 0, 8), A(n, 0, 8), A("COL", 1, 2), ALU.subtract)
-        ts(A(n, 12, 24), A(n, 12, 24), A("COL", 1, 2), ALU.subtract)
+        fill(A(n, 0, 8), Z)
+        iota(A(n, 8, 12), [[16, 4]], Z + 1024 + 32 * t, 0)
+        iota(A(n, 12, 24), [[2048, 3], [0, 4]], Z, 0)
+        iota(A(n, 24, 32), [[2048, 2], [16, 4]], Z + 1024 + 32 * t, 0)
+        ts(A(n, 8, 12), A(n, 8, 12), A("COL", 1, 2), ALU.add)
+        ts(A(n, 24, 32), A(n, 24, 32), A("COL", 1, 2), ALU.add)
     nx = [0]
 
     def xbank(h):
@@ -295,195 +335,176 @@ def program():
         return ("pX%d" if nx[0] % 2 else "pM%d") % h
 
     def nodes(t):
-        return A("D%d" % t, 0, 1152)
+        return A("D%d" % t, Z, Z + 1152) if t else A("ND")
 
-    def recs(t):
-        return A("R%d" % ((t + 1) // 2))
+    def recs(t, c0=Z):
+        return A("R%d" % ((t + 1) // 2), c0)
 
-    def pen(out, cnt, need):
-        ts(out, cnt, need, ALU.is_lt)
-        either(ACT.Relu, cnt, {"bias": need, "scale": -1.0})
-        return A("UW", 0, 128)
+    def whole(t, h):
+        return h == 0 and t % 2 == 0
 
-    def guards(t, h):
-        H = str(h)
-        K, KH, gu, rg, cm, pn, pM = [x + H for x in ("K", "KH", "GU", "RGG", "CMG", "PENG", "pM")]
-        xt, init = A("XX%d" % t, 256 + 128 * h, 384 + 128 * h), A("VV%d" % t, 16 + 8 * h, 24 + 8 * h)
-        if t == 0:
-            ms(A(K), NONE - 1023.5)
-            cp(A(K, 16, 24), init)
-            ms(A(KH), NONE)
-            return
-        gm = "GM%d%d" % (t, h)
-        cp(A(gu, 0, 24), A(gm, 32, 56))
-        cp(A(rg), IND(recs(t), A(gu, 0, 24)), "S")
-        mm([(A(pM, 128 * k, 128 * k + 128), xt, A("ID"), True, True) for k in range(3)])
-        tt(A(cm), A(rg), A(pM, 0, 384), ALU.is_le)
-        mm([(A(pM, 8 * k, 8 * k + 8), A(cm, 128 * k, 128 * k + 128), A("BO24", 24, 32), True, True) for k in range(3)] +
-           [(A(pM, 32, 56), A("ONE", 0, 128), A("CG", 0, 24), True, False), (A(pM, 32, 56), A("ID32"), A(gm, 0, 24), False, False)] +
-           [(A(pM, 32 + 8 * k, 40 + 8 * k), A(rg, 128 * k, 128 * k + 128), A("BO24", 0, 8), False, k == 2) for k in range(3)])
-        ts(A("DF" + H, 0, 24), A(pM, 0, 24), A("KA%d" % t, 0, 1), ALU.is_lt, -B, ALU.mult)
-        tt(A("DF" + H, 0, 24), A("DF" + H, 0, 24), A(pM, 32, 56), ALU.add)
-        ts(A(K, 0, 16), A("DF" + H, 0, 16), NONE - 1023.5, ALU.max)
-        tt(A(K, 16, 24), A("DF" + H, 16, 24), init, ALU.max)
-        ts(A(KH, 0, 24), A(K, 0, 24), RND, ALU.add, RND, ALU.subtract)
+    def names(out, keys):
+        mm([acc(out, A("ID32"), keys, True), acc(out, A("L1"), A("CT", 0, 8)), acc(out, A("L2"), A("CT", 0, 8)), acc(out, A("NID32"), keys),
+            acc(out, A("L1"), A("CT", 64, 72), False, True)])
 
     def gather(t, h, s):
         H = str(h)
         vo = A("VS16", 16 * t + 8 * h, 16 * t + 8 * h + 8) if s == 2 else A("VO" + H, 0, 8)
-        cp(A("EU" + H), IND(nodes(t), vo))
-        for c0, c1, e in O["chunks"][h]:
-            cp(A("RG" + H, c0, c1), IND(recs(t), A("EU" + H, c0 // 16, c1 // 16)), e)
-        if O["en"] == "S":
-            comp("S", "activation", [A("EN" + H), IND(nodes(t), vo), ACT.Identity], {"bias": A("COL", 7, 8), "scale": -1.0})
+        if s == 2 or (s == 0 and whole(t, h)):
+            cp(A("EU" + H), IND(nodes(t), vo))
+        else:
+            ts(A("EU" + H), IND(nodes(t), vo), 4095.0 if s else 2048.0, ALU.min)
+        for j, e in enumerate(O["gath"][h]):
+            cp(A("RG" + H, 512 * j, 512 * j + 512), IND(recs(t), A("EU" + H, 32 * j, 32 * j + 32)), e)
 
     def level(t, h, s):
         n = s + 1
         H = str(h)
-        EU, RG, CM, pV, pM, SC, K, KH, HI, NW, DF, VM = [x + H for x in ("EU", "RG", "CM", "pV", "pM", "SC", "K", "KH", "HI", "NW", "DF", "VM")]
-        xt = A("XX%d" % t, 256 + 128 * h, 384 + 128 * h)
-        vm = A("VV%d" % t, 8 * h, 8 * h + 8) if s == 2 else A(VM, 16 * s, 16 * s + 8)
-        ts(A("U" + H), A(EU), 2048.0, ALU.is_ge)
-        if s:
+        EU, RG, CM, pV, SC, NW = [x + H for x in ("EU", "RG", "CM", "pV", "SC", "NW")]
+        xt, cc, bk = A("XX%d" % t, 128 * h, 128 * h + 128), A("CC", COFF[s], COFF[s] + 144 * n), "BK%d" % t
+        lst = [acc(A(pV, 0, 144 * n), A("L1"), cc, True)]
+        if s < 2:
+            lst += [acc(A(pV, 0, 144 * n, W), A("ID32"), A(SC, W - 1, 144 * n, W)), acc(A(pV, 0, 144 * n, W), A("ID2K"), A(NW, 16 - 16 * s, 16 - 16 * s + 8 * n))]
+        if s == 1:
+            out, keys = A(pV, 145, 288, W), A(SC, 288 + W - 1, 432, W)
+            lst += [acc(out, A("NID32"), keys), acc(out, A("L1"), A("CT", 0, 8)), acc(out, A("L2"), A("CT", 0, 8)), acc(out, A("ID32"), keys)]
+        if s == 2:
+            lst += [acc(A(pV, 289, 432, W), A("ID32"), A("VV%d" % t, 16 + 8 * h, 24 + 8 * h))]
+        mm(lst)
+        if s or whole(t, h):
+            ts(A("U" + H), A(EU), 2048.0, ALU.is_ge)
+            mm([acc(A(pV, 0, 288 if s else 144), A("U" + H), A("UW", 0, 288 if s else 144))])
+        if s == 2:
             ts(A("W" + H), A(EU), 4096.0, ALU.is_ge)
-            mm([(A(pV, 0, 128 * n), A("ONE", 0, 128), A("CST", 0, 128 * n), True, False),
-                (A(pV, 0, 256), A("U" + H), A("UW"), False, False),
-                (A(pV, 128, 128 * n), A("W" + H), A("UW", 0, 128 * s), False, False)])
-        else:
-            mm([(A(pV, 0, 128), A("U" + H), A("UW", 0, 128), True, False)])
-        for k in range(n):
-            if O["en"] == "S":
-                mm([(A(pV, 128 * k, 128 * k + 128), A("EN" + H), A("ID32"), False, False)])
-            else:
-                ts(A("EH" + H, 128 * k, 128 * k + 128), A(EU), -1.0, ALU.mult, 1023.5 + 2048 * k, ALU.add)
-                mm([(A(pV, 128 * k, 128 * k + 128), A("EH" + H, 128 * k, 128 * k + 128), A("ID"), False, False)])
+            mm([acc(A(pV, 144, 432), A("W" + H), A("UW"))])
+        ts(A("E0" + H), A(EU), -1.0, ALU.mult, 1024.0, ALU.add)
+        if s:
+            ts(A("E1" + H), A(EU), -1.0, ALU.mult, 3072.0, ALU.add)
+        post = []
+        if s == 2 and t:
+            rg, cm, gm, px = "RGG" + H, "CMG" + H, "GM%d%d" % (t, h), xbank(h)
+            cp(A(rg), IND(recs(t), A("GU%d%d" % (t, h), 0, 24)), "S")
+            mm([acc(A(px, 128 * k, 128 * k + 128), xt, A("ID"), True, True) for k in range(3)])
+            tt(A(cm), A(rg), A(px, 0, 384), ALU.is_le)
+            mm([acc(A(pV, 144 * k, 144 * k + 144, W), A(cm, 128 * k, 128 * k + 128), A(bk, 0, 8)) for k in range(3)])
+            post = [acc(A(pV, 144 * k, 144 * k + 144, W), A(rg, 128 * k, 128 * k + 128), A("BO4K", 0, 8)) for k in range(3)] + \
+                   [acc(A(pV, 0, 432, W), A("ID32"), A(gm, 0, 24)), acc(A(pV, 0, 432, W), A("ID32"), A(gm, 32, 56)), acc(A(pV, 0, 432, W), A("L1"), A("CG", 0, 24))]
         for j in range(4):
             px = xbank(h)
-            cm, rg = A(CM, 512 * j, 512 * j + 512), A(RG, 512 * j, 512 * j + 512)
-            mm([(A(px), xt, A("REP", 512 * j, 512 * j + 512), True, j not in O["sign"][h])])
-            if j in O["sign"][h]:
-                mm([(A(px), A("NID"), rg, False, True)])
-                comp("S", "activation", [cm, A(px), ACT.Sign], {"bias": A("COL", 8, 9)})
-            else:
-                tt(cm, rg, A(px), ALU.is_le)
-        for q in (0, 8):
-            mm([(A(pV, i, 128 * n, 16), A(RG, i, 2048, 16), A("BO24", 0, 8 * n), False, False) for i in range(q, q + 8)])
+            mm([acc(A(px), xt, A("REP", 512 * j, 512 * j + 512), True, True)])
+            tt(A(CM, 512 * j, 512 * j + 512), A(RG, 512 * j, 512 * j + 512), A(px), ALU.is_le)
+        return post
 
-    def choose(t, h, s):
+    def choose(t, h, s, post):
         n = s + 1
         H = str(h)
-        CM, pV, pM, SC, K, KH, HI, NW, DF, VM = [x + H for x in ("CM", "pV", "pM", "SC", "K", "KH", "HI", "NW", "DF", "VM")]
-        vm = A("VV%d" % t, 8 * h, 8 * h + 8) if s == 2 else A(VM, 16 * s, 16 * s + 8)
-        mm([(A(pM, i, 128, 16), A(CM, i, 2048, 16), A("BO24", 24, 32), True, True) for i in range(16)])
-        big = pen(A("PEN" + H), A(pM, 0, 128), A("KC", 2 * t + h, 2 * t + h + 1))
-        mm([(A(pV, 128 * k, 128 * k + 128), big, A("PEN" + H), False, k == s) for k in range(n)])
-        comp("V", "tensor_tensor_scan", [A(SC, 0, 128 * n), A("RST", 0, 128 * n), A(pV, 0, 128 * n), -4 * B, ALU.add, ALU.max])
-        if s == 2:
-            guards(t, h)
-        best, m = A(SC, 15, 128 * n, 16), 8 * n
-        if O["t2"]:
-            aff(A("TH" + H, 0, m), A(KH, 0, m), 1.0, 1024.0)
-            tt(A(NW, 0, m), best, A("TH" + H, 0, m), ALU.is_gt)
-        ts(A(HI, 0, m), best, RND, ALU.add, RND, ALU.subtract)
-        tt(A(DF, 0, m), best, A(K, 0, m), ALU.subtract)
-        if not O["t2"]:
-            tt(A(NW, 0, m), A(HI, 0, m), A(KH, 0, m), ALU.is_gt)
-        tt(A(DF, 0, m), A(DF, 0, m), A(NW, 0, m), ALU.mult)
-        tt(A(KH, 0, m), A(KH, 0, m), A(HI, 0, m), ALU.max)
-        tt(A(K, 0, m), A(K, 0, m), A(DF, 0, m), ALU.add)
-        if s:
-            v2 = A(VM, 16 * s - 16, 16 * s - 8)
-            tt(IND(A("Y" + H), A("SO", 0, 1)), A(KH, 8 * s, 8 * s + 16), A(K, 8 * s, 8 * s + 16), ALU.subtract)
-            turn("Y" + H, "YC" + H, 1, 1, A("VO" + H), pM, 1023.5)
-            if s == 2 or h == 0:
-                tt(v2, A(KH, 8 * s, m), A(K, 8 * s, m), ALU.subtract)
-            if s == 2:
-                aff(A("FX" + H, 0, 8), v2, -1.0, NONE)
-                tt(A(K, 8, 16), A(K, 8, 16), A("FX" + H, 0, 8), ALU.max)
+        RG, CM, pV, SC, NW = [x + H for x in ("RG", "CM", "pV", "SC", "NW")]
+        mm([acc(A(pV, 2 + i, 144 * n, W), A(CM, i, 2048, 16), A("BK%d" % t, 0, 8 * n)) for i in range(16)] +
+           [acc(A(pV, 0, 144 * n), A("L2"), A("CC", COFF[s], COFF[s] + 144 * n)), acc(A(pV, 0, 144), A("E0" + H), A("IW", 0, 144))] +
+           [acc(A(pV, 144, 144 * n), A("E1" + H), A("IW", 0, 144 * s))] * (s > 0) + post +
+           [acc(A(pV, 2 + i, 144 * n, W), A(RG, i, 2048, 16), A("BO4K", 0, 8 * n), False, i == 15) for i in range(16)])
+        comp("V", "tensor_tensor_scan", [A(SC, 0, 144 * n), A("RST", 0, 144 * n), A(pV, 0, 144 * n), -4 * B, ALU.add, ALU.max])
         k = 1 - t % 2
-        if h == 0 and s >= k:
-            nw = A(NW, 8 * k, 8 * k + 8)
-            if s == 2:
-                aff(A("DV", 0, 8), vm, 1.0, 1023.5)
-                tt(A("HM", 0, 8), A("DV", 0, 8), nw, ALU.mult)
+        if s:
+            if O["turn"][h] == "E":
+                out = A(pV, 448, 456)
+                tt(A("KE" + H), IND(A(SC, 144 * s, 144 * n), A("EXK", 0, 8)), A("R16"), ALU.mult)
+                mm([acc(out, A("KE" + H), A("BSEL", 0, 8), True), acc(out, A("L1"), A("CT", 0, 8)), acc(out, A("L2"), A("CT", 0, 8)),
+                    acc(out, A("KE" + H), A("BSEL", 8, 16), False, True)])
+                ts(A("VO" + H, 0, 8), out, 1024.0, ALU.add)
             else:
-                aff(A("AB", 8, 16), vm, 1.0, 1023.5)
-                tt(A("DV", 0, 8), A("AB", 8, 16), A("HM", 0, 8), ALU.subtract)
-                tt(A("DV", 0, 8), A("DV", 0, 8), nw, ALU.mult)
-                tt(A("HM", 0, 8), A("HM", 0, 8), A("DV", 0, 8), ALU.add)
+                cp(IND(A("Y" + H), A("SO", 0, 1)), A(SC, 144 * s + W - 1, 144 * s + 288, W))
+                ts(A("VO" + H), turn("Y" + H, "YC" + H, 1, 1, pV, 448, True), 1024.0, ALU.add)
+        m = (8, 16 if whole(t, h) else 8, 16)[s]
+        if s or (h == 0 and k == 0):
+            tt(A(NW, 32 - 16 * s, 32 - 16 * s + m), A(SC, W - 1, W * m, W), A(SC, 1, W * m, W), ALU.is_gt)
+        if h == 0 and s >= k:
+            nw = A(NW, 32 - 16 * s + 8 * k, 40 - 16 * s + 8 * k)
+            if s == 2:
+                tt(A("HM", 0, 8), A("VV%d" % t, 0, 8), nw, ALU.mult)
+            else:
+                tt(A("DV", 8, 16), A("DV", 0, 8), nw, ALU.mult)
+                tt(A("AB" if s == k else "HM", 0, 8), A("HM", 0, 8), A("DV", 8, 16), ALU.add)
+        if h == 0 and s:
+            out = A("pA", 16 - 8 * s, 24 - 8 * s)
+            names(out, A(SC, 144 * s + W - 1, 144 * n, W))
+            if s == 1:
+                cp(A("AB", 8, 16), out)
+            if s > k:
+                tt(A("DV", 0, 8), out if s == 2 else A("AB", 8, 16), A("HM", 0, 8), ALU.subtract)
 
     def handon(t, h):
         H = str(h)
-        K, KH, GN, NM, NZ, pM = [x + H for x in ("K", "KH", "GN", "NM", "NZ", "pM")]
-        low = A("SG%d%d" % (t, h), 0, 24) if t < 3 else A("LO" + H, 0, 24)
-        tt(low, A(K, 0, 24), A(KH, 0, 24), ALU.subtract)
-        aff(A(NM, 0, 24), low, -1.0, 1023.5)
-        ts(A(NZ, 0, 24), A(KH, 0, 24), NONE, ALU.is_gt)
-        if t == 3 or (h == 0 and t % 2):
-            tt(A(GN, 0, 24), A(NM, 0, 24), A(NZ, 0, 24), ALU.mult)
+        keys, low, pV = A("SC" + H, W - 1, 432, W), "SG%d%d" % (t, h), "pV" + H
+        ts(A("HI" + H, 0, 24), keys, R2K, ALU.add, R2K, ALU.subtract)
+        tt(A(low, 0, 24), keys, A("HI" + H, 0, 24), ALU.subtract)
         if t < 3:
-            tt(IND(A("YG" + H), A("SO", 0, 2)), A(NM), A(NZ), ALU.mult)
-            turn("YG" + H, "YGC" + H, 3, 2, A(low[1], 32, 64), pM)
-            send(A(low[1]), A("GM%d%d" % (t + 1, h)), 1, "gm%d%d" % (t + 1, h))
+            ts(A(low, 32, 56), keys, THR, ALU.is_lt, -B, ALU.mult)
+            send(A(low), A("GM%d%d" % (t + 1, h)), 1, "gm%d%d" % (t + 1, h))
+            cp(IND(A("YG" + H), A("SO", 0, 2)), A(low, 0, 32))
+            su = A("SU%d%d" % (t, h))
+            ts(su, turn("YG" + H, "YGC" + H, 3, 2, pV), -1.0, ALU.mult, 1024.0, ALU.add)
+            send(su, A("GU%d%d" % (t + 1, h)), 1, "gu%d%d" % (t + 1, h))
         else:
-            mm([(A(pM, 0, 128, 1, 0, 24), A(GN, 0, 24), A("ID32"), True, True)])
-            cp(A("YO", 128 * h, 128 * h + 128, 1, 0, 24), A(pM, 0, 128, 1, 0, 24), "E")
+            aff(A("NM" + H, 0, 24), A(low, 0, 24), -1.0, 1024.0)
+            ts(A("NZ" + H, 0, 24), keys, THR, ALU.is_ge)
+            tt(A("GN" + H, 0, 24), A("NM" + H, 0, 24), A("NZ" + H, 0, 24), ALU.mult)
+            mm([acc(A(pV, 0, 128, 1, 0, 24), A("GN" + H, 0, 24), A("ID32"), True, True)])
+            cp(A("YO", 128 * h, 128 * h + 128, 1, 0, 24), A(pV, 0, 128, 1, 0, 24))
             for k in range(3):
                 dma("Y", ("hbm", "yg", (256 * k + 128 * h, 256 * k + 128 * h + 128)), A("YO", 128 * h, 128 * h + 128, 1, 8 * k, 8 * k + 8), "out", 2000)
 
     def decide(t):
         even = t % 2 == 0
-        X, m, low = "XX%d" % t, 32 if even else 16, (1, 0, 64)
-        cp(A("EB"), A("EU0", 0, 64))
-        cp(IND(A("YA"), A("SO", 0, 1)), A("HM"))
-        turn("YA", "YAC", 1, 1, A("AO"), "pA" if even else "pB")
-        cp(A("EA"), IND(nodes(t), A("AO", 0, 4)), "E")
-        ts(A("FR"), A("EA" if even else "EB"), 0.0, ALU.is_equal)
-        either(ACT.Relu, A("EA" if even else "EB"), {"scale": -1.0, "bias": 1.0})
-        mm([(A("pA", 64, 72, *low), A("FR"), A("BO24", 24, 32), True, True)])
-        if even:
-            aff(A("AB", 8, 16), A("VM0", 0, 8), 1.0, 1023.5)
-        tt(A("Q1", 0, 8), A("HM", 0, 8), A("AB", 8, 16), ALU.not_equal)
-        tt(A("Q2", 0, 8, *low), A("pA", 64, 72, *low), A("HM", 0, 8, *low), ALU.min)
-        tt(A("Q2", 0, 8, *low), A("Q2", 0, 8, *low), A("Q1", 0, 8, *low), ALU.min)
-        tt(A("ABM", 0, 8, *low), A("HM", 0, 8, *low), A("Q2", 0, 8, *low), ALU.mult)
-        tt(A("ABM", 8, 16, *low), A("AB", 8, 16, *low), A("Q2", 0, 8, *low), ALU.mult)
-        cp(A("OTH"), IND(A("ABM"), A("EX")))
-        tt(A("OWN", 0, 128), IND(A("ABM"), A("EX", 0, 8)), A("R16"), ALU.mult)
-        tt(A("OWN", 128, 256), IND(A("ABM"), A("EX", 8, 16)), A("R16"), ALU.mult)
-        for cs in ((0, 1, 2), (3,)):
-            o0 = off[cs[0]]
-            mm([(A("pA", 0, off[cs[-1] + 1] - o0), A("R16B", 0, 128, 1, 0, 16), A("MASK", o0, off[cs[-1] + 1], 1, 0, 16), True, False)])
-            for c in cs:
-                w, lst = 16 * c + 16, []
-                for b, (o, o2) in enumerate(((0, 0), (1, 1), (0, 1), (1, 0))):
-                    out = A("pA", off[c] - o0 + b * w, off[c] - o0 + b * w + w)
-                    lst.append((out, A("OWN", 128 * o, 128 * o + 128, *low), A("CSEL", 64 * c, 64 * c + w, *low), False, False))
-                    lst.append((out, A("OTH", 128 * o2, 128 * o2 + 128, *low), A("NID", 0, w, *low), False, c == cs[-1] and b == 3))
-                mm(lst)
-            for c in cs:
-                comp("V", "tensor_reduce", [A("MN", c, c + 1), A("pA", off[c] - o0, off[c + 1] - o0), AxisListType.X, ALU.min],
-                     {"apply_absolute_value": True})
-        ts(A("ACR", 0, m), IND(A("MN"), A("RA", 0, m // 16)), 0.0, ALU.is_gt)
-        if t < 3:
-            ts(A("ACB", 0, 4), A("MN", 0, 4), 0.0, ALU.is_gt)
-            mm([(A("pA", 0, 4), A("ONE", 0, 128), A("ACB", 0, 4), True, True)])
-            comp("V", "tensor_reduce", [A("AS", 0, 1), A("pA", 0, 4), AxisListType.X, ALU.add])
-            ts(A("AS", 1, 2), A("AS", 0, 1), -0.5, ALU.add, RND2, ALU.add)
-            ts(A("SK%d" % t, 0, 1), A("AS", 1, 2), RND2 - 12.0, ALU.subtract, A("AS", 0, 1), ALU.subtract)
-            send(A("SK%d" % t, 0, 4), A("KA%d" % (t + 1)), 1, "ka%d" % (t + 1))
-        cp(A("BASE", 0, 4), A("AO", 0, 4))
-        for c in ((4, 12, 16, 20) if even else (4,)):
-            cp(A("BASE", c, c + 4), A("VO0", 0, 4))
-        tt(A("XD", 0, m), A("BASE", 0, m), A("ADD%d" % (t & 2), 0, m), ALU.add)
-        tt(A("OF", 0, m), A("XD", 0, m), A("ACR", 0, m), ALU.mult)
-        tt(A("OF", 0, m), A("OF", 0, m), A("DUM", 0, m), ALU.add)
-        cp(A("OU", 0, m), A("OF", 0, m))
-        new = A("D%d" % (t + 1))
+        X, m, low = A("XX%d" % t, 256, 320), 32 if even else 16, (1, 0, 64)
+        old, new = A("D%d" % max(t, 1), Z, Z + 1152), A("D%d" % (t + 1))
+
+        def room(e):
+            ts(A("FR"), A(e), 0.0, ALU.is_equal)
+            either(ACT.Relu, A(e), {"scale": -1.0, "bias": 1.0})
+            mm([acc(A("pA", 16, 24, *low), A("FR"), A("BO1", 0, 8), True, True)])
+
+        cp(A("EB"), IND(old, A("VO0", 0, 4)))
         if not even:
-            cp(A("G0X"), IND(A("GN0"), A("EX", 0, 8)))
-            mm([(A("pB", 0, 64), A("G0X", 0, 128, *low), A("ID", 0, 64, *low), True, True),
-                (A("pB", 64, 128), A("TP"), A("FR"), True, True)])
+            room("EB")
+            cp(A("Q2", 8, 16, *low), A("pA", 16, 24, *low))
+        tt(A("OWN"), IND(A("AB", 0, 16), A("EX")), A("R16B"), ALU.mult)
+        mm([acc(A("pA", 32, 64), A("OWN", 128, 256, *low), A("BSB", 0, 32, *low), True), acc(A("pA", 32, 36), A("OWN", 0, 128, *low), A("BSB", 4, 8, *low), False, True)])
+        cp(A("AO", 0, 4), A("pA", 32, 36))
+        tt(A("XT", 0, m), A("pA", 32, 32 + m), A("ADD%d" % (t & 2), 0, m), ALU.add)
+        cp(A("EA"), IND(old, A("AO", 0, 4)))
+        if even:
+            room("EA")
+        tt(A("Q1", 0, 8), A("AB", 0, 8), A("AB", 8, 16), ALU.not_equal)
+        tt(A("Q2", 0, 8, *low), A("pA", 16, 24, *low) if even else A("Q2", 8, 16, *low), A("AB", 0, 8, *low), ALU.min)
+        tt(A("AB", 16, 24, *low), A("Q2", 0, 8, *low), A("Q1", 0, 8, *low), ALU.min)
+        mm([acc(A("pA", 64, 128, 1, 0, 24), A("AB", 0, 24, *low), A("ID32", 0, 64, *low), True, True)])
+        cp(A("TT", 0, 64, 1, 0, 24), A("pA", 64, 128, 1, 0, 24))
+        for cs, ps in zip(((0, 1, 2), (3,)), O["cb"]):
+            o0 = off[cs[0]]
+            lst = [acc(A(ps, 0, off[cs[-1] + 1] - o0), A("R16B", 0, 128, 1, 0, 48), A("MASK", o0, off[cs[-1] + 1], 1, 0, 48), True)]
+            for c in cs:
+                w, at = 16 * c + 16, off[c] - o0
+                lst += [acc(A(ps, at + 2 * w * j, at + 2 * w * j + 2 * w), A("OWN", 128 * j, 128 * j + 128, *low), A("CSEL", 128 * c, 128 * c + 2 * w, *low)) for j in (0, 1)]
+            mm(lst)
+            for c in cs:
+                w, at = 16 * c + 16, off[c] - o0
+                mm([acc(A(ps, at + b * w, at + b * w + w), A(o, 0, 128, 1, 0, 24), A("TT", 0, w, 1, 0, 24), False, c == cs[-1] and b == 3)
+                    for b, o in enumerate(("SEA", "SEB", "SEB", "SEA"))])
+            for c in cs:
+                comp("V", "tensor_reduce", [A("MN", c, c + 1), A(ps, off[c] - o0, off[c + 1] - o0), AxisListType.X, ALU.min], {"apply_absolute_value": True})
+        tt(A("OF", 0, m), IND(A("MN"), A("RA", 0, m // 16)), A("XT", 0, m), ALU.min)
+        cp(A("OU", 0, m), A("OF", 0, m))
+        if t < 3:
+            ts(A("ACB", 0, 4), A("MN", 0, 4), 4096.0, ALU.is_gt)
+            mm([acc(A("pA", 0, 1), A("ONE", 0, 128), A("ACB", c, c + 1), c == 0, c == 3) for c in range(4)])
+            ts(A("AS", 0, 1), A("pA", 0, 1), 0.5, ALU.add, RND2, ALU.add)
+            ts(A("AS", 1, 2), A("AS", 0, 1), RND2 - 12.0, ALU.subtract, A("pA", 0, 1), ALU.subtract)
+            aff(A("SK%d" % t, 0, 24), A("BOS", 0, 24), A("AS", 1, 2))
+            send(A("SK%d" % t), A("BK%d" % (t + 1)), 1, "ka%d" % (t + 1))
+        if not even:
+            ts(A("G0X"), IND(A("SG%d0" % t, 0, 16), A("EX", 0, 8)), -1.0, ALU.mult, 1024.0, ALU.add)
+            mm([acc(A("pB", 0, 64), A("G0X", 0, 128, *low), A("ID", 0, 64, *low), True, True), acc(A("pB", 64, 128), A("TP"), A("FR"), True, True)])
             tt(A("NE"), A("EA"), A("pB", 0, 64), ALU.not_equal)
             ts(A("P0"), A("pB", 64, 128), 64.0, ALU.is_equal)
             tt(A("P0"), A("P0"), A("pB", 0, 64), ALU.mult)
@@ -492,72 +513,84 @@ def program():
             return
         for o, x, r in (("RC", "XC", 8 + t), ("RH", "XH", t)):
             aff(A(o), IND(recs(t), A("VO0", 0, 4)), A("KEEP", r, r + 1))
-            aff(A(x), A(X, 0, 64), A("R16", r, r + 1))
+            aff(A(x), X, A("R16", r, r + 1))
         for j in range(5):
             o, x = ("RC", "XC") if j < 3 else ("RH", "XH")
-            tt(IND(recs(t + 1), A("OU", 12 + 4 * j, 16 + 4 * j)), A(o), A(x), ALU.add)
+            tt(IND(recs(t + 1, 0), A("OU", 12 + 4 * j, 16 + 4 * j)), A(o), A(x), ALU.add)
         for b, r in ((0, t), (1, 8 + t)):
             out = A("pB", 64 * b, 64 * b + 64)
-            mm([(out, A("BJ", 128 * (r ^ 8), 128 * (r ^ 8) + 128), A(X, 0, 64), True, False)] +
-               [(out, A("SL%d" % r, r + 16 - i, r + 144 - i), A("RG0", i, 1024, 16), False, i == 15) for i in range(16)])
+            mm([acc(out, A("BJ", 128 * (r ^ 8), 128 * (r ^ 8) + 128), X, True)] +
+               [acc(out, A("SL%d" % r, r + 16 - i, r + 144 - i), A("RG0", i, 1024, 16), False, i == 15) for i in range(16)])
         ts(A("NGS"), A("pB", 0, 128), 0.0, ALU.is_lt)
         tt(A("STR"), A("NGS", 0, 64), A("NGS", 64, 128), ALU.mult)
         tt(A("EBN"), A("EB"), A("NGS", 0, 64), ALU.mult)
-        cp(A("EHI"), A("EB"), "E")
+        ts(A("EHI"), A("EB"), R1K, ALU.add, R1K, ALU.subtract)
         tt(A("ELO"), A("EB"), A("EHI"), ALU.subtract)
-        mm([(A("pB", 0, 64), A("TN"), A("STR"), True, True), (A("pB", 64, 128), A("TP"), A("FR"), True, True),
-            (A("pB", 128, 192), A("BO"), A("FR"), True, False), (A("pB", 128, 192), A("NTRI"), A("STR"), False, True)])
-        aff(A("NB"), A("pB", 0, 64), 16384.0, 96.0 * 16384.0)
-        aff(A("PL"), A("pB", 64, 128), -16384.0)
+        mm([acc(A("pB", 0, 64), A("L1"), A("CT", 80, 144), True), acc(A("pB", 0, 64), A("TN"), A("STR"), False, True),
+            acc(A("pB", 64, 128), A("TP"), A("FR"), True, True),
+            acc(A("pB", 128, 192), A("BO"), A("FR"), True), acc(A("pB", 128, 192), A("NTRI"), A("STR"), False, True),
+            acc(A("pB", 192, 256), A("TQ"), A("FR"), True), acc(A("pB", 192, 256), A("BO"), A("STR"), False, True)])
+        tt(A("NBE"), A("pB", 0, 64), A("EHI"), ALU.add)
+        aff(A("PL"), A("pB", 64, 128), -16384.0, 64.0 * 16384)
         ts(A("P0"), A("pB", 64, 128), 64.0, ALU.is_equal)
         ts(A("PUT"), A("pB", 128, 192), 0.0, ALU.is_gt)
-        for b, ps in ((1, "pB"), (0, "pA")):
+        ts(A("M1"), A("pB", 192, 256), 64.0, ALU.is_lt, -8192.0, ALU.mult)
+        for b, ps in enumerate(O["zb"]):
             for q in (0, 4):
                 lst = []
                 for j in range(q, q + 4):
                     out, bj = A(ps, j, 512, 8), A("BJ", 128 * (8 * b + j), 128 * (8 * b + j) + 128)
-                    lst += [(out, A("ID"), A("PL"), True, False), (out, bj, A("NB"), False, False), (out, bj, A("EHI"), False, False),
-                            (out, bj, A("ELO"), False, True)]
+                    lst += [acc(out, A("ID"), A("PL"), True), acc(out, bj, A("NBE")), acc(out, bj, A("ELO"), False, True)]
                 mm(lst)
             comp("S", "activation", [A("ZA", 512 * b, 512 * b + 512), A(ps), ACT.Abs])
-            comp("V", "tensor_tensor_scan", [A("ZS", 512 * b, 512 * b + 512), A("RST8"), A("ZA", 512 * b, 512 * b + 512), 4 * B, ALU.add, ALU.min])
+            comp("V", "tensor_tensor_scan", [A("ZS", 512 * b, 512 * b + 512), A("RST8"), A("ZA", 512 * b, 512 * b + 512), 0.0, ALU.max, ALU.min])
+        aff(A("NE"), A("EA"), 1.0, -8192.0)
         tt(A("P0"), A("P0"), A("NV", 32 * t, 32 * t + 64), ALU.mult)
-        tt(A("P0"), A("P0"), A("EA"), ALU.add)
+        tt(A("M1"), A("M1"), A("NE"), ALU.add)
+        tt(A("P0"), A("P0"), A("M1"), ALU.add)
         tt(A("PUT"), A("PUT"), A("STR"), ALU.mult)
         tt(A("EP"), A("EB"), A("PUT"), ALU.mult)
         tt(IND(new, A("OU", 4, 8)), A("EBN"), A("EP"), ALU.subtract)
         tt(IND(new, A("OU", 8, 12)), A("EB"), A("EBN"), ALU.subtract)
-        tt(A("RES"), A("ZS", 7, 512, 8), A("ZS", 519, 1024, 8), ALU.min)
-        ts(A("RM"), A("RES"), 8192.0, ALU.is_lt)
-        tt(A("RM"), A("RM"), A("RES"), ALU.mult)
-        tt(IND(new, A("OU", 0, 4)), A("P0"), A("RM"), ALU.add)
+        tt(A("P0"), A("P0"), A("ZS", 7, 512, 8), ALU.add)
+        tt(IND(new, A("OU", 0, 4)), A("P0"), A("ZS", 519, 1024, 8), ALU.add)
 
     def copies(t):
         last = len(ops) - 1
-        dma("Y", nodes(t + 1), nodes(t), "cd%d" % (t + 1), 3000)
-        ops[-1]["also"] = last
+        if t:
+            dma("Y", nodes(t + 1), nodes(t), "cd%d" % (t + 1), 3000)
+            ops[-1]["also"] = last
         if t % 2 == 0:
             dma("Y", recs(t + 1), recs(t), "cr%d" % (t // 2 + 1), 6000)
             ops[-1]["also"] = last
         if t == 3:
-            dma("Y", ("hbm", "yr", None), A("R2", 2048, 3200), "out", 3000)
+            dma("Y", ("hbm", "yr", (0, 2)), A("R2", Z + 4096, Z + 4098), "out", 3000)
+            ops[-1]["also"] = last
+            dma("Y", ("hbm", "yr", (2, 1152)), A("R2", Z + 2050, Z + 3200), "out", 3000)
             ops[-1]["also"] = last
 
     for t in range(NT):
         even = t % 2 == 0
         cp(A("VS16", 16 * t, 16 * t + 16), A("VV%d" % t, 32, 48) if t else A("VS", 0, 16))
         for h in (0, 1):
-            aff(A("KC", 2 * t + h, 2 * t + h + 1), A("KA%d" % t, 0, 1), A("COL", 9 + h, 10 + h), A("COL", 11 + h, 12 + h))
-            steps = []
             for s in (2, 1, 0):
-                steps += [(gather, t, h, s), (level, t, h, s)] + [(decide, t)] * (s == 0 and h == 0 and even) + [(choose, t, h, s)]
-            for step in steps + [(handon, t, h)] + [(decide, t)] * (h == 0 and not even):
-                part[0] += 1
-                step[0](*step[1:])
-                if step == (choose, t, 0, 2):
+                part[0] = (t, h, "walk")
+                gather(t, h, s)
+                post = level(t, h, s)
+                if s == 0 and h == 0 and even:
+                    part[0] = (t, h, "act")
+                    decide(t)
+                    part[0] = (t, h, "walk")
+                choose(t, h, s, post)
+                if (h, s) == (0, 2):
                     copies(t)
-    dma("Y", ("hbm", "yn", (0, 576)), A("D4", 0, 576), "out", 3000)
-    dma("S", ("hbm", "yn", (576, 1152)), A("D4", 576, 1152), "out", 3000)
+            part[0] = (t, h, "hand")
+            handon(t, h)
+            if h == 0 and not even:
+                part[0] = (t, h, "act")
+                decide(t)
+    dma("Y", ("hbm", "yn", (0, 576)), A("D4", Z, Z + 576), "out", 3000)
+    dma("S", ("hbm", "yn", (576, 1152)), A("D4", Z + 576, Z + 1152), "out", 3000)
     return ops
 
 
@@ -593,7 +626,7 @@ def order(ops):
     rank = [0.0] * n
     for i in range(n - 1, -1, -1):
         rank[i] = dur[i] + max([rank[j] + C["lat"] for j in suc[i]], default=0.0)
-    rank = [rank[i] + 100.0 * URGE.get(ops[i]["part"], 0) for i in range(n)]
+    rank = [rank[i] + OPT["urge"] * (ops[i]["part"][1] == 0) + OPT["late"] * ops[i]["part"][0] for i in range(n)]
     left = [len(p) for p in pre]
     ready = {i: 0.0 for i in range(n) if not left[i]}
     free, seq, end = {}, [], 0.0

@@ -12,8 +12,9 @@ NONE0, NONE1, THR = -4092.0 * 4096, -4088.0 * 4096, -4085.0 * 4096
 BIG = 1280.0 * 8192
 Z = 64
 COFF = {2: 0, 1: 432, 0: 720}
-OPT = dict(gath=("SSSS", "SSSS"), turn="EE", war=True, eng=8, zb=("pB", "pA"), cb=("pA", "pB"), urge=0.0, late=0.0)
-COST = dict(c=0.95, g=1.8, sc=3.8, pe=0.475, lat=190, look=0.0, rem=2500.0, lean=0)
+OPT = dict(mode=[[['SVST', 'TVST', 'SSST'], ['SVST', 'SUST', 'TTTU']], [['SVST', 'SVST', 'SVST'], ['STSU', 'VSST', 'STST']]],
+           gmode="S", turn="EE", split=False, run=100, war=True, eng=8, banks=("AAMXAABX", "XMABXMAA"), seed=1, tries=1500)
+COST = dict(c=0.85, g=1.5, sc=3.5, pe=0.42, lat=150, look=300.0, rem=3000.0, lean=500, vf=10, pf=10, beta=15.0)
 
 f32, b16, f16, i32, u16 = "float32", "bfloat16", "float16", "int32", "uint16"
 TILE = {}
@@ -25,32 +26,32 @@ def _decl(where, dtype, halves=False, **kw):
             TILE[k + x] = (where, [128, n], dtype)
 
 
-ZERO = dict(YV=512, Y0=128, Y1=128, YC0=128, YC1=128, MN=16, AB=32)
-ZERO2 = dict(YG0=256, YG1=256, YGC0=256, YGC1=256, SG00=64, SG01=64, SG10=64, SG11=64, SG20=64, SG21=64, SG30=64, SG31=64, RST8=512)
-_decl("sbuf", f32, **ZERO)
-_decl("sbuf", f32, **ZERO2)
+_decl("sbuf", f32, YV=512, MN=16, AB=32)
+_decl("sbuf", f32, SG00=48, SG01=48, SG10=48, SG11=48, SG20=48, SG21=48, SG30=48, SG31=48)
+_decl("sbuf", b16, RST8=512, RST=432)
 _decl("psum", f32, pX0=512, pX1=512, pB=512, pV0=512, pV1=512, pM0=512, pM1=512, pA=512)
 _decl("sbuf", b16, True, RG=2048, CM=2048, RGG=384, CMG=384, U=128, W=128, NW=48)
-_decl("sbuf", b16, R0=Z + 5248, R1=Z + 5248, R2=Z + 5248, XX0=320, XX1=320, XX2=320, XX3=320, ZL=256, ONE=512, REP=2048, BJ=2048, ID=128, ID2K=128,
-      BO=128, BO1=16, BO4K=32, BOS=32, BK0=32, BK1=32, BK2=32, BK3=32, SK0=32, SK1=32, SK2=32, IW=288, UW=288, CC=864, CT=144, CG=32, L1=128, L2=128,
-      TRI=128, NTRI=128, TP=128, TN=128, TQ=128, DG=160, SL0=160, SL8=160, SL2=160, SL10=160, MASK=640, R16B=256, CSEL=512, SEA=128, SEB=128, BSB=32,
+_decl("sbuf", b16, R0=Z + 5248, R1=Z + 5248, R2=Z + 5248, XX0=512, XX1=512, XX2=512, XX3=512,
+      NID=128, MONE=128, ID3=384, ONE=512, REP=2048, BJ=2048, ID=128, ID2K=128,
+      BO=128, BO1=16, BO4K=32, BOS=32, BK0=32, BK1=32, BK2=32, BK3=32, SK0=32, SK1=32, SK2=32, IW=288, UW=288, CC=864, CT=240, CG=32, L1=128, L2=128,
+      TRI=128, NBO=128, T63=128, TN=128, TQ=128, DG=160, SL0=160, SL8=160, SL2=160, SL10=160, MASK=640, R16B=256, CSEL=512, SEA=128, SEB=128, BSB=32,
       FR=64, NGS=128, STR=64, NBE=64, PL=64, ACB=16, RC=64, RH=64, XC=64, XH=64)
 _decl("sbuf", f16, True, E0=128, E1=128)
 _decl("sbuf", f16, OWN=256, G0X=128, TT=64, ELO=64)
-_decl("sbuf", f32, True, SC=576, KE=128, HI=32, NM=32, NZ=32, GN=32)
-_decl("sbuf", f32, D1=Z + 1152, D2=Z + 1152, D3=Z + 1152, D4=Z + 1152, ID32=128, NID32=128, R16=128, NR16=128, BSEL=16, RST=432, HM=16, DV=16,
+_decl("sbuf", f32, True, SC=432, KE=128, HI=32, NM=32, NZ=32, GN=32)
+_decl("sbuf", f32, D1=Z + 1152, D2=Z + 1152, D3=Z + 1152, D4=Z + 1152, ID32=128, NID32=128, R16=128, BSEL=16, HM=16, DV=16,
       YVC=512, VS32=64, VL=64, VV0=48, VV1=48, VV2=48, VV3=48, SV1=48, SV2=48, SV3=48,
-      GM10=64, GM11=64, GM20=64, GM21=64, GM30=64, GM31=64, YO=256, COL=16, COLI=32,
-      EA=64, EB=64, Q1=16, Q2=16, ADD0=32, ADD2=32, XT=32, OF=32, AS=16, EBN=64, PUT=64, EP=64, P0=64, M1=64, NE=64, EHI=64, NV=128,
+      GM10=48, GM11=48, GM20=48, GM21=48, GM30=48, GM31=48, YO=256, COL=16, COLI=32,
+      EA=64, EB=64, Q1=16, Q2=16, ADD0=32, ADD2=32, XT=32, OF=32, GON=64, KP=64, P0=64, NE=64, EHI=64, NV=128,
       ZA=1024, ZS=1024, KEEP=16)
 _decl("sbuf", i32, ND=1024, VS=64, PI=16, IT=128, IT2=128)
 _decl("sbuf", u16, True, EU=128, VO=16)
 _decl("sbuf", u16, VS16=64, AO=16, SO=4, GO=4, EX=16, EXK=16, RA=2, OU=32, GU10=32, GU11=32, GU20=32, GU21=32, GU30=32, GU31=32,
-      SU00=32, SU01=32, SU10=32, SU11=32, SU20=32, SU21=32)
+      SU00=32, SU01=32, SU10=32, SU11=32, SU20=32, SU21=32, SU30=32, SU31=32)
 
 MSGS = ["xx%d" % t for t in (1, 2, 3)] + ["vv%d" % t for t in (1, 2, 3)] + ["g%s%d%d" % (x, t, h) for x in "mu" for t in (1, 2, 3) for h in (0, 1)] + \
        ["ka%d" % t for t in (1, 2, 3)]
-SEMAPHORES = ["eV", "eS", "eP", "eG", "sent", "ldz", "ldx", "ldv", "ldn0", "ldn1", "ldr0", "ldr1", "out", "cd2", "cd3", "cd4", "cr1", "cr2"] + MSGS
+SEMAPHORES = ["eV", "eS", "eP", "eG", "sent", "ldz", "ldv", "ldn0", "ldn1", "ldr0", "ldr1", "out", "cd2", "cd3", "cd4", "cr10", "cr11", "cr20", "cr21"] + MSGS
 WIDE = {f32: 4, i32: 4, b16: 2, u16: 2, f16: 2}
 PLACE, SCRATCH = {}, {}
 for _k, (_w, _s, _d) in TILE.items():
@@ -87,7 +88,8 @@ def program():
     C, O = COST, OPT
 
     def add(eng, calls, cost, w, r, **kw):
-        ops.append(dict(eng=eng, calls=calls, cost=cost, w=w, r=r, part=part[0], **kw))
+        ops.append(dict(eng=eng, calls=calls, cost=cost, w=w, r=r, part=part[0],
+                        ind=any(_isv(x) and x[0] == "ind" for _, a, _ in calls for x in a), **kw))
 
     def comp(eng, meth, args, kw=None):
         w, r = [], []
@@ -110,7 +112,7 @@ def program():
             f = 0.5 if all(WIDE[TILE[x[1]][2]] == 2 for x in vs if _n(x) > 1) else 1.0
             if meth == "tensor_tensor":
                 f = 2.0 if all(TILE[x[1]][0] == "sbuf" for x in vs[1:]) else 1.0
-            cost = 20 + max(64, n * f) * C["c"]
+            cost = C["vf"] + max(64, n * f) * C["c"]
         add(eng, [(meth, args, kw or {})], cost, w, r)
 
     def ts(out, in0, s1, op0, s2=None, op1=None):
@@ -162,12 +164,15 @@ def program():
         comp("G", "affine_select", [out, a, pat, op, other, base, cm])
 
     def mm(lst):
+        if len(lst) > O["run"]:
+            mm(lst[:O["run"]])
+            return mm(lst[O["run"]:])
         w, r, cost = [], [], 0.0
         for o, l, x, _, _ in lst:
             w.append(o)
             r += [l, x]
             cost += max(min(64, _n(l)), _n(x)) * (4 if TILE[x[1]][2] == f32 else 1) * C["pe"]
-        add("P", [("matmul", list(m), {}) for m in lst], cost + 30, w, r)
+        add("P", [("matmul", list(m), {}) for m in lst], cost + C["pf"], w, r)
 
     def acc(out, l, x, start=False, stop=False):
         return (out, l, x, start, stop)
@@ -179,29 +184,12 @@ def program():
         add("G", [("remote", [dst, src, hop, sem], {})], 800.0, [], [src], sem="sent", lat=C["rem"] + more)
         add("R", [], 0.0, [dst], [], sem=sem, lat=C["rem"], after=len(ops) - 1)
 
-    def zero(tiles, groups):
-        at, names = 0, list(tiles)
-        for n in groups:
-            some, names = names[:n], names[n:]
-            ms(A(some[0], 0, sum(tiles[x] for x in some)), 0.0)
-            ops[-1]["w"] = [A(x) for x in some]
-
-    def turn(y, yc, nq, k, ps, c0=0, keys=False):
-        out, src = A(ps, c0, c0 + 64 * nq), A(y, 0, 64 * nq)
-        if keys:
-            mm([acc(out, A("R16"), src, True), acc(out, A("L1"), A("CT", 0, 64)), acc(out, A("L2"), A("CT", 0, 64)), acc(out, A("NR16"), src, False, True)])
-        else:
-            mm([acc(out, A("R16"), src, True, True)])
-        cp(A(yc, 0, 64 * nq), out)
-        return IND(A(yc, 0, 128 * k), A("GO", 0, k))
-
     dma("Y", A("VS"), ("hbm", "vs", None), "ldv", 1800)
     dma("S", A("R0", Z, Z + 1152), ("hbm", "rg", (0, 1152)), "ldr0", 3000)
     dma("Y", A("ND", 0, 512), ("hbm", "nd", (0, 512)), "ldn0", 3400)
     dma("S", A("ND", 512, 1024), ("hbm", "nd", (512, 1024)), "ldn1", 3800)
-    dma("Y", A("ZL"), ("hbm", "z", None), "ldz", 3000)
+    dma("Y", A("XX0", 256, 512), ("hbm", "z", None), "ldz", 3000)
     dma("Y", A("R0", Z + 1152, Z + 2048), ("hbm", "rg", (1152, 2048)), "ldr1", 4300)
-    dma("Y", A("XX0", 256, 320), ("hbm", "z", (0, 64)), "ldx", 4300)
     ms(A("ONE"), 1.0, False)
     sel(A("ID"), A("ONE", 0, 128), [[-1, 128]], ALU.is_equal, 0, 1)
     iota(A("PI", 0, 1), [[0, 1]], 0, 1)
@@ -215,10 +203,13 @@ def program():
         cp(A("REP", i, 2048, 16), A("ID"))
     ts(A("IT2"), A("IT"), 15, ALU.bitwise_and)
     ts(A("R16"), A("IT2"), 0.0, ALU.is_equal)
-    aff(A("NR16"), A("R16"), -1.0)
     cp(A("ID32"), A("ID"))
     aff(A("NID32"), A("ID"), -1.0)
     aff(A("ID2K"), A("ID"), 2048.0)
+    aff(A("NID"), A("ID"), -1.0)
+    ms(A("COL", 8, 9), 32.0)
+    ms(A("COL", 9, 10), THR * 8192)
+    ms(A("COL", 10, 11), -32.0)
     aff(A("UW", 0, 144), A("IW", 0, 144), -B)
     aff(A("UW", 144, 288), A("IW", 0, 144), B)
     bo = A("BO", 0, 128, 16)
@@ -235,12 +226,14 @@ def program():
         ms(A(n), 0.0)
     for n, p, v in (("L1", 0, 1.0), ("L1", 32, 1.0), ("L1", 64, 11.0), ("L2", 0, -1.0), ("L2", 96, 7.0)):
         ms(A(n, 0, 128, 1, p, p + 1), v)
-    for c0, c1, v in ((0, 64, R2K), (64, 80, 1024.0), (80, 144, 32.0 * 16384)):
+    for c0, c1, v in ((0, 64, R2K), (64, 80, 1024.0), (80, 144, 65.0 * 8192), (144, 168, RB), (176, 240, -63.0 * 32768),
+                      (168, 169, 0.5), (169, 170, RND2), (170, 171, -RND2)):
         ms(A("CT", c0, c1, 1, 0, 1), v)
+    ms(A("CT", 170, 171, 1, 32, 33), 12.0)
     ms(A("CG", 0, 16, 1, 0, 1), 2048.0)
     ms(A("CC", 0, 432), 0.0)
     ms(A("CC", 432, 864), 0.0)
-    for p, c0, c1, st, v in ((0, 0, 432, 1, RB), (0, 432, 864, 1, RB), (0, 1, 864, W, 0.0), (0, 432, 864, W, 0.0),
+    for p, c0, c1, st, v in ((0, 0, 432, 1, RB), (0, 432, 864, 1, RB), (0, 1, 864, W, 0.0), (0, 0, 864, W, 0.0),
                              (32, 0, 144, 1, -B), (32, 144, 432, 1, -2 * B), (32, 432, 864, 1, -B), (32, 576, 720, 1, -2 * B), (32, 0, 432, W, -B),
                              (32, 432, 864, W, 0.0), (32, 1, 432, W, 0.0), (32, 577, 720, W, 0.0),
                              (64, 1, 288, W, NONE0 / 11), (96, 577, 720, W, NONE1 / 7)):
@@ -256,18 +249,19 @@ def program():
     cp(A("EX"), A("COLI", 0, 16))
     ts(A("EXK"), A("COLI", 0, 16), float(W), ALU.mult, W - 1.0, ALU.add)
     ts(A("RA"), A("COLI", 0, 2), 0.0, ALU.mult, A("COL", 4, 5), ALU.add)
-    zero(ZERO, (1, 6))
-    for h in "01":
-        ms(A("SC" + h, 432, 576), 0.0)
+    ms(A("YV"), 0.0)
+    fill(A("MN"), 0)
     ms(A("R0", Z + 3200, Z + 4096), 256.0)
     cp(A("R0", Z + 2048, Z + 3200), A("R0", Z, Z + 1152), "V")
     cp(A("R0", Z + 4096, Z + 5248), A("R0", Z, Z + 1152), "V")
     ms(A("R0", Z, Z + 2049, 2048), 256.0)
-    mm([acc(A("pM0", 128 * h, 128 * h + 128), A("ZL", 128 * h, 128 * h + 128), A("ID"), True, True) for h in (0, 1)])
+    mm([acc(A("pM0", 128 * h, 128 * h + 128), A("XX0", 256 + 128 * h, 384 + 128 * h), A("ID"), True, True) for h in (0, 1)])
     cp(A("XX0", 0, 256), A("pM0", 0, 256))
     cp(A("VS32"), A("VS"))
     cp(IND(A("YV"), A("SO", 0, 4)), A("VS32"))
-    cp(A("VL"), turn("YV", "YVC", 8, 4, "pA"))
+    mm([acc(A("pA"), A("R16"), A("YV"), True, True)])
+    cp(A("YVC"), A("pA"))
+    cp(A("VL"), IND(A("YVC"), A("GO")))
     for t in range(NT):
         n = "VV0" if t == 0 else "SV%d" % t
         cp(A(n, 0, 16), A("VL", 16 * t, 16 * t + 16))
@@ -280,16 +274,20 @@ def program():
     cp(A("D1", Z, Z + 512), A("ND", 0, 512))
     cp(A("D1", Z + 512, Z + 1024), A("ND", 512, 1024))
     ms(A("D1", Z + 1024, Z + 1152), 0.0)
-    zero(ZERO2, (2, 2, 8, 1))
+    fill(A("RST8"), 0)
+    fill(A("MONE"), -1)
+    for n in ("R1", "R2"):
+        fill(A(n, Z + 3200, Z + 4096), 256)
+    sel(A("ID3"), A("ONE", 0, 384), [[0, 3], [-1, 128]], ALU.is_equal, 0, 1)
     ms(A("RST8", 0, 512, 8), 8192.0)
     for t in range(3):
         fill(A("SK%d" % t, 24, 32), 0)
     sel(A("TRI"), A("BO"), [[1, 128]], ALU.is_ge, 0, -1)
-    sel(A("TP"), A("TRI"), [[-1, 128]], ALU.not_equal, 0, 1, 64.0)
-    aff(A("NTRI"), A("TRI"), -1.0)
-    aff(A("TN"), A("TRI"), 16384.0)
-    sel(A("TN"), A("TN"), [[-1, 128]], ALU.not_equal, 0, 1, -31.0 * 16384)
-    sel(A("TQ"), A("NTRI"), [[-1, 128]], ALU.not_equal, 0, 1, 64.0)
+    sel(A("T63"), A("TRI"), [[-1, 128]], ALU.not_equal, 0, 1, -63.0)
+    aff(A("NBO"), A("BO"), -1.0)
+    for n, v, d in (("TN", 16384.0, -31.0), ("TQ", -32768.0, -64.0)):
+        aff(A(n), A("TRI"), v)
+        sel(A(n), A(n), [[-1, 128]], ALU.not_equal, 0, 1, d * v)
     sel(A("DG"), A("ONE", 0, 160), [[-1, 160]], ALU.is_equal, 16, 1)
     for t in (0, 8, 2, 10):
         sel(A("SL%d" % t), A("DG"), [[0, 10], [1, 16]], ALU.is_equal, -t, 0)
@@ -297,9 +295,8 @@ def program():
         sel(A("BJ", 512 * j, 512 * j + 512), A("ONE"), [[-1, 4], [-16, 8], [0, 16]], ALU.is_equal, -4 * j, 1)
     off = [0, 64, 192, 384, 640]
     for c in range(4):
-        iota(A("MASK", off[c], off[c + 1]), [[0, 64 * c + 64]], 16 * c - 32, 1)
-    sel(A("MASK"), A("MASK"), [[0, 640]], ALU.is_ge, -32, 1)
-    fill(A("MASK", 0, 640, 1, 0, 16), -int(BIG))
+        iota(A("MASK", off[c], off[c + 1], 1, 0, 32), [[0, 64 * c + 64]], 16 * c - 16, 1)
+    sel(A("MASK", 0, 640, 1, 0, 32), A("MASK", 0, 640, 1, 0, 32), [[0, 640]], ALU.is_ge, -16, 1, -BIG)
     for c in range(4):
         w = 16 * c + 16
         x = A("MASK", off[c], off[c + 1], 1, 0, 16)
@@ -308,9 +305,13 @@ def program():
         sel(x, x, [[1, w]], ALU.not_equal, -16 * c, -1, 0.0)
     for j in (0, 1):
         cp(A("R16B", 128 * j, 128 * j + 128), A("R16"))
-    fill(A("CSEL"), 8192)
-    sel(A("CSEL"), A("CSEL"), [[-16, 4], [0, 128]], ALU.is_ge, 0, 1)
-    sel(A("CSEL"), A("CSEL"), [[16, 4], [0, 128]], ALU.is_ge, 15, -1)
+    for c in range(4):
+        x = A("CSEL", 128 * c, 128 * c + 32 * c + 32)
+        fill(x, 8192)
+        if c:
+            sel(x, x, [[0, _n(x)]], ALU.is_ge, -16 * c, 1)
+        if c < 3:
+            sel(x, x, [[0, _n(x)]], ALU.is_ge, 16 * c + 15, -1)
     for n, at in (("SEA", 0), ("SEB", 8)):
         fill(A(n), 0)
         sel(A(n), A(n), [[-1, 8], [0, 16]], ALU.not_equal, -at, 1, -8192.0)
@@ -318,7 +319,7 @@ def program():
     fill(A("BSB"), 0)
     for c in (4, 12, 16, 20):
         cp(A("BSB", c, c + 4), A("BO", 0, 64, 16))
-    iota(A("NV"), [[1, 128]], 2048 + 1024 - 8192, 0)
+    iota(A("NV"), [[1, 128]], 2048 + 1024 + 16384, 0)
     aff(A("KEEP"), A("R16", 0, 16), -1.0, 1.0)
     for t in (0, 2):
         n = "ADD%d" % t
@@ -349,13 +350,22 @@ def program():
 
     def gather(t, h, s):
         H = str(h)
-        vo = A("VS16", 16 * t + 8 * h, 16 * t + 8 * h + 8) if s == 2 else A("VO" + H, 0, 8)
+        vo = A("VS16", 16 * t + 8 * h, 16 * t + 8 * h + 8) if s == 2 else A("SU%d%d" % (t, h), 8 - 8 * s, 16 - 8 * s)
         if s == 2 or (s == 0 and whole(t, h)):
             cp(A("EU" + H), IND(nodes(t), vo))
         else:
             ts(A("EU" + H), IND(nodes(t), vo), 4095.0 if s else 2048.0, ALU.min)
-        for j, e in enumerate(O["gath"][h]):
-            cp(A("RG" + H, 512 * j, 512 * j + 512), IND(recs(t), A("EU" + H, 32 * j, 32 * j + 32)), e)
+        for j, e in enumerate(O["mode"][t % 2][h][2 - s]):
+            cp(A("RG" + H, 512 * j, 512 * j + 512), IND(recs(t), A("EU" + H, 32 * j, 32 * j + 32)), "S" if e in "ST" else "V")
+
+    def compare(e, cm, rg, px, xt, rep):
+        if e in "SV":
+            mm([acc(px, xt, rep, True, True)])
+            tt(cm, rg, px, ALU.is_le)
+        else:
+            mm([acc(px, xt, rep, True)])
+            mm([acc(px, A("NID"), rg, False, True)])
+            comp("S", "activation", [cm, px, ACT.Sigmoid], {"scale": 64.0, "bias": A("COL", 8, 9)})
 
     def level(t, h, s):
         n = s + 1
@@ -380,41 +390,35 @@ def program():
         ts(A("E0" + H), A(EU), -1.0, ALU.mult, 1024.0, ALU.add)
         if s:
             ts(A("E1" + H), A(EU), -1.0, ALU.mult, 3072.0, ALU.add)
-        post = []
+        for j, e in enumerate(O["mode"][t % 2][h][2 - s]):
+            compare(e, A(CM, 512 * j, 512 * j + 512), A(RG, 512 * j, 512 * j + 512), A(xbank(h)), xt, A("REP", 512 * j, 512 * j + 512))
         if s == 2 and t:
             rg, cm, gm, px = "RGG" + H, "CMG" + H, "GM%d%d" % (t, h), xbank(h)
             cp(A(rg), IND(recs(t), A("GU%d%d" % (t, h), 0, 24)), "S")
-            mm([acc(A(px, 128 * k, 128 * k + 128), xt, A("ID"), True, True) for k in range(3)])
-            tt(A(cm), A(rg), A(px, 0, 384), ALU.is_le)
-            mm([acc(A(pV, 144 * k, 144 * k + 144, W), A(cm, 128 * k, 128 * k + 128), A(bk, 0, 8)) for k in range(3)])
-            post = [acc(A(pV, 144 * k, 144 * k + 144, W), A(rg, 128 * k, 128 * k + 128), A("BO4K", 0, 8)) for k in range(3)] + \
-                   [acc(A(pV, 0, 432, W), A("ID32"), A(gm, 0, 24)), acc(A(pV, 0, 432, W), A("ID32"), A(gm, 32, 56)), acc(A(pV, 0, 432, W), A("L1"), A("CG", 0, 24))]
-        for j in range(4):
-            px = xbank(h)
-            mm([acc(A(px), xt, A("REP", 512 * j, 512 * j + 512), True, True)])
-            tt(A(CM, 512 * j, 512 * j + 512), A(RG, 512 * j, 512 * j + 512), A(px), ALU.is_le)
-        return post
+            compare(O["gmode"], A(cm), A(rg), A(px, 0, 384), xt, A("ID3"))
+            out = A(pV, 0, 432, W)
+            mm([acc(out, A("L1"), A("CT", 144, 168))] +
+               [acc(A(pV, 144 * k, 144 * k + 144, W), A(cm, 256 - 128 * k, 384 - 128 * k), A(bk, 0, 8)) for k in range(3)] + [acc(out, A("L2"), A("CT", 144, 168))] +
+               [acc(A(pV, 144 * k, 144 * k + 144, W), A(rg, 256 - 128 * k, 384 - 128 * k), A("BO4K", 0, 8)) for k in range(3)] +
+               [acc(out, A("ID32"), A(gm, 0, 24)), acc(out, A("NID32"), A(gm, 24, 48)), acc(out, A("L1"), A("CG", 0, 24))])
 
-    def choose(t, h, s, post):
+    def choose(t, h, s):
         n = s + 1
         H = str(h)
         RG, CM, pV, SC, NW = [x + H for x in ("RG", "CM", "pV", "SC", "NW")]
         mm([acc(A(pV, 2 + i, 144 * n, W), A(CM, i, 2048, 16), A("BK%d" % t, 0, 8 * n)) for i in range(16)] +
            [acc(A(pV, 0, 144 * n), A("L2"), A("CC", COFF[s], COFF[s] + 144 * n)), acc(A(pV, 0, 144), A("E0" + H), A("IW", 0, 144))] +
-           [acc(A(pV, 144, 144 * n), A("E1" + H), A("IW", 0, 144 * s))] * (s > 0) + post +
+           [acc(A(pV, 144, 144 * n), A("E1" + H), A("IW", 0, 144 * s))] * (s > 0) +
            [acc(A(pV, 2 + i, 144 * n, W), A(RG, i, 2048, 16), A("BO4K", 0, 8 * n), False, i == 15) for i in range(16)])
-        comp("V", "tensor_tensor_scan", [A(SC, 0, 144 * n), A("RST", 0, 144 * n), A(pV, 0, 144 * n), -4 * B, ALU.add, ALU.max])
+        for c0, c1 in ((144 * s, 144 * n), (0, 144 * s)) if s and O["split"] else ((0, 144 * n),):
+            comp("V", "tensor_tensor_scan", [A(SC, c0, c1), A("RST", c0, c1), A(pV, c0, c1), -4 * B, ALU.add, ALU.max])
         k = 1 - t % 2
-        if s:
-            if O["turn"][h] == "E":
-                out = A(pV, 448, 456)
-                tt(A("KE" + H), IND(A(SC, 144 * s, 144 * n), A("EXK", 0, 8)), A("R16"), ALU.mult)
-                mm([acc(out, A("KE" + H), A("BSEL", 0, 8), True), acc(out, A("L1"), A("CT", 0, 8)), acc(out, A("L2"), A("CT", 0, 8)),
-                    acc(out, A("KE" + H), A("BSEL", 8, 16), False, True)])
-                ts(A("VO" + H, 0, 8), out, 1024.0, ALU.add)
-            else:
-                cp(IND(A("Y" + H), A("SO", 0, 1)), A(SC, 144 * s + W - 1, 144 * s + 288, W))
-                ts(A("VO" + H), turn("Y" + H, "YC" + H, 1, 1, pV, 448, True), 1024.0, ALU.add)
+        if s or t < 3:
+            out = A(pV, 448, 456)
+            tt(A("KE" + H), IND(A(SC, 144 * s, 144 * n), A("EXK", 0, 8)), A("R16"), ALU.mult)
+            mm([acc(out, A("KE" + H), A("BSEL", 0, 8), True), acc(out, A("L1"), A("CT", 0, 8)), acc(out, A("L2"), A("CT", 0, 8)),
+                acc(out, A("KE" + H), A("BSEL", 8, 16), False, True)])
+            ts(A("SU%d%d" % (t, h), 16 - 8 * s, 24 - 8 * s), out, 1024.0, ALU.add)
         m = (8, 16 if whole(t, h) else 8, 16)[s]
         if s or (h == 0 and k == 0):
             tt(A(NW, 32 - 16 * s, 32 - 16 * s + m), A(SC, W - 1, W * m, W), A(SC, 1, W * m, W), ALU.is_gt)
@@ -439,12 +443,10 @@ def program():
         ts(A("HI" + H, 0, 24), keys, R2K, ALU.add, R2K, ALU.subtract)
         tt(A(low, 0, 24), keys, A("HI" + H, 0, 24), ALU.subtract)
         if t < 3:
-            ts(A(low, 32, 56), keys, THR, ALU.is_lt, -B, ALU.mult)
+            ts(A(low, 24, 48), keys, THR, ALU.is_lt, B, ALU.mult)
+            either(ACT.Relu, keys, {"scale": -8192.0, "bias": A("COL", 9, 10)})
             send(A(low), A("GM%d%d" % (t + 1, h)), 1, "gm%d%d" % (t + 1, h))
-            cp(IND(A("YG" + H), A("SO", 0, 2)), A(low, 0, 32))
-            su = A("SU%d%d" % (t, h))
-            ts(su, turn("YG" + H, "YGC" + H, 3, 2, pV), -1.0, ALU.mult, 1024.0, ALU.add)
-            send(su, A("GU%d%d" % (t + 1, h)), 1, "gu%d%d" % (t + 1, h))
+            send(A("SU%d%d" % (t, h), 0, 24), A("GU%d%d" % (t + 1, h), 0, 24), 1, "gu%d%d" % (t + 1, h))
         else:
             aff(A("NM" + H, 0, 24), A(low, 0, 24), -1.0, 1024.0)
             ts(A("NZ" + H, 0, 24), keys, THR, ALU.is_ge)
@@ -458,31 +460,39 @@ def program():
         even = t % 2 == 0
         X, m, low = A("XX%d" % t, 256, 320), 32 if even else 16, (1, 0, 64)
         old, new = A("D%d" % max(t, 1), Z, Z + 1152), A("D%d" % (t + 1))
+        pxt, ptt, pc0, pc1, pct, pg, pz0, pz1 = [{"A": "pA", "B": "pB", "X": "pX0", "M": "pM0"}[x] for x in O["banks"][t % 2]]
 
         def room(e):
             ts(A("FR"), A(e), 0.0, ALU.is_equal)
             either(ACT.Relu, A(e), {"scale": -1.0, "bias": 1.0})
             mm([acc(A("pA", 16, 24, *low), A("FR"), A("BO1", 0, 8), True, True)])
+            first = A(pg, 128, 192)
+            mm([acc(first, A("L1"), A("CT", 176, 240), True), acc(first, A("TQ"), A("FR"), False, True)])
+            if even:
+                aff(A("PL"), first, 0.5, -16384.0)
+                tt(A("P0"), first, A("NV", 32 * t, 32 * t + 64), ALU.min)
+            else:
+                ts(A("P0"), first, 0.0, ALU.is_gt)
 
-        cp(A("EB"), IND(old, A("VO0", 0, 4)))
+        cp(A("EB"), IND(old, A("SU%d0" % t, 8, 12)))
         if not even:
             room("EB")
             cp(A("Q2", 8, 16, *low), A("pA", 16, 24, *low))
         tt(A("OWN"), IND(A("AB", 0, 16), A("EX")), A("R16B"), ALU.mult)
-        mm([acc(A("pA", 32, 64), A("OWN", 128, 256, *low), A("BSB", 0, 32, *low), True), acc(A("pA", 32, 36), A("OWN", 0, 128, *low), A("BSB", 4, 8, *low), False, True)])
-        cp(A("AO", 0, 4), A("pA", 32, 36))
-        tt(A("XT", 0, m), A("pA", 32, 32 + m), A("ADD%d" % (t & 2), 0, m), ALU.add)
+        mm([acc(A(pxt, 32, 64), A("OWN", 128, 256, *low), A("BSB", 0, 32, *low), True), acc(A(pxt, 32, 36), A("OWN", 0, 128, *low), A("BSB", 4, 8, *low), False, True)])
+        cp(A("AO", 0, 4), A(pxt, 32, 36))
+        tt(A("XT", 0, m), A(pxt, 32, 32 + m), A("ADD%d" % (t & 2), 0, m), ALU.add)
         cp(A("EA"), IND(old, A("AO", 0, 4)))
         if even:
             room("EA")
         tt(A("Q1", 0, 8), A("AB", 0, 8), A("AB", 8, 16), ALU.not_equal)
         tt(A("Q2", 0, 8, *low), A("pA", 16, 24, *low) if even else A("Q2", 8, 16, *low), A("AB", 0, 8, *low), ALU.min)
         tt(A("AB", 16, 24, *low), A("Q2", 0, 8, *low), A("Q1", 0, 8, *low), ALU.min)
-        mm([acc(A("pA", 64, 128, 1, 0, 24), A("AB", 0, 24, *low), A("ID32", 0, 64, *low), True, True)])
-        cp(A("TT", 0, 64, 1, 0, 24), A("pA", 64, 128, 1, 0, 24))
-        for cs, ps in zip(((0, 1, 2), (3,)), O["cb"]):
+        mm([acc(A(ptt, 64, 128, 1, 0, 24), A("AB", 0, 24, *low), A("ID32", 0, 64, *low), True, True)])
+        cp(A("TT", 0, 64, 1, 0, 24), A(ptt, 64, 128, 1, 0, 24))
+        for cs, ps in zip(((0, 1, 2), (3,)), (pc0, pc1)):
             o0 = off[cs[0]]
-            lst = [acc(A(ps, 0, off[cs[-1] + 1] - o0), A("R16B", 0, 128, 1, 0, 48), A("MASK", o0, off[cs[-1] + 1], 1, 0, 48), True)]
+            lst = [acc(A(ps, 0, off[cs[-1] + 1] - o0), A("R16B", 0, 128, 1, 0, 32), A("MASK", o0, off[cs[-1] + 1], 1, 0, 32), True)]
             for c in cs:
                 w, at = 16 * c + 16, off[c] - o0
                 lst += [acc(A(ps, at + 2 * w * j, at + 2 * w * j + 2 * w), A("OWN", 128 * j, 128 * j + 128, *low), A("CSEL", 128 * c, 128 * c + 2 * w, *low)) for j in (0, 1)]
@@ -497,22 +507,22 @@ def program():
         cp(A("OU", 0, m), A("OF", 0, m))
         if t < 3:
             ts(A("ACB", 0, 4), A("MN", 0, 4), 4096.0, ALU.is_gt)
-            mm([acc(A("pA", 0, 1), A("ONE", 0, 128), A("ACB", c, c + 1), c == 0, c == 3) for c in range(4)])
-            ts(A("AS", 0, 1), A("pA", 0, 1), 0.5, ALU.add, RND2, ALU.add)
-            ts(A("AS", 1, 2), A("AS", 0, 1), RND2 - 12.0, ALU.subtract, A("pA", 0, 1), ALU.subtract)
-            aff(A("SK%d" % t, 0, 24), A("BOS", 0, 24), A("AS", 1, 2))
+            out = A(pct, 0, 1)
+            mm([acc(out, A("L1"), A("CT", 168, 169), True)] + [acc(out, A("ONE", 0, 128), A("ACB", c, c + 1)) for c in range(4)] +
+               [acc(out, A("L1"), A("CT", 169, 170)), acc(out, A("L1"), A("CT", 170, 171))] +
+               [acc(out, A("MONE"), A("ACB", c, c + 1), False, c == 3) for c in range(4)])
+            ts(A("SK%d" % t, 0, 24), A("BOS", 0, 24), out, ALU.mult)
             send(A("SK%d" % t), A("BK%d" % (t + 1)), 1, "ka%d" % (t + 1))
         if not even:
             ts(A("G0X"), IND(A("SG%d0" % t, 0, 16), A("EX", 0, 8)), -1.0, ALU.mult, 1024.0, ALU.add)
-            mm([acc(A("pB", 0, 64), A("G0X", 0, 128, *low), A("ID", 0, 64, *low), True, True), acc(A("pB", 64, 128), A("TP"), A("FR"), True, True)])
-            tt(A("NE"), A("EA"), A("pB", 0, 64), ALU.not_equal)
-            ts(A("P0"), A("pB", 64, 128), 64.0, ALU.is_equal)
-            tt(A("P0"), A("P0"), A("pB", 0, 64), ALU.mult)
+            mm([acc(A(pg, 0, 64), A("G0X", 0, 128, *low), A("ID", 0, 64, *low), True, True)])
+            tt(A("NE"), A("EA"), A(pg, 0, 64), ALU.not_equal)
+            tt(A("P0"), A("P0"), A(pg, 0, 64), ALU.mult)
             tt(IND(new, A("OU", 0, 4)), A("EA"), A("NE"), ALU.mult)
             tt(IND(new, A("OU", 4, 8)), A("EB"), A("P0"), ALU.add)
             return
         for o, x, r in (("RC", "XC", 8 + t), ("RH", "XH", t)):
-            aff(A(o), IND(recs(t), A("VO0", 0, 4)), A("KEEP", r, r + 1))
+            aff(A(o), IND(recs(t), A("SU%d0" % t, 8, 12)), A("KEEP", r, r + 1))
             aff(A(x), X, A("R16", r, r + 1))
         for j in range(5):
             o, x = ("RC", "XC") if j < 3 else ("RH", "XH")
@@ -522,20 +532,16 @@ def program():
             mm([acc(out, A("BJ", 128 * (r ^ 8), 128 * (r ^ 8) + 128), X, True)] +
                [acc(out, A("SL%d" % r, r + 16 - i, r + 144 - i), A("RG0", i, 1024, 16), False, i == 15) for i in range(16)])
         ts(A("NGS"), A("pB", 0, 128), 0.0, ALU.is_lt)
+        either(ACT.Sigmoid, A("pB", 0, 128), {"scale": -64.0, "bias": A("COL", 10, 11)})
         tt(A("STR"), A("NGS", 0, 64), A("NGS", 64, 128), ALU.mult)
-        tt(A("EBN"), A("EB"), A("NGS", 0, 64), ALU.mult)
+        aff(A("GON"), A("NGS", 0, 64), -1.0, 1.0)
         ts(A("EHI"), A("EB"), R1K, ALU.add, R1K, ALU.subtract)
-        tt(A("ELO"), A("EB"), A("EHI"), ALU.subtract)
-        mm([acc(A("pB", 0, 64), A("L1"), A("CT", 80, 144), True), acc(A("pB", 0, 64), A("TN"), A("STR"), False, True),
-            acc(A("pB", 64, 128), A("TP"), A("FR"), True, True),
-            acc(A("pB", 128, 192), A("BO"), A("FR"), True), acc(A("pB", 128, 192), A("NTRI"), A("STR"), False, True),
-            acc(A("pB", 192, 256), A("TQ"), A("FR"), True), acc(A("pB", 192, 256), A("BO"), A("STR"), False, True)])
-        tt(A("NBE"), A("pB", 0, 64), A("EHI"), ALU.add)
-        aff(A("PL"), A("pB", 64, 128), -16384.0, 64.0 * 16384)
-        ts(A("P0"), A("pB", 64, 128), 64.0, ALU.is_equal)
-        ts(A("PUT"), A("pB", 128, 192), 0.0, ALU.is_gt)
-        ts(A("M1"), A("pB", 192, 256), 64.0, ALU.is_lt, -8192.0, ALU.mult)
-        for b, ps in enumerate(O["zb"]):
+        tt(A("ELO"), A("EHI"), A("EB"), ALU.subtract)
+        mm([acc(A("pB", 0, 64), A("L1"), A("CT", 80, 144), True), acc(A("pB", 0, 64), A("TN"), A("STR"), False, True)])
+        tt(A("NBE"), A("pB", 0, 64), A("EHI"), ALU.subtract)
+        mm([acc(A("pB", 64, 128), A("NBO"), A("FR"), True), acc(A("pB", 64, 128), A("T63"), A("STR")), acc(A("pB", 64, 128), A("ID2K"), A("NGS", 0, 64), False, True)])
+        ts(A("KP"), A("pB", 64, 128), 1984.0, ALU.is_ge)
+        for b, ps in enumerate((pz0, pz1)):
             for q in (0, 4):
                 lst = []
                 for j in range(q, q + 4):
@@ -544,24 +550,21 @@ def program():
                 mm(lst)
             comp("S", "activation", [A("ZA", 512 * b, 512 * b + 512), A(ps), ACT.Abs])
             comp("V", "tensor_tensor_scan", [A("ZS", 512 * b, 512 * b + 512), A("RST8"), A("ZA", 512 * b, 512 * b + 512), 0.0, ALU.max, ALU.min])
-        aff(A("NE"), A("EA"), 1.0, -8192.0)
-        tt(A("P0"), A("P0"), A("NV", 32 * t, 32 * t + 64), ALU.mult)
-        tt(A("M1"), A("M1"), A("NE"), ALU.add)
-        tt(A("P0"), A("P0"), A("M1"), ALU.add)
-        tt(A("PUT"), A("PUT"), A("STR"), ALU.mult)
-        tt(A("EP"), A("EB"), A("PUT"), ALU.mult)
-        tt(IND(new, A("OU", 4, 8)), A("EBN"), A("EP"), ALU.subtract)
-        tt(IND(new, A("OU", 8, 12)), A("EB"), A("EBN"), ALU.subtract)
-        tt(A("P0"), A("P0"), A("ZS", 7, 512, 8), ALU.add)
-        tt(IND(new, A("OU", 0, 4)), A("P0"), A("ZS", 519, 1024, 8), ALU.add)
+        aff(A("NE"), A("EA"), 1.0, 16384.0)
+        tt(A("P0"), A("P0"), A("NE"), ALU.max)
+        tt(IND(new, A("OU", 4, 8)), A("EB"), A("KP"), ALU.mult)
+        tt(IND(new, A("OU", 8, 12)), A("EB"), A("GON"), ALU.mult)
+        tt(A("P0"), A("P0"), A("ZS", 7, 512, 8), ALU.subtract)
+        tt(IND(new, A("OU", 0, 4)), A("P0"), A("ZS", 519, 1024, 8), ALU.subtract)
 
     def copies(t):
-        last = len(ops) - 1
-        if t:
-            dma("Y", nodes(t + 1), nodes(t), "cd%d" % (t + 1), 3000)
-            ops[-1]["also"] = last
+        last = max(i for i, o in enumerate(ops) if o["calls"] and o["calls"][0][0] == "tensor_tensor_scan")
         if t % 2 == 0:
-            dma("Y", recs(t + 1), recs(t), "cr%d" % (t // 2 + 1), 6000)
+            for j, (c0, c1) in enumerate(((Z, Z + 3200), (Z + 4096, Z + 5248))):
+                dma("Y", A("R%d" % (t // 2 + 1), c0, c1), A("R%d" % (t // 2), c0, c1), "cr%d%d" % (t // 2 + 1, j), 6000)
+                ops[-1]["also"] = last
+        if t:
+            dma("Y", nodes(t + 1), nodes(t), "cd%d" % (t + 1), 4000)
             ops[-1]["also"] = last
         if t == 3:
             dma("Y", ("hbm", "yr", (0, 2)), A("R2", Z + 4096, Z + 4098), "out", 3000)
@@ -576,12 +579,12 @@ def program():
             for s in (2, 1, 0):
                 part[0] = (t, h, "walk")
                 gather(t, h, s)
-                post = level(t, h, s)
+                level(t, h, s)
                 if s == 0 and h == 0 and even:
                     part[0] = (t, h, "act")
                     decide(t)
                     part[0] = (t, h, "walk")
-                choose(t, h, s, post)
+                choose(t, h, s)
                 if (h, s) == (0, 2):
                     copies(t)
             part[0] = (t, h, "hand")
@@ -609,12 +612,13 @@ def order(ops):
             ps = TILE[x[1]][0] == "psum"
             lo, hi = (0, 512) if ps else (x[2], x[3])
             lst = seen.setdefault(x[1], [])
-            for a, b, j, w2 in lst:
-                if j != i and a < hi and lo < b and (wr or w2 or ps):
+            for a, b, j, w2, y in lst:
+                apart = not ps and ((x[4] == y[4] and (a - lo) % x[4]) or x[6] <= y[5] or y[6] <= x[5])
+                if j != i and a < hi and lo < b and (wr or w2 or ps) and not apart:
                     d[j] = d.get(j, False) or (w2 and not wr)
             if (wr and x[4] == 1 and x[6] - x[5] == 128) or ps:
                 lst[:] = [e for e in lst if not (lo <= e[0] and e[1] <= hi)]
-            lst.append((lo, hi, i, wr))
+            lst.append((lo, hi, i, wr, x))
         deps.append(d)
     n = len(ops)
     pre = [list(deps[i]) + ([ops[i]["after"]] if "after" in ops[i] else []) for i in range(n)]
@@ -622,35 +626,70 @@ def order(ops):
     for i in range(n):
         for j in pre[i]:
             suc[j].append(i)
-    dur = [o["cost"] + (o["lat"] if "lat" in o and o["eng"] != "R" else 0.0) for o in ops]
+    late = [o["lat"] if "lat" in o and o["eng"] != "R" else 0.0 for o in ops]
+    alt = [o.get("alt") for o in ops]
+
+    def lay(rank):
+        left, eng, cost = [len(p) for p in pre], [o["eng"] for o in ops], [o["cost"] for o in ops]
+        ready = {i: 0.0 for i in range(n) if not left[i]}
+        free, seq, t0, t1 = dict.fromkeys("VSPGYR", 0.0), [], [0.0] * n, [0.0] * n
+        while ready:
+            st, first = {}, None
+            for i, r in ready.items():
+                if alt[i]:
+                    eng[i] = "V" if max(r, free["V"]) + alt[i]["V"][1] + C["lean"] * (ops[i]["part"][2] == "act") <= max(r, free["S"]) + alt[i]["S"][1] else "S"
+                    cost[i] = alt[i][eng[i]][1]
+                st[i] = max(r, free[eng[i]])
+                if first is None or (st[i], -rank[i]) < (st[first], -rank[first]):
+                    first = i
+            till = st[first] + min(C["look"], cost[first])
+            i = max((j for j in st if eng[j] == eng[first] and st[j] <= till), key=lambda j: rank[j] - C["beta"] * st[j])
+            del ready[i]
+            if eng[i] != "R":
+                free[eng[i]] = st[i] + cost[i]
+            t0[i], t1[i] = st[i], st[i] + cost[i] + late[i]
+            seq.append(i)
+            for j in suc[i]:
+                left[j] -= 1
+                if not left[j]:
+                    ready[j] = max(t1[k] + (0.0 if eng[k] == eng[j] == "P" else C["lat"]) for k in pre[j])
+        return max(t1), seq, eng, t0, t1
+
+    def replay(seq, eng, lat, gather):
+        free, t1 = dict.fromkeys("VSPGYR", 0.0), [0.0] * n
+        for i in seq:
+            e = eng[i]
+            st = max([free[e]] + [t1[k] + (0.0 if eng[k] == e == "P" else lat) for k in pre[i]])
+            c = (alt[i][e][1] if alt[i] else ops[i]["cost"]) * (gather if ops[i]["ind"] else 1.0)
+            if e != "R":
+                free[e] = st + c
+            t1[i] = st + c + late[i]
+        return max(t1)
+
+    def worth(rank):
+        end, seq, eng, t0, t1 = lay(rank)
+        return (end + replay(seq, eng, C["lat"] - 50, 0.8) + replay(seq, eng, C["lat"] + 50, 1.2)) / 3
+
     rank = [0.0] * n
     for i in range(n - 1, -1, -1):
-        rank[i] = dur[i] + max([rank[j] + C["lat"] for j in suc[i]], default=0.0)
-    rank = [rank[i] + OPT["urge"] * (ops[i]["part"][1] == 0) + OPT["late"] * ops[i]["part"][0] for i in range(n)]
-    left = [len(p) for p in pre]
-    ready = {i: 0.0 for i in range(n) if not left[i]}
-    free, seq, end = {}, [], 0.0
-    while ready:
-        for i, r in ready.items():
-            if "alt" in ops[i]:
-                e = min("VS", key=lambda e: max(r, free.get(e, 0.0)) + ops[i]["alt"][e][1] + (C["lean"] if e == "V" else 0.0))
-                ops[i].update(eng=e, calls=ops[i]["alt"][e][0], cost=ops[i]["alt"][e][1])
-                dur[i] = ops[i]["cost"]
-        st = {i: max(r, free.get(ops[i]["eng"], 0.0)) for i, r in ready.items()}
-        i0 = min(st, key=lambda i: (st[i], -rank[i]))
-        i = max((j for j in st if ops[j]["eng"] == ops[i0]["eng"] and st[j] <= st[i0] + C["look"]), key=lambda j: rank[j])
-        del ready[i]
-        ops[i]["t0"] = st[i]
-        if ops[i]["eng"] != "R":
-            free[ops[i]["eng"]] = st[i] + ops[i]["cost"]
-        fin = st[i] + dur[i]
-        ops[i]["t1"] = fin
-        end = max(end, fin)
-        seq.append(i)
-        for j in suc[i]:
-            left[j] -= 1
-            if not left[j]:
-                ready[j] = max(ops[k]["t1"] + (0.0 if inorder(ops, deps, j, k) else C["lat"]) for k in pre[j])
+        rank[i] = ops[i]["cost"] + late[i] + max([rank[j] + C["lat"] for j in suc[i]], default=0.0)
+    best, seed = worth(rank), [OPT["seed"]]
+
+    def draw(m):
+        seed[0] = (seed[0] * 1103515245 + 12345) % 2 ** 31
+        return (seed[0] >> 8) % m
+
+    for _ in range(OPT["tries"]):
+        a, w, d = draw(n), (1, 3, 10, 30, 80)[draw(5)], (draw(201) - 100) * (5, 15, 50, 120)[draw(4)]
+        other = rank[:a] + [x + d for x in rank[a:a + w]] + rank[a + w:]
+        v = worth(other)
+        if v <= best + draw(40):
+            rank, best = other, v
+    end, seq, eng, t0, t1 = lay(rank)
+    for i, o in enumerate(ops):
+        o.update(t0=t0[i], t1=t1[i])
+        if alt[i]:
+            o.update(eng=eng[i], calls=alt[i][eng[i]][0], cost=alt[i][eng[i]][1])
     return seq, deps, end
 
 

@@ -12,9 +12,11 @@ NONE0, NONE1, THR = -4092.0 * 4096, -4088.0 * 4096, -4085.0 * 4096
 BIG = 1280.0 * 8192
 Z = 64
 COFF = {2: 0, 1: 432, 0: 720}
-OPT = dict(mode=[[['SVST', 'TVST', 'SSST'], ['SVST', 'SUST', 'TTTU']], [['SVST', 'SVST', 'SVST'], ['STSU', 'VSST', 'STST']]],
-           gmode="S", turn="EE", split=False, run=100, war=True, eng=8, banks=("AAMXAABX", "XMABXMAA"), seed=1, tries=1500)
-COST = dict(c=0.85, g=1.5, sc=3.5, pe=0.42, lat=150, look=300.0, rem=3000.0, lean=500, vf=10, pf=10, beta=15.0)
+OPT = dict(mode=[[['STsF', 'STSF', 'SSSF'], ['STTF', 'STTV', 'STTF']], [['STSF', 'STSF', 'STSF'], ['SsTF', 'STTF', 'TTTF']]], f0="SS",
+           gmode="S", turn="HH", split=False, run=100, war=True, eng=8, banks=("AAMXAABX", "AXABXBAA"), seed=1, turns=6,
+           lag=[[4, 0, 3], [-1, -1, -1], [3, -1, 3], [0, 2, 5]], tries=19000)
+COST = dict(c=0.85, g=1.5, sc=3.5, pe=0.42, lat=150, look=300.0, rem=3000.0, lean=500, heat=8e-4, vf=10, pf=10, beta=15.0)
+CASES = ((0, 1.0), (-50, 0.8), (50, 1.2))
 
 f32, b16, f16, i32, u16 = "float32", "bfloat16", "float16", "int32", "uint16"
 TILE = {}
@@ -26,21 +28,21 @@ def _decl(where, dtype, halves=False, **kw):
             TILE[k + x] = (where, [128, n], dtype)
 
 
-_decl("sbuf", f32, YV=512, MN=16, AB=32)
+_decl("sbuf", f32, YV=512, MN=16, AB=32, NN=16)
 _decl("sbuf", f32, SG00=48, SG01=48, SG10=48, SG11=48, SG20=48, SG21=48, SG30=48, SG31=48)
 _decl("sbuf", b16, RST8=512, RST=432)
 _decl("psum", f32, pX0=512, pX1=512, pB=512, pV0=512, pV1=512, pM0=512, pM1=512, pA=512)
 _decl("sbuf", b16, True, RG=2048, CM=2048, RGG=384, CMG=384, U=128, W=128, NW=48)
 _decl("sbuf", b16, R0=Z + 5248, R1=Z + 5248, R2=Z + 5248, XX0=512, XX1=512, XX2=512, XX3=512,
-      NID=128, MONE=128, ID3=384, ONE=512, REP=2048, BJ=2048, ID=128, ID2K=128,
+      XR00=2048, XR01=2048, XR10=2048, XR11=2048, NID=128, MONE=128, ID3=256, ONE=512, REP=2048, BJ=2048, ID=128, ID2K=128,
       BO=128, BO1=16, BO4K=32, BOS=32, BK0=32, BK1=32, BK2=32, BK3=32, SK0=32, SK1=32, SK2=32, IW=288, UW=288, CC=864, CT=240, CG=32, L1=128, L2=128,
       TRI=128, NBO=128, T63=128, TN=128, TQ=128, DG=160, SL0=160, SL8=160, SL2=160, SL10=160, MASK=640, R16B=256, CSEL=512, SEA=128, SEB=128, BSB=32,
-      FR=64, NGS=128, STR=64, NBE=64, PL=64, ACB=16, RC=64, RH=64, XC=64, XH=64)
-_decl("sbuf", f16, True, E0=128, E1=128)
+      NBIG=256, ASR=640, AX0=128, AX1=128, FS=128, FR=64, NGS=128, STR=64, NBE=64, PL=64, ACB=16, RC=64, RH=64, XC=64, XH=64)
+_decl("sbuf", f16, True, E0=128, E1=128, RD=2048)
 _decl("sbuf", f16, OWN=256, G0X=128, TT=64, ELO=64)
 _decl("sbuf", f32, True, SC=432, KE=128, HI=32, NM=32, NZ=32, GN=32)
 _decl("sbuf", f32, D1=Z + 1152, D2=Z + 1152, D3=Z + 1152, D4=Z + 1152, ID32=128, NID32=128, R16=128, BSEL=16, HM=16, DV=16,
-      YVC=512, VS32=64, VL=64, VV0=48, VV1=48, VV2=48, VV3=48, SV1=48, SV2=48, SV3=48,
+      YVC=512, VV0=128, VV1=128, VV2=128, VV3=128,
       GM10=48, GM11=48, GM20=48, GM21=48, GM30=48, GM31=48, YO=256, COL=16, COLI=32,
       EA=64, EB=64, Q1=16, Q2=16, ADD0=32, ADD2=32, XT=32, OF=32, GON=64, KP=64, P0=64, NE=64, EHI=64, NV=128,
       ZA=1024, ZS=1024, KEEP=16)
@@ -49,9 +51,9 @@ _decl("sbuf", u16, True, EU=128, VO=16)
 _decl("sbuf", u16, VS16=64, AO=16, SO=4, GO=4, EX=16, EXK=16, RA=2, OU=32, GU10=32, GU11=32, GU20=32, GU21=32, GU30=32, GU31=32,
       SU00=32, SU01=32, SU10=32, SU11=32, SU20=32, SU21=32, SU30=32, SU31=32)
 
-MSGS = ["xx%d" % t for t in (1, 2, 3)] + ["vv%d" % t for t in (1, 2, 3)] + ["g%s%d%d" % (x, t, h) for x in "mu" for t in (1, 2, 3) for h in (0, 1)] + \
+MSGS = ["xx%d" % t for t in (1, 2, 3)] + ["vv%d" % t for t in (1, 2, 3)] + ["g%s%d%d" % (x, t, h) for x in "muw" for t in (1, 2, 3) for h in (0, 1)] + \
        ["ka%d" % t for t in (1, 2, 3)]
-SEMAPHORES = ["eV", "eS", "eP", "eG", "sent", "ldz", "ldv", "ldn0", "ldn1", "ldr0", "ldr1", "out", "cd2", "cd3", "cd4", "cr10", "cr11", "cr20", "cr21"] + MSGS
+SEMAPHORES = ["eV", "eS", "eP", "eG", "sent", "ldz", "ldv", "ldn0", "ldn1", "ldr0", "ldr1", "out", "cd2", "cd3", "cd4", "cr1", "cr2"] + MSGS
 WIDE = {f32: 4, i32: 4, b16: 2, u16: 2, f16: 2}
 PLACE, SCRATCH = {}, {}
 for _k, (_w, _s, _d) in TILE.items():
@@ -84,7 +86,7 @@ def _real(x):
 
 
 def program():
-    ops, part = [], [(0, 0, "")]
+    ops, part = [], [(0, 0, "", 0)]
     C, O = COST, OPT
 
     def add(eng, calls, cost, w, r, **kw):
@@ -222,21 +224,21 @@ def program():
     aff(A("BK0", 0, 24), A("BO4K", 0, 24), 12 * 15.0 * B / 4096 / 4096)
     ms(A("RST"), 0.0)
     ms(A("RST", 0, 432, W), -4 * B)
-    for n in ("L1", "L2", "CT", "CG"):
-        ms(A(n), 0.0)
+    ms(A("CC", 0, 432), 0.0)
+    ms(A("CC", 432, 864), 0.0)
+    ms(A("CT", 0, 528), 0.0)
+    ops[-1]["w"] = [A(n) for n in ("CT", "CG", "L1", "L2")]
     for n, p, v in (("L1", 0, 1.0), ("L1", 32, 1.0), ("L1", 64, 11.0), ("L2", 0, -1.0), ("L2", 96, 7.0)):
         ms(A(n, 0, 128, 1, p, p + 1), v)
-    for c0, c1, v in ((0, 64, R2K), (64, 80, 1024.0), (80, 144, 65.0 * 8192), (144, 168, RB), (176, 240, -63.0 * 32768),
+    for c0, c1, v in ((0, 8, R2K), (80, 144, 65.0 * 8192), (144, 168, RB), (176, 240, -63.0 * 32768),
                       (168, 169, 0.5), (169, 170, RND2), (170, 171, -RND2)):
         ms(A("CT", c0, c1, 1, 0, 1), v)
     ms(A("CT", 170, 171, 1, 32, 33), 12.0)
     ms(A("CG", 0, 16, 1, 0, 1), 2048.0)
-    ms(A("CC", 0, 432), 0.0)
-    ms(A("CC", 432, 864), 0.0)
-    for p, c0, c1, st, v in ((0, 0, 432, 1, RB), (0, 432, 864, 1, RB), (0, 1, 864, W, 0.0), (0, 0, 864, W, 0.0),
-                             (32, 0, 144, 1, -B), (32, 144, 432, 1, -2 * B), (32, 432, 864, 1, -B), (32, 576, 720, 1, -2 * B), (32, 0, 432, W, -B),
-                             (32, 432, 864, W, 0.0), (32, 1, 432, W, 0.0), (32, 577, 720, W, 0.0),
-                             (64, 1, 288, W, NONE0 / 11), (96, 577, 720, W, NONE1 / 7)):
+    for p, c0, c1, st, v in ((0, 0, 432, 1, RB), (0, 1, 432, W, 0.0), (0, 0, 432, W, 0.0), (0, 432, 864, 1, RB), (0, 433, 864, W, 0.0), (0, 432, 864, W, 0.0),
+                             (32, 0, 144, 1, -B), (32, 432, 864, 1, -B), (32, 144, 432, 1, -2 * B), (32, 576, 720, 1, -2 * B), (32, 144, 432, W, -B),
+                             (32, 432, 864, W, 0.0), (32, 1, 432, W, 1024.0), (32, 577, 720, W, 0.0),
+                             (64, 1, 432, W, NONE0 / 11), (96, 577, 720, W, NONE1 / 7)):
         ms(A("CC", c0, c1, st, p, p + 1), v)
     for i, (v, o) in enumerate(((4, ALU.arith_shift_right), (15, ALU.bitwise_and), (8, ALU.bitwise_and), (7, ALU.bitwise_and), (3, ALU.bitwise_and))):
         ts(A("PI", 1 + i, 2 + i), A("PI", 0, 1), v, o)
@@ -253,35 +255,25 @@ def program():
     fill(A("MN"), 0)
     ms(A("R0", Z + 3200, Z + 4096), 256.0)
     cp(A("R0", Z + 2048, Z + 3200), A("R0", Z, Z + 1152), "V")
-    cp(A("R0", Z + 4096, Z + 5248), A("R0", Z, Z + 1152), "V")
+    cp(A("R0", Z + 4096, Z + 5248), A("R0", Z, Z + 1152))
     ms(A("R0", Z, Z + 2049, 2048), 256.0)
     mm([acc(A("pM0", 128 * h, 128 * h + 128), A("XX0", 256 + 128 * h, 384 + 128 * h), A("ID"), True, True) for h in (0, 1)])
     cp(A("XX0", 0, 256), A("pM0", 0, 256))
-    cp(A("VS32"), A("VS"))
-    cp(IND(A("YV"), A("SO", 0, 4)), A("VS32"))
+    cp(A("VV0", 64, 128), A("VS"))
+    cp(IND(A("YV"), A("SO", 0, 4)), A("VV0", 64, 128))
     mm([acc(A("pA"), A("R16"), A("YV"), True, True)])
     cp(A("YVC"), A("pA"))
-    cp(A("VL"), IND(A("YVC"), A("GO")))
-    for t in range(NT):
-        n = "VV0" if t == 0 else "SV%d" % t
-        cp(A(n, 0, 16), A("VL", 16 * t, 16 * t + 16))
-        aff(A(n, 16, 32), A("VL", 16 * t, 16 * t + 16), -1.0, NONE0 + 1024)
-        if t:
-            cp(A(n, 32, 48), A("VS32", 16 * t, 16 * t + 16))
+    cp(A("VV0", 0, 64), IND(A("YVC"), A("GO")))
     for t in (1, 2, 3):
         send(A("XX0"), A("XX%d" % t), t, "xx%d" % t, 12000.0)
-        send(A("SV%d" % t), A("VV%d" % t), t, "vv%d" % t, 8000.0)
+        send(A("VV0"), A("VV%d" % t), t, "vv%d" % t, 8000.0)
     cp(A("D1", Z, Z + 512), A("ND", 0, 512))
     cp(A("D1", Z + 512, Z + 1024), A("ND", 512, 1024))
     ms(A("D1", Z + 1024, Z + 1152), 0.0)
-    fill(A("RST8"), 0)
+    ms(A("RST8"), 0.0)
     fill(A("MONE"), -1)
-    for n in ("R1", "R2"):
-        fill(A(n, Z + 3200, Z + 4096), 256)
-    sel(A("ID3"), A("ONE", 0, 384), [[0, 3], [-1, 128]], ALU.is_equal, 0, 1)
+    sel(A("ID3"), A("ONE", 0, 256), [[0, 2], [-1, 128]], ALU.is_equal, 0, 1)
     ms(A("RST8", 0, 512, 8), 8192.0)
-    for t in range(3):
-        fill(A("SK%d" % t, 24, 32), 0)
     sel(A("TRI"), A("BO"), [[1, 128]], ALU.is_ge, 0, -1)
     sel(A("T63"), A("TRI"), [[-1, 128]], ALU.not_equal, 0, 1, -63.0)
     aff(A("NBO"), A("BO"), -1.0)
@@ -294,24 +286,19 @@ def program():
     for j in range(4):
         sel(A("BJ", 512 * j, 512 * j + 512), A("ONE"), [[-1, 4], [-16, 8], [0, 16]], ALU.is_equal, -4 * j, 1)
     off = [0, 64, 192, 384, 640]
-    for c in range(4):
-        iota(A("MASK", off[c], off[c + 1], 1, 0, 32), [[0, 64 * c + 64]], 16 * c - 16, 1)
-    sel(A("MASK", 0, 640, 1, 0, 32), A("MASK", 0, 640, 1, 0, 32), [[0, 640]], ALU.is_ge, -16, 1, -BIG)
+    fill(A("NBIG", 0, 256, 1, 0, 16), -int(BIG))
+    ts(A("COL", 11, 12), A("PI", 0, 1), -16.0, ALU.add)
     for c in range(4):
         w = 16 * c + 16
-        x = A("MASK", off[c], off[c + 1], 1, 0, 16)
-        sel(x, x, [[0, 4], [-1, w]], ALU.is_ge, 16 * c - 1, 1, BIG)
+        ts(A("MASK", off[c], off[c + 1], 1, 0, 32), A("ONE", 0, 4 * w, 1, 0, 32), A("COL", 11, 12, 1, 0, 32), ALU.mult, 16.0 * c, ALU.add)
+        ts(A("CSEL", 128 * c, 128 * c + 2 * w), A("ONE", 0, 2 * w), A("BSEL", c, c + 1), ALU.mult, 8192.0, ALU.mult)
+        sel(A("MASK", off[c], off[c + 1], 1, 0, 16), A("NBIG", 0, 4 * w, 1, 0, 16), [[0, 4], [-1, w]], ALU.is_ge, 16 * c - 1, 1, BIG)
         x = A("MASK", off[c], off[c] + w, 1, 0, 16)
         sel(x, x, [[1, w]], ALU.not_equal, -16 * c, -1, 0.0)
+        sel(A("ASR", off[c], off[c + 1]), A("ONE", 0, 4 * w), [[0, 4], [-1, w]], ALU.is_equal, 0, 1)
+    fill(A("AB", 24, 32), 0)
     for j in (0, 1):
         cp(A("R16B", 128 * j, 128 * j + 128), A("R16"))
-    for c in range(4):
-        x = A("CSEL", 128 * c, 128 * c + 32 * c + 32)
-        fill(x, 8192)
-        if c:
-            sel(x, x, [[0, _n(x)]], ALU.is_ge, -16 * c, 1)
-        if c < 3:
-            sel(x, x, [[0, _n(x)]], ALU.is_ge, 16 * c + 15, -1)
     for n, at in (("SEA", 0), ("SEB", 8)):
         fill(A(n), 0)
         sel(A(n), A(n), [[-1, 8], [0, 16]], ALU.not_equal, -at, 1, -8192.0)
@@ -344,10 +331,6 @@ def program():
     def whole(t, h):
         return h == 0 and t % 2 == 0
 
-    def names(out, keys):
-        mm([acc(out, A("ID32"), keys, True), acc(out, A("L1"), A("CT", 0, 8)), acc(out, A("L2"), A("CT", 0, 8)), acc(out, A("NID32"), keys),
-            acc(out, A("L1"), A("CT", 64, 72), False, True)])
-
     def gather(t, h, s):
         H = str(h)
         vo = A("VS16", 16 * t + 8 * h, 16 * t + 8 * h + 8) if s == 2 else A("SU%d%d" % (t, h), 8 - 8 * s, 16 - 8 * s)
@@ -355,11 +338,36 @@ def program():
             cp(A("EU" + H), IND(nodes(t), vo))
         else:
             ts(A("EU" + H), IND(nodes(t), vo), 4095.0 if s else 2048.0, ALU.min)
-        for j, e in enumerate(O["mode"][t % 2][h][2 - s]):
-            cp(A("RG" + H, 512 * j, 512 * j + 512), IND(recs(t), A("EU" + H, 32 * j, 32 * j + 32)), "S" if e in "ST" else "V")
+        mode = how(t, h, s)
+        heads = [j for j, e in enumerate(mode) if j == 0 or e.isupper() or mode[j - 1] == "F"] + [4]
+        for j, j2 in zip(heads, heads[1:]):
+            rec = IND(recs(t), A("EU" + H, 32 * j, 32 * j2))
+            if mode[j] == "F":
+                tt(A("RD" + H, 512 * j, 512 * j2), rec, A("XR%d%d" % (t % 2, h), 512 * j, 512 * j2), ALU.subtract)
+            else:
+                cp(A("RG" + H, 512 * j, 512 * j2), rec, "S" if mode[j] in "STst" else "V")
+
+    def how(t, h, s):
+        mode = O["mode"][t % 2][h][2 - s]
+        return mode if t else mode.replace("F", O["f0"][h])
+
+    def spread(t, h):
+        f = [j for j in range(4) if any(how(t, h, s)[j] == "F" for s in range(3))]
+        for i in range(16 if f else 0):
+            x = A("XX%d" % t, 256 + 128 * h + 32 * f[0], 288 + 128 * h + 32 * f[-1])
+            sel(A("XR%d%d" % (t % 2, h), 512 * f[0] + i, 512 * f[-1] + 512, 16), x, [[0, _n(x)]], ALU.is_ge, 0, 0)
+
+    def runs(t, h, s):
+        f, out = [e == "F" for e in how(t, h, s)], []
+        for j in range(4):
+            if j and f[j] == f[j - 1] and (out[-1][0] == 0 or (out[-1][0] == 2 and j == 3)):
+                out[-1][1] = j + 1
+            else:
+                out.append([j, j + 1, "RD" if f[j] else "RG"])
+        return out
 
     def compare(e, cm, rg, px, xt, rep):
-        if e in "SV":
+        if e in "SVsv":
             mm([acc(px, xt, rep, True, True)])
             tt(cm, rg, px, ALU.is_le)
         else:
@@ -376,10 +384,9 @@ def program():
         if s < 2:
             lst += [acc(A(pV, 0, 144 * n, W), A("ID32"), A(SC, W - 1, 144 * n, W)), acc(A(pV, 0, 144 * n, W), A("ID2K"), A(NW, 16 - 16 * s, 16 - 16 * s + 8 * n))]
         if s == 1:
-            out, keys = A(pV, 145, 288, W), A(SC, 288 + W - 1, 432, W)
-            lst += [acc(out, A("NID32"), keys), acc(out, A("L1"), A("CT", 0, 8)), acc(out, A("L2"), A("CT", 0, 8)), acc(out, A("ID32"), keys)]
+            lst += [acc(A(pV, 145, 288, W), A("ID32"), A("SG%d%d" % (t, h), 16, 24))]
         if s == 2:
-            lst += [acc(A(pV, 289, 432, W), A("ID32"), A("VV%d" % t, 16 + 8 * h, 24 + 8 * h))]
+            lst += [acc(A(pV, 289, 432, W), A("NID32"), A("VV%d" % t, 16 * t + 8 * h, 16 * t + 8 * h + 8))]
         mm(lst)
         if s or whole(t, h):
             ts(A("U" + H), A(EU), 2048.0, ALU.is_ge)
@@ -390,17 +397,23 @@ def program():
         ts(A("E0" + H), A(EU), -1.0, ALU.mult, 1024.0, ALU.add)
         if s:
             ts(A("E1" + H), A(EU), -1.0, ALU.mult, 3072.0, ALU.add)
-        for j, e in enumerate(O["mode"][t % 2][h][2 - s]):
-            compare(e, A(CM, 512 * j, 512 * j + 512), A(RG, 512 * j, 512 * j + 512), A(xbank(h)), xt, A("REP", 512 * j, 512 * j + 512))
+        for j, e in enumerate(how(t, h, s)):
+            if e == "F":
+                ts(A(CM, 512 * j, 512 * j + 512), A("RD" + H, 512 * j, 512 * j + 512), 0.0, ALU.is_le)
+            else:
+                compare(e, A(CM, 512 * j, 512 * j + 512), A(RG, 512 * j, 512 * j + 512), A(xbank(h)), xt, A("REP", 512 * j, 512 * j + 512))
         if s == 2 and t:
             rg, cm, gm, px = "RGG" + H, "CMG" + H, "GM%d%d" % (t, h), xbank(h)
-            cp(A(rg), IND(recs(t), A("GU%d%d" % (t, h), 0, 24)), "S")
-            compare(O["gmode"], A(cm), A(rg), A(px, 0, 384), xt, A("ID3"))
+            mm([acc(A(px, 0, 256), xt, A("ID3", 0, 256), True, True)])
+            for ks, c0, c1 in (((2, 1), 0, 256), ((0,), 256, 384)):
+                cp(A(rg, c0, c1), IND(recs(t), A("GU%d%d" % (t, h), c0 // 16, c1 // 16)), "S" if c0 == 0 else "E")
+                tt(A(cm, c0, c1), A(rg, c0, c1), A(px, 0, c1 - c0), ALU.is_le)
+                out, n8 = A(pV, 144 * ks[-1], 144 * ks[0] + 144, W), 8 * len(ks)
+                mm([acc(out, A("L1"), A("CT", 144, 144 + n8))] +
+                   [acc(A(pV, 144 * k, 144 * k + 144, W), A(cm, 256 - 128 * k, 384 - 128 * k), A(bk, 0, 8)) for k in ks] + [acc(out, A("L2"), A("CT", 144, 144 + n8))] +
+                   [acc(A(pV, 144 * k, 144 * k + 144, W), A(rg, 256 - 128 * k, 384 - 128 * k), A("BO4K", 0, 8)) for k in ks])
             out = A(pV, 0, 432, W)
-            mm([acc(out, A("L1"), A("CT", 144, 168))] +
-               [acc(A(pV, 144 * k, 144 * k + 144, W), A(cm, 256 - 128 * k, 384 - 128 * k), A(bk, 0, 8)) for k in range(3)] + [acc(out, A("L2"), A("CT", 144, 168))] +
-               [acc(A(pV, 144 * k, 144 * k + 144, W), A(rg, 256 - 128 * k, 384 - 128 * k), A("BO4K", 0, 8)) for k in range(3)] +
-               [acc(out, A("ID32"), A(gm, 0, 24)), acc(out, A("NID32"), A(gm, 24, 48)), acc(out, A("L1"), A("CG", 0, 24))])
+            mm([acc(out, A("ID32"), A(gm, 0, 24)), acc(out, A("NID32"), A(gm, 24, 48)), acc(out, A("L1"), A("CG", 0, 24))])
 
     def choose(t, h, s):
         n = s + 1
@@ -409,44 +422,58 @@ def program():
         mm([acc(A(pV, 2 + i, 144 * n, W), A(CM, i, 2048, 16), A("BK%d" % t, 0, 8 * n)) for i in range(16)] +
            [acc(A(pV, 0, 144 * n), A("L2"), A("CC", COFF[s], COFF[s] + 144 * n)), acc(A(pV, 0, 144), A("E0" + H), A("IW", 0, 144))] +
            [acc(A(pV, 144, 144 * n), A("E1" + H), A("IW", 0, 144 * s))] * (s > 0) +
-           [acc(A(pV, 2 + i, 144 * n, W), A(RG, i, 2048, 16), A("BO4K", 0, 8 * n), False, i == 15) for i in range(16)])
+           [acc(A(pV, 2 + i, 144 * n, W, 32 * a, 32 * b), A(x + H, 512 * a + i, 512 * b, 16), A("BO4K", 0, 8 * n), False, i == 15)
+            for i in range(16) for a, b, x in runs(t, h, s)])
         for c0, c1 in ((144 * s, 144 * n), (0, 144 * s)) if s and O["split"] else ((0, 144 * n),):
             comp("V", "tensor_tensor_scan", [A(SC, c0, c1), A("RST", c0, c1), A(pV, c0, c1), -4 * B, ALU.add, ALU.max])
         k = 1 - t % 2
+        sg, out, su = "SG%d%d" % (t, h), A(pV, 448, 456), A("SU%d%d" % (t, h), 16 - 8 * s, 24 - 8 * s)
         if s or t < 3:
-            out = A(pV, 448, 456)
             tt(A("KE" + H), IND(A(SC, 144 * s, 144 * n), A("EXK", 0, 8)), A("R16"), ALU.mult)
             mm([acc(out, A("KE" + H), A("BSEL", 0, 8), True), acc(out, A("L1"), A("CT", 0, 8)), acc(out, A("L2"), A("CT", 0, 8)),
                 acc(out, A("KE" + H), A("BSEL", 8, 16), False, True)])
-            ts(A("SU%d%d" % (t, h), 16 - 8 * s, 24 - 8 * s), out, 1024.0, ALU.add)
+            ts(su, out, 1024.0, ALU.add)
+        k0 = 0 if (h, s, k) == (0, 1, 0) else s
+        keys, hi = A(SC, 144 * k0 + W - 1, 144 * n, W), A("HI" + H, 8 * k0, 8 * n)
+        ts(hi, keys, R2K, ALU.add, R2K, ALU.subtract)
+        tt(A(sg, 8 * k0, 8 * n), keys, hi, ALU.subtract)
         m = (8, 16 if whole(t, h) else 8, 16)[s]
-        if s or (h == 0 and k == 0):
+        if s:
             tt(A(NW, 32 - 16 * s, 32 - 16 * s + m), A(SC, W - 1, W * m, W), A(SC, 1, W * m, W), ALU.is_gt)
-        if h == 0 and s >= k:
-            nw = A(NW, 32 - 16 * s + 8 * k, 40 - 16 * s + 8 * k)
-            if s == 2:
-                tt(A("HM", 0, 8), A("VV%d" % t, 0, 8), nw, ALU.mult)
-            else:
-                tt(A("DV", 8, 16), A("DV", 0, 8), nw, ALU.mult)
-                tt(A("AB" if s == k else "HM", 0, 8), A("HM", 0, 8), A("DV", 8, 16), ALU.add)
         if h == 0 and s:
-            out = A("pA", 16 - 8 * s, 24 - 8 * s)
-            names(out, A(SC, 144 * s + W - 1, 144 * n, W))
-            if s == 1:
-                cp(A("AB", 8, 16), out)
-            if s > k:
-                tt(A("DV", 0, 8), out if s == 2 else A("AB", 8, 16), A("HM", 0, 8), ALU.subtract)
+            source(t, s)
+
+    def source(t, s):
+        k, NW, sg = 1 - t % 2, "NW0", "SG%d0" % t
+        nw = A(NW, 32 - 16 * s + 8 * k, 40 - 16 * s + 8 * k)
+        if s == 2:
+            tt(A("HM", 0, 8), A("VV%d" % t, 16 * t, 16 * t + 8), nw, ALU.mult)
+            if k:
+                tt(A("HM", 0, 8), A("pA", 16, 24), A("HM", 0, 8), ALU.min)
+            aff(A("HM", 8, 16), A(sg, 16, 24), -1.0, 1024.0)
+            if not k:
+                tt(A("DV", 0, 8), A("HM", 8, 16), A("HM", 0, 8), ALU.subtract)
+        else:
+            tt(A("DV", 8, 16), A("DV", 0, 8), nw, ALU.mult)
+            tt(A("AB", 16, 24), A("HM", 0, 8), A("DV", 8, 16), ALU.add)
+            aff(A("AB", 8 * k, 16), A(sg, 8 * k, 16), -1.0, 1024.0)
+
+    def roomy(t, s):
+        ts(A("FS"), A("EU0"), 0.0, ALU.is_equal)
+        mm([acc(A("pA", 16, 24), A("FS"), A("BO4K", 0, 8), True, True)])
+        if s == 1:
+            tt(A("HM", 8, 16), A("pA", 16, 24), A("HM", 8, 16), ALU.min)
+            tt(A("DV", 0, 8), A("HM", 8, 16), A("HM", 0, 8), ALU.subtract)
 
     def handon(t, h):
         H = str(h)
         keys, low, pV = A("SC" + H, W - 1, 432, W), "SG%d%d" % (t, h), "pV" + H
-        ts(A("HI" + H, 0, 24), keys, R2K, ALU.add, R2K, ALU.subtract)
-        tt(A(low, 0, 24), keys, A("HI" + H, 0, 24), ALU.subtract)
         if t < 3:
             ts(A(low, 24, 48), keys, THR, ALU.is_lt, B, ALU.mult)
             either(ACT.Relu, keys, {"scale": -8192.0, "bias": A("COL", 9, 10)})
+            send(A("SU%d%d" % (t, h), 0, 16), A("GU%d%d" % (t + 1, h), 0, 16), 1, "gw%d%d" % (t + 1, h))
+            send(A("SU%d%d" % (t, h), 16, 24), A("GU%d%d" % (t + 1, h), 16, 24), 1, "gu%d%d" % (t + 1, h))
             send(A(low), A("GM%d%d" % (t + 1, h)), 1, "gm%d%d" % (t + 1, h))
-            send(A("SU%d%d" % (t, h), 0, 24), A("GU%d%d" % (t + 1, h), 0, 24), 1, "gu%d%d" % (t + 1, h))
         else:
             aff(A("NM" + H, 0, 24), A(low, 0, 24), -1.0, 1024.0)
             ts(A("NZ" + H, 0, 24), keys, THR, ALU.is_ge)
@@ -456,7 +483,7 @@ def program():
             for k in range(3):
                 dma("Y", ("hbm", "yg", (256 * k + 128 * h, 256 * k + 128 * h + 128)), A("YO", 128 * h, 128 * h + 128, 1, 8 * k, 8 * k + 8), "out", 2000)
 
-    def decide(t):
+    def ask(t):
         even = t % 2 == 0
         X, m, low = A("XX%d" % t, 256, 320), 32 if even else 16, (1, 0, 64)
         old, new = A("D%d" % max(t, 1), Z, Z + 1152), A("D%d" % (t + 1))
@@ -465,7 +492,9 @@ def program():
         def room(e):
             ts(A("FR"), A(e), 0.0, ALU.is_equal)
             either(ACT.Relu, A(e), {"scale": -1.0, "bias": 1.0})
-            mm([acc(A("pA", 16, 24, *low), A("FR"), A("BO1", 0, 8), True, True)])
+            if not even:
+                mm([acc(A("pA", 16, 24, *low), A("FR"), A("BO1", 0, 8), True, True)])
+                tt(A("Q2", 0, 8, *low), A("pA", 16, 24, *low), A("AB", 16, 24, *low), ALU.min)
             first = A(pg, 128, 192)
             mm([acc(first, A("L1"), A("CT", 176, 240), True), acc(first, A("TQ"), A("FR"), False, True)])
             if even:
@@ -477,19 +506,24 @@ def program():
         cp(A("EB"), IND(old, A("SU%d0" % t, 8, 12)))
         if not even:
             room("EB")
-            cp(A("Q2", 8, 16, *low), A("pA", 16, 24, *low))
-        tt(A("OWN"), IND(A("AB", 0, 16), A("EX")), A("R16B"), ALU.mult)
-        mm([acc(A(pxt, 32, 64), A("OWN", 128, 256, *low), A("BSB", 0, 32, *low), True), acc(A(pxt, 32, 36), A("OWN", 0, 128, *low), A("BSB", 4, 8, *low), False, True)])
+        tt(A("Q1", 0, 8), A("AB", 8, 16), A("AB", 16, 24), ALU.not_equal)
+        tt(A("AB", 24, 32, *low), A("AB", 16, 24, *low) if even else A("Q2", 0, 8, *low), A("Q1", 0, 8, *low), ALU.min)
+        rows = (1, 0, 24 if even else 16)
+        mm([acc(A(ptt, 64, 128, *rows), A("AB", 8, 8 + rows[2], *low), A("ID32", 0, 64, *low), True, True)])
+        cp(A("TT", 0, 64, *rows), A(ptt, 64, 128, *rows))
+        tt(A("OWN"), IND(A("AB", 8, 24), A("EX")), A("R16B"), ALU.mult)
+        mm([acc(A(pxt, 32, 64), A("OWN", 0, 128, *low), A("BSB", 0, 32, *low), True), acc(A(pxt, 32, 36), A("OWN", 128, 256, *low), A("BSB", 4, 8, *low), False, True)])
         cp(A("AO", 0, 4), A(pxt, 32, 36))
         tt(A("XT", 0, m), A(pxt, 32, 32 + m), A("ADD%d" % (t & 2), 0, m), ALU.add)
         cp(A("EA"), IND(old, A("AO", 0, 4)))
         if even:
             room("EA")
-        tt(A("Q1", 0, 8), A("AB", 0, 8), A("AB", 8, 16), ALU.not_equal)
-        tt(A("Q2", 0, 8, *low), A("pA", 16, 24, *low) if even else A("Q2", 8, 16, *low), A("AB", 0, 8, *low), ALU.min)
-        tt(A("AB", 16, 24, *low), A("Q2", 0, 8, *low), A("Q1", 0, 8, *low), ALU.min)
-        mm([acc(A(ptt, 64, 128, 1, 0, 24), A("AB", 0, 24, *low), A("ID32", 0, 64, *low), True, True)])
-        cp(A("TT", 0, 64, 1, 0, 24), A(ptt, 64, 128, 1, 0, 24))
+        else:
+            cp(A("G0X"), IND(A("AB", 0, 8), A("EX", 0, 8)))
+            mm([acc(A(pg, 0, 64), A("G0X", 0, 128, *low), A("ID", 0, 64, *low), True, True)])
+            tt(A("NE"), A("EA"), A(pg, 0, 64), ALU.not_equal)
+            tt(A("P0"), A("P0"), A(pg, 0, 64), ALU.mult)
+            aff(A("AX0"), IND(A("AB", 24, 32), A("EX", 0, 8)), BIG)
         for cs, ps in zip(((0, 1, 2), (3,)), (pc0, pc1)):
             o0 = off[cs[0]]
             lst = [acc(A(ps, 0, off[cs[-1] + 1] - o0), A("R16B", 0, 128, 1, 0, 32), A("MASK", o0, off[cs[-1] + 1], 1, 0, 32), True)]
@@ -499,10 +533,28 @@ def program():
             mm(lst)
             for c in cs:
                 w, at = 16 * c + 16, off[c] - o0
-                mm([acc(A(ps, at + b * w, at + b * w + w), A(o, 0, 128, 1, 0, 24), A("TT", 0, w, 1, 0, 24), False, c == cs[-1] and b == 3)
+                mm([acc(A(ps, at + b * w, at + b * w + w), A(o, 0, 128, *rows), A("TT", 0, w, *rows), False, even and c == cs[-1] and b == 3)
                     for b, o in enumerate(("SEA", "SEB", "SEB", "SEA"))])
-            for c in cs:
-                comp("V", "tensor_reduce", [A("MN", c, c + 1), A(ps, off[c] - o0, off[c + 1] - o0), AxisListType.X, ALU.min], {"apply_absolute_value": True})
+            if even:
+                least(cs, ps)
+        if even:
+            act(t)
+
+    def least(cs, ps):
+        for c in cs:
+            comp("V", "tensor_reduce", [A("MN", c, c + 1), A(ps, off[c] - off[cs[0]], off[c + 1] - off[cs[0]]), AxisListType.X, ALU.min],
+                 {"apply_absolute_value": True})
+
+    def act(t):
+        even = t % 2 == 0
+        X, m, low, new = A("XX%d" % t, 256, 320), 32 if even else 16, (1, 0, 64), A("D%d" % (t + 1))
+        pxt, ptt, pc0, pc1, pct, pg, pz0, pz1 = [{"A": "pA", "B": "pB", "X": "pX0", "M": "pM0"}[x] for x in O["banks"][t % 2]]
+        if not even:
+            tt(A("NN", 0, 8), A("SC0", W - 1, 144, W), A("SC0", 1, 144, W), ALU.is_le)
+            tt(A("AX1"), IND(A("NN", 0, 8), A("EX", 0, 8)), A("AX0"), ALU.mult)
+            for cs, ps in zip(((0, 1, 2), (3,)), (pc0, pc1)):
+                mm([acc(A(ps, 0, off[cs[-1] + 1] - off[cs[0]]), A("AX1", 0, 128, *low), A("ASR", off[cs[0]], off[cs[-1] + 1], *low), False, True)])
+                least(cs, ps)
         tt(A("OF", 0, m), IND(A("MN"), A("RA", 0, m // 16)), A("XT", 0, m), ALU.min)
         cp(A("OU", 0, m), A("OF", 0, m))
         if t < 3:
@@ -512,12 +564,8 @@ def program():
                [acc(out, A("L1"), A("CT", 169, 170)), acc(out, A("L1"), A("CT", 170, 171))] +
                [acc(out, A("MONE"), A("ACB", c, c + 1), False, c == 3) for c in range(4)])
             ts(A("SK%d" % t, 0, 24), A("BOS", 0, 24), out, ALU.mult)
-            send(A("SK%d" % t), A("BK%d" % (t + 1)), 1, "ka%d" % (t + 1))
+            send(A("SK%d" % t, 0, 24), A("BK%d" % (t + 1), 0, 24), 1, "ka%d" % (t + 1))
         if not even:
-            ts(A("G0X"), IND(A("SG%d0" % t, 0, 16), A("EX", 0, 8)), -1.0, ALU.mult, 1024.0, ALU.add)
-            mm([acc(A(pg, 0, 64), A("G0X", 0, 128, *low), A("ID", 0, 64, *low), True, True)])
-            tt(A("NE"), A("EA"), A(pg, 0, 64), ALU.not_equal)
-            tt(A("P0"), A("P0"), A(pg, 0, 64), ALU.mult)
             tt(IND(new, A("OU", 0, 4)), A("EA"), A("NE"), ALU.mult)
             tt(IND(new, A("OU", 4, 8)), A("EB"), A("P0"), ALU.add)
             return
@@ -560,9 +608,8 @@ def program():
     def copies(t):
         last = max(i for i, o in enumerate(ops) if o["calls"] and o["calls"][0][0] == "tensor_tensor_scan")
         if t % 2 == 0:
-            for j, (c0, c1) in enumerate(((Z, Z + 3200), (Z + 4096, Z + 5248))):
-                dma("Y", A("R%d" % (t // 2 + 1), c0, c1), A("R%d" % (t // 2), c0, c1), "cr%d%d" % (t // 2 + 1, j), 6000)
-                ops[-1]["also"] = last
+            dma("Y", recs(t + 1), recs(t), "cr%d" % (t // 2 + 1), 7000)
+            ops[-1]["also"] = last
         if t:
             dma("Y", nodes(t + 1), nodes(t), "cd%d" % (t + 1), 4000)
             ops[-1]["also"] = last
@@ -574,31 +621,35 @@ def program():
 
     for t in range(NT):
         even = t % 2 == 0
-        cp(A("VS16", 16 * t, 16 * t + 16), A("VV%d" % t, 32, 48) if t else A("VS", 0, 16))
+        cp(A("VS16", 16 * t, 16 * t + 16), A("VV%d" % t, 64 + 16 * t, 80 + 16 * t) if t else A("VS", 0, 16))
         for h in (0, 1):
+            part[0] = (t, h, "walk", 2)
+            spread(t, h)
             for s in (2, 1, 0):
-                part[0] = (t, h, "walk")
+                part[0] = (t, h, "walk", s)
                 gather(t, h, s)
+                if s and whole(t, h):
+                    roomy(t, s)
                 level(t, h, s)
-                if s == 0 and h == 0 and even:
-                    part[0] = (t, h, "act")
-                    decide(t)
-                    part[0] = (t, h, "walk")
+                if s == 0 and h == 0:
+                    part[0] = (t, h, "act", s)
+                    ask(t)
+                    part[0] = (t, h, "walk", s)
                 choose(t, h, s)
                 if (h, s) == (0, 2):
                     copies(t)
-            part[0] = (t, h, "hand")
-            handon(t, h)
             if h == 0 and not even:
-                part[0] = (t, h, "act")
-                decide(t)
-    dma("Y", ("hbm", "yn", (0, 576)), A("D4", Z, Z + 576), "out", 3000)
-    dma("S", ("hbm", "yn", (576, 1152)), A("D4", Z + 576, Z + 1152), "out", 3000)
+                part[0] = (t, h, "act", 0)
+                act(t)
+            part[0] = (t, h, "hand", 0)
+            handon(t, h)
+    dma("Y", ("hbm", "yn", None), nodes(4), "out", 4000)
     return ops
 
 
 def inorder(ops, deps, i, j):
-    return ops[i]["eng"] == ops[j]["eng"] and "sem" not in ops[j] and (ops[i]["eng"] == "P" or not (deps[i].get(j) or OPT["war"]))
+    return ops[i]["eng"] == ops[j]["eng"] and "sem" not in ops[j] and (ops[i]["eng"] == "P" or deps[i].get(j, True) is None or
+                                                                               (not OPT["war"] and ops[i]["eng"] in "VS" and "sem" not in ops[i] and not deps[i].get(j, True)))
 
 
 def order(ops):
@@ -615,7 +666,7 @@ def order(ops):
             for a, b, j, w2, y in lst:
                 apart = not ps and ((x[4] == y[4] and (a - lo) % x[4]) or x[6] <= y[5] or y[6] <= x[5])
                 if j != i and a < hi and lo < b and (wr or w2 or ps) and not apart:
-                    d[j] = d.get(j, False) or (w2 and not wr)
+                    d[j] = (d.get(j) or (w2 and not wr)) if wr or w2 else d.get(j)
             if (wr and x[4] == 1 and x[6] - x[5] == 128) or ps:
                 lst[:] = [e for e in lst if not (lo <= e[0] and e[1] <= hi)]
             lst.append((lo, hi, i, wr, x))
@@ -627,16 +678,19 @@ def order(ops):
         for j in pre[i]:
             suc[j].append(i)
     late = [o["lat"] if "lat" in o and o["eng"] != "R" else 0.0 for o in ops]
-    alt = [o.get("alt") for o in ops]
+    loose = set(x for i in range(n) for j, v in deps[i].items() if v is None or not (v or OPT["war"] or ops[i]["eng"] not in "VS" or "sem" in ops[i] or "sem" in ops[j]) for x in ((i, j), (j, i)))
+    alt, links, base, ind = [o.get("alt") for o in ops], (pre, suc), [o["cost"] for o in ops], [o["ind"] for o in ops]
 
-    def lay(rank):
-        left, eng, cost = [len(p) for p in pre], [o["eng"] for o in ops], [o["cost"] for o in ops]
-        ready = {i: 0.0 for i in range(n) if not left[i]}
+    def lay(rank, back=None):
+        pre, suc = (links[1], links[0]) if back else links
+        left, eng = [len(p) for p in pre], back or [o["eng"] for o in ops]
+        cost = [alt[i][eng[i]][1] if alt[i] else ops[i]["cost"] for i in range(n)]
+        ready = {i: late[i] if back else 0.0 for i in range(n) if not left[i]}
         free, seq, t0, t1 = dict.fromkeys("VSPGYR", 0.0), [], [0.0] * n, [0.0] * n
         while ready:
             st, first = {}, None
             for i, r in ready.items():
-                if alt[i]:
+                if alt[i] and not back:
                     eng[i] = "V" if max(r, free["V"]) + alt[i]["V"][1] + C["lean"] * (ops[i]["part"][2] == "act") <= max(r, free["S"]) + alt[i]["S"][1] else "S"
                     cost[i] = alt[i][eng[i]][1]
                 st[i] = max(r, free[eng[i]])
@@ -647,50 +701,91 @@ def order(ops):
             del ready[i]
             if eng[i] != "R":
                 free[eng[i]] = st[i] + cost[i]
-            t0[i], t1[i] = st[i], st[i] + cost[i] + late[i]
+            t0[i], t1[i] = st[i], st[i] + cost[i] + (0.0 if back else late[i])
             seq.append(i)
             for j in suc[i]:
                 left[j] -= 1
                 if not left[j]:
-                    ready[j] = max(t1[k] + (0.0 if eng[k] == eng[j] == "P" else C["lat"]) for k in pre[j])
+                    ready[j] = max(t1[k] + (0.0 if eng[k] == eng[j] and (eng[k] == "P" or (k, j) in loose) else C["lat"]) for k in pre[j]) + (late[j] if back else 0.0)
         return max(t1), seq, eng, t0, t1
 
     def replay(seq, eng, lat, gather):
-        free, t1 = dict.fromkeys("VSPGYR", 0.0), [0.0] * n
+        free, last, t1, why = dict.fromkeys("VSPGYR", 0.0), dict.fromkeys("VSPGYR", -1), [0.0] * n, [-1] * n
         for i in seq:
             e = eng[i]
-            st = max([free[e]] + [t1[k] + (0.0 if eng[k] == e == "P" else lat) for k in pre[i]])
-            c = (alt[i][e][1] if alt[i] else ops[i]["cost"]) * (gather if ops[i]["ind"] else 1.0)
+            st, w = free[e], last[e]
+            for k in pre[i]:
+                v = t1[k] if e == eng[k] and (e == "P" or (k, i) in loose) else t1[k] + lat
+                if v > st:
+                    st, w = v, k
+            c = alt[i][e][1] if alt[i] else base[i]
+            if ind[i]:
+                c *= gather
             if e != "R":
-                free[e] = st + c
-            t1[i] = st + c + late[i]
-        return max(t1)
+                free[e], last[e] = st + c, i
+            t1[i], why[i] = st + c + late[i], w
+        return t1, why
 
     def worth(rank):
         end, seq, eng, t0, t1 = lay(rank)
-        return (end + replay(seq, eng, C["lat"] - 50, 0.8) + replay(seq, eng, C["lat"] + 50, 1.2)) / 3
+        return sum(max(replay(seq, eng, C["lat"] + a, b)[0]) for a, b in CASES)
 
     rank = [0.0] * n
     for i in range(n - 1, -1, -1):
         rank[i] = ops[i]["cost"] + late[i] + max([rank[j] + C["lat"] for j in suc[i]], default=0.0)
-    best, seed = worth(rank), [OPT["seed"]]
+    rank = [rank[i] - 1000 * OPT["lag"][o["part"][0]][2 - o["part"][3]] * o["part"][1] for i, o in enumerate(ops)]
+    best, seed, other = worth(rank), [OPT["seed"]], rank
+    for _ in range(OPT["turns"]):
+        end, seq, eng, t0, t1 = lay(other)
+        other = lay(t1, eng)[4]
+        v = worth(other)
+        if v < best:
+            rank, best = other, v
 
     def draw(m):
         seed[0] = (seed[0] * 1103515245 + 12345) % 2 ** 31
         return (seed[0] >> 8) % m
 
-    for _ in range(OPT["tries"]):
-        a, w, d = draw(n), (1, 3, 10, 30, 80)[draw(5)], (draw(201) - 100) * (5, 15, 50, 120)[draw(4)]
-        other = rank[:a] + [x + d for x in rank[a:a + w]] + rank[a + w:]
-        v = worth(other)
-        if v <= best + draw(40):
-            rank, best = other, v
+    def ends(seq, eng):
+        runs = [replay(seq, eng, C["lat"] + a, b) for a, b in CASES]
+        return sum(max(r[0]) for r in runs), runs[draw(len(runs))]
+
     end, seq, eng, t0, t1 = lay(rank)
+    seq.sort(key=lambda i: t0[i])
+    now, (t1, why) = ends(seq, eng)
+    best = (now, seq, eng)
+    for step in range(OPT["tries"]):
+        chain = [max(range(n), key=lambda i: t1[i])]
+        while why[chain[-1]] >= 0:
+            chain.append(why[chain[-1]])
+        pairs = [(a, b) for b, a in zip(chain, chain[1:]) if eng[a] == eng[b] and a not in pre[b]]
+        both, seq2, eng2 = [i for i in chain if alt[i]], seq, eng
+        if both and draw(7) == 0:
+            i = both[draw(len(both))]
+            eng2 = eng[:i] + ["S" if eng[i] == "V" else "V"] + eng[i + 1:]
+        else:
+            a, b = pairs[draw(len(pairs))]
+            lo, hi, ahead = seq.index(a), seq.index(b), draw(2)
+            for _ in range((0, 0, 1, 2, 4)[draw(5)]):
+                more = [q for q in (range(lo - 1, max(lo - 40, -1), -1) if ahead else range(hi + 1, min(hi + 40, n))) if eng[seq[q]] == eng[a]]
+                lo, hi = (more[0] if more and ahead else lo), (more[0] if more and not ahead else hi)
+            mid, tied = seq[lo:hi + 1], {b if ahead else a}
+            for i in reversed(mid) if ahead else mid:
+                if i in tied:
+                    tied.update(pre[i] if ahead else suc[i])
+            seq2 = seq[:lo] + [i for i in mid if (i in tied) == bool(ahead)] + [i for i in mid if (i in tied) != bool(ahead)] + seq[hi + 1:]
+        v, run = ends(seq2, eng2)
+        if v <= now + draw(1000) ** 2 * C["heat"] * (1 - step / OPT["tries"]) ** 2:
+            now, seq, eng, (t1, why) = v, seq2, eng2, run
+            if now < best[0]:
+                best = (now, seq, eng)
+    _, seq, eng = best
+    t1 = replay(seq, eng, C["lat"], 1.0)[0]
     for i, o in enumerate(ops):
-        o.update(t0=t0[i], t1=t1[i])
         if alt[i]:
             o.update(eng=eng[i], calls=alt[i][eng[i]][0], cost=alt[i][eng[i]][1])
-    return seq, deps, end
+        o.update(t0=t1[i] - late[i] - o["cost"], t1=t1[i])
+    return seq, deps, max(t1)
 
 
 def waits(ops, seq, deps):

from concourse.mybir import AluOpType, AxisListType, ActivationFunctionType

ALU, ACT = AluOpType, ActivationFunctionType

NR, NT, W = 4, 4, 18
B = 2.0 ** 26
RB = 1.5 * 2.0 ** 23 * B
R2K = 1.5 * 2.0 ** 34
R1K = 1.5 * 2.0 ** 33
RND2 = 1.5 * 2.0 ** 24
NONE0, NONE1, THR = -4092.0 * 4096, -4088.0 * 4096, -4085.0 * 4096
BIG = 1280.0 * 8192
Z = 64
COFF = {2: 0, 1: 432, 0: 720}
OPT = dict(mode=[[['STsF', 'STSF', 'SSSF'], ['STTF', 'STTV', 'STTF']], [['STSF', 'STSF', 'STSF'], ['SsTF', 'STTF', 'TTTF']]], f0="SS",
           gmode="S", turn="HH", split=False, run=100, war=True, eng=8, banks=("AAMXAABX", "AXABXBAA"), seed=1, turns=6,
           lag=[[4, 0, 3], [-1, -1, -1], [3, -1, 3], [0, 2, 5]], tries=19000)
COST = dict(c=0.85, g=1.5, sc=3.5, pe=0.42, lat=150, look=300.0, rem=3000.0, lean=500, heat=8e-4, vf=10, pf=10, beta=15.0)
CASES = ((0, 1.0), (-50, 0.8), (50, 1.2))

f32, b16, f16, i32, u16 = "float32", "bfloat16", "float16", "int32", "uint16"
TILE = {}


def _decl(where, dtype, halves=False, **kw):
    for k, n in kw.items():
        for x in (("0", "1") if halves else ("",)):
            TILE[k + x] = (where, [128, n], dtype)


_decl("sbuf", f32, YV=512, MN=16, AB=32, NN=16)
_decl("sbuf", f32, SG00=48, SG01=48, SG10=48, SG11=48, SG20=48, SG21=48, SG30=48, SG31=48)
_decl("sbuf", b16, RST8=512, RST=432)
_decl("psum", f32, pX0=512, pX1=512, pB=512, pV0=512, pV1=512, pM0=512, pM1=512, pA=512)
_decl("sbuf", b16, True, RG=2048, CM=2048, RGG=384, CMG=384, U=128, W=128, NW=48)
_decl("sbuf", b16, R0=Z + 5248, R1=Z + 5248, R2=Z + 5248, XX0=512, XX1=512, XX2=512, XX3=512,
      XR00=2048, XR01=2048, XR10=2048, XR11=2048, NID=128, MONE=128, ID3=256, ONE=512, REP=2048, BJ=2048, ID=128, ID2K=128,
      BO=128, BO1=16, BO4K=32, BOS=32, BK0=32, BK1=32, BK2=32, BK3=32, SK0=32, SK1=32, SK2=32, IW=288, UW=288, CC=864, CT=240, CG=32, L1=128, L2=128,
      TRI=128, NBO=128, T63=128, TN=128, TQ=128, DG=160, SL0=160, SL8=160, SL2=160, SL10=160, MASK=640, R16B=256, CSEL=512, SEA=128, SEB=128, BSB=32,
      NBIG=256, ASR=640, AX0=128, AX1=128, FS=128, FR=64, NGS=128, STR=64, NBE=64, PL=64, ACB=16, RC=64, RH=64, XC=64, XH=64)
_decl("sbuf", f16, True, E0=128, E1=128, RD=2048)
_decl("sbuf", f16, OWN=256, G0X=128, TT=64, ELO=64)
_decl("sbuf", f32, True, SC=432, KE=128, HI=32, NM=32, NZ=32, GN=32)
_decl("sbuf", f32, D1=Z + 1152, D2=Z + 1152, D3=Z + 1152, D4=Z + 1152, ID32=128, NID32=128, R16=128, BSEL=16, HM=16, DV=16,
      YVC=512, VV0=128, VV1=128, VV2=128, VV3=128,
      GM10=48, GM11=48, GM20=48, GM21=48, GM30=48, GM31=48, YO=256, COL=16, COLI=32,
      EA=64, EB=64, Q1=16, Q2=16, ADD0=32, ADD2=32, XT=32, OF=32, GON=64, KP=64, P0=64, NE=64, EHI=64, NV=128,
      ZA=1024, ZS=1024, KEEP=16)
_decl("sbuf", i32, ND=1024, VS=64, PI=16, IT=128, IT2=128)
_decl("sbuf", u16, True, EU=128, VO=16)
_decl("sbuf", u16, VS16=64, AO=16, SO=4, GO=4, EX=16, EXK=16, RA=2, OU=32, GU10=32, GU11=32, GU20=32, GU21=32, GU30=32, GU31=32,
      SU00=32, SU01=32, SU10=32, SU11=32, SU20=32, SU21=32, SU30=32, SU31=32)

MSGS = ["xx%d" % t for t in (1, 2, 3)] + ["vv%d" % t for t in (1, 2, 3)] + ["g%s%d%d" % (x, t, h) for x in "muw" for t in (1, 2, 3) for h in (0, 1)] + \
       ["ka%d" % t for t in (1, 2, 3)]
SEMAPHORES = ["eV", "eS", "eP", "eG", "sent", "ldz", "ldv", "ldn0", "ldn1", "ldr0", "ldr1", "out", "cd2", "cd3", "cd4", "cr1", "cr2"] + MSGS
WIDE = {f32: 4, i32: 4, b16: 2, u16: 2, f16: 2}
PLACE, SCRATCH = {}, {}
for _k, (_w, _s, _d) in TILE.items():
    _b = _k if _w == "psum" else "all_" + _d
    _at = SCRATCH[_b][1][1] if _b in SCRATCH else 0
    PLACE[_k] = (_b, _at)
    SCRATCH[_b] = (_w, [128, _at + -(-_s[1] // 16) * 16], _d)


def A(name, c0=0, c1=None, step=1, p0=0, p1=128):
    if c1 is None:
        c1 = TILE[name][1][1]
    return ("ap", name, c0, c1, step, p0, p1)


def IND(win, off):
    return ("ind", win, off)


def _n(x):
    return (x[2][3] - x[2][2]) * 16 if x[0] == "ind" else len(range(x[2], x[3], x[4]))


def _isv(x):
    return isinstance(x, tuple) and x[0] in ("ap", "ind")


def _real(x):
    return TILE[x[1][1] if x[0] == "ind" else x[1]][2] in (f32, b16)


def program():
    ops, part = [], [(0, 0, "", 0)]
    C, O = COST, OPT

    def add(eng, calls, cost, w, r, **kw):
        ops.append(dict(eng=eng, calls=calls, cost=cost, w=w, r=r, part=part[0],
                        ind=any(_isv(x) and x[0] == "ind" for _, a, _ in calls for x in a), **kw))

    def comp(eng, meth, args, kw=None):
        w, r = [], []
        for i, x in enumerate(list(args) + list((kw or {}).values())):
            if _isv(x):
                (w if i == 0 else r).append(x[1] if x[0] == "ind" else x)
                if x[0] == "ind":
                    r.append(x[2])
        vs = [x for x in args if _isv(x)]
        n = max(_n(x) for x in vs)
        if eng == "G":
            cost = 170 + 2 * n * C["c"]
        elif args[0][0] == "ind":
            cost = 50 + n * C["sc"] * C["c"]
        elif any(x[0] == "ind" for x in vs):
            cost = (50 if eng == "V" else 65) + n * C["g"] * C["c"]
        elif eng == "S":
            cost = 65 + n * C["c"]
        else:
            f = 0.5 if all(WIDE[TILE[x[1]][2]] == 2 for x in vs if _n(x) > 1) else 1.0
            if meth == "tensor_tensor":
                f = 2.0 if all(TILE[x[1]][0] == "sbuf" for x in vs[1:]) else 1.0
            cost = C["vf"] + max(64, n * f) * C["c"]
        add(eng, [(meth, args, kw or {})], cost, w, r)

    def ts(out, in0, s1, op0, s2=None, op1=None):
        comp("V", "tensor_scalar", [out, in0, s1, s2, op0] + ([op1] if op1 is not None else []))

    def tt(out, a, b, op):
        comp("V", "tensor_tensor", [out, a, b, op])

    def either(func, a, kw):
        out = ops[-1]["calls"][0][1][0]
        if not (_real(out) and _real(a)) or out[0] == "ind":
            return
        first = ops.pop()
        comp("S", "activation", [out, a, func], kw)
        other = ops.pop()
        first["r"] = first["r"] + [x for x in other["r"] if x not in first["r"]]
        first["alt"] = {"V": (first["calls"], first["cost"]), "S": (other["calls"], other["cost"])}
        ops.append(first)

    def cp(out, a, eng="E"):
        if eng == "S":
            comp("S", "activation", [out, a, ACT.Copy])
            return
        comp("V", "tensor_copy", [out, a])
        if eng == "E":
            either(ACT.Copy, a, {})

    def aff(out, a, scale, bias=None):
        if bias is None:
            ts(out, a, scale, ALU.mult)
            either(ACT.Copy, a, {"scale": scale})
        else:
            ts(out, a, scale, ALU.mult, bias, ALU.add)
            either(ACT.Identity, a, {"scale": scale, "bias": bias})

    def ms(out, v, free=True):
        comp("V", "memset", [out, v])
        if free and _n(out) <= 512:
            either(ACT.Copy, A("ONE", 0, _n(out), 1, out[5], out[6]), {"scale": v})

    def iota(out, pat, base, cm):
        kw = {} if TILE[out[1]][2] == i32 else {"allow_small_or_imprecise_dtypes": True}
        comp("G", "iota", [out, pat, base, cm], kw)

    def fill(out, v):
        iota(out, [[0, _n(out)]], v, 0)

    def sel(out, a, pat, op, base, cm, other=0.0):
        comp("G", "affine_select", [out, a, pat, op, other, base, cm])

    def mm(lst):
        if len(lst) > O["run"]:
            mm(lst[:O["run"]])
            return mm(lst[O["run"]:])
        w, r, cost = [], [], 0.0
        for o, l, x, _, _ in lst:
            w.append(o)
            r += [l, x]
            cost += max(min(64, _n(l)), _n(x)) * (4 if TILE[x[1]][2] == f32 else 1) * C["pe"]
        add("P", [("matmul", list(m), {}) for m in lst], cost + C["pf"], w, r)

    def acc(out, l, x, start=False, stop=False):
        return (out, l, x, start, stop)

    def dma(q, out, in_, sem, lat):
        add(q, [("dma_start", [out, in_], {})], 60.0, [out] if out[0] == "ap" else [], [in_] if in_[0] == "ap" else [], sem=sem, lat=lat)

    def send(src, dst, hop, sem, more=0.0):
        add("G", [("remote", [dst, src, hop, sem], {})], 800.0, [], [src], sem="sent", lat=C["rem"] + more)
        add("R", [], 0.0, [dst], [], sem=sem, lat=C["rem"], after=len(ops) - 1)

    dma("Y", A("VS"), ("hbm", "vs", None), "ldv", 1800)
    dma("S", A("R0", Z, Z + 1152), ("hbm", "rg", (0, 1152)), "ldr0", 3000)
    dma("Y", A("ND", 0, 512), ("hbm", "nd", (0, 512)), "ldn0", 3400)
    dma("S", A("ND", 512, 1024), ("hbm", "nd", (512, 1024)), "ldn1", 3800)
    dma("Y", A("XX0", 256, 512), ("hbm", "z", None), "ldz", 3000)
    dma("Y", A("R0", Z + 1152, Z + 2048), ("hbm", "rg", (1152, 2048)), "ldr1", 4300)
    ms(A("ONE"), 1.0, False)
    sel(A("ID"), A("ONE", 0, 128), [[-1, 128]], ALU.is_equal, 0, 1)
    iota(A("PI", 0, 1), [[0, 1]], 0, 1)
    iota(A("IT"), [[-1, 128]], 128, 1)
    iota(A("COLI"), [[1, 32]], 0, 0)
    sel(A("BO"), A("ONE", 0, 128), [[-16, 8], [0, 16]], ALU.is_ge, 0, 1)
    sel(A("BO"), A("BO"), [[16, 8], [0, 16]], ALU.is_ge, 15, -1)
    sel(A("IW"), A("ONE", 0, 288), [[0, 2], [-16, 8], [-1, W]], ALU.is_equal, 2, 1)
    sel(A("IW"), A("IW"), [[0, 16], [1, W]], ALU.is_ge, -2, 0)
    for i in range(16):
        cp(A("REP", i, 2048, 16), A("ID"))
    ts(A("IT2"), A("IT"), 15, ALU.bitwise_and)
    ts(A("R16"), A("IT2"), 0.0, ALU.is_equal)
    cp(A("ID32"), A("ID"))
    aff(A("NID32"), A("ID"), -1.0)
    aff(A("ID2K"), A("ID"), 2048.0)
    aff(A("NID"), A("ID"), -1.0)
    ms(A("COL", 8, 9), 32.0)
    ms(A("COL", 9, 10), THR * 8192)
    ms(A("COL", 10, 11), -32.0)
    aff(A("UW", 0, 144), A("IW", 0, 144), -B)
    aff(A("UW", 144, 288), A("IW", 0, 144), B)
    bo = A("BO", 0, 128, 16)
    for k in range(3):
        aff(A("BO4K", 8 * k, 8 * k + 8), bo, 4096.0)
    cp(A("BO1", 0, 8), bo)
    cp(A("BSEL", 0, 8), bo)
    aff(A("BSEL", 8, 16), bo, -1.0)
    aff(A("BOS", 0, 24), A("BO4K", 0, 24), 15.0 * B / 4096 / 4096)
    aff(A("BK0", 0, 24), A("BO4K", 0, 24), 12 * 15.0 * B / 4096 / 4096)
    ms(A("RST"), 0.0)
    ms(A("RST", 0, 432, W), -4 * B)
    ms(A("CC", 0, 432), 0.0)
    ms(A("CC", 432, 864), 0.0)
    ms(A("CT", 0, 528), 0.0)
    ops[-1]["w"] = [A(n) for n in ("CT", "CG", "L1", "L2")]
    for n, p, v in (("L1", 0, 1.0), ("L1", 32, 1.0), ("L1", 64, 11.0), ("L2", 0, -1.0), ("L2", 96, 7.0)):
        ms(A(n, 0, 128, 1, p, p + 1), v)
    for c0, c1, v in ((0, 8, R2K), (80, 144, 65.0 * 8192), (144, 168, RB), (176, 240, -63.0 * 32768),
                      (168, 169, 0.5), (169, 170, RND2), (170, 171, -RND2)):
        ms(A("CT", c0, c1, 1, 0, 1), v)
    ms(A("CT", 170, 171, 1, 32, 33), 12.0)
    ms(A("CG", 0, 16, 1, 0, 1), 2048.0)
    for p, c0, c1, st, v in ((0, 0, 432, 1, RB), (0, 1, 432, W, 0.0), (0, 0, 432, W, 0.0), (0, 432, 864, 1, RB), (0, 433, 864, W, 0.0), (0, 432, 864, W, 0.0),
                             (32, 0, 144, 1, -B), (32, 432, 864, 1, -B), (32, 144, 432, 1, -2 * B), (32, 576, 720, 1, -2 * B), (32, 144, 432, W, -B),
                             (32, 432, 864, W, 0.0), (32, 1, 432, W, 1024.0), (32, 577, 720, W, 0.0),
                             (64, 1, 432, W, NONE0 / 11), (96, 577, 720, W, NONE1 / 7)):
        ms(A("CC", c0, c1, st, p, p + 1), v)
    for i, (v, o) in enumerate(((4, ALU.arith_shift_right), (15, ALU.bitwise_and), (8, ALU.bitwise_and), (7, ALU.bitwise_and), (3, ALU.bitwise_and))):
        ts(A("PI", 1 + i, 2 + i), A("PI", 0, 1), v, o)
    cp(A("COL", 0, 5), A("PI", 1, 6))
    ts(A("COL", 5, 6), A("COL", 1, 2), 8.0, ALU.mult, A("COL", 0, 1), ALU.add)
    ts(A("COL", 6, 7), A("COL", 0, 1), A("COL", 2, 3), ALU.add, 8.0, ALU.mult)
    ts(A("COL", 6, 7), A("COL", 6, 7), A("COL", 3, 4), ALU.add)
    ts(A("SO"), A("COLI", 0, 4), 128.0, ALU.mult, A("COL", 5, 6), ALU.add)
    ts(A("GO"), A("COLI", 0, 4), 128.0, ALU.mult, A("COL", 6, 7), ALU.add)
    cp(A("EX"), A("COLI", 0, 16))
    ts(A("EXK"), A("COLI", 0, 16), float(W), ALU.mult, W - 1.0, ALU.add)
    ts(A("RA"), A("COLI", 0, 2), 0.0, ALU.mult, A("COL", 4, 5), ALU.add)
    ms(A("YV"), 0.0)
    fill(A("MN"), 0)
    ms(A("R0", Z + 3200, Z + 4096), 256.0)
    cp(A("R0", Z + 2048, Z + 3200), A("R0", Z, Z + 1152), "V")
    cp(A("R0", Z + 4096, Z + 5248), A("R0", Z, Z + 1152))
    ms(A("R0", Z, Z + 2049, 2048), 256.0)
    mm([acc(A("pM0", 128 * h, 128 * h + 128), A("XX0", 256 + 128 * h, 384 + 128 * h), A("ID"), True, True) for h in (0, 1)])
    cp(A("XX0", 0, 256), A("pM0", 0, 256))
    cp(A("VV0", 64, 128), A("VS"))
    cp(IND(A("YV"), A("SO", 0, 4)), A("VV0", 64, 128))
    mm([acc(A("pA"), A("R16"), A("YV"), True, True)])
    cp(A("YVC"), A("pA"))
    cp(A("VV0", 0, 64), IND(A("YVC"), A("GO")))
    for t in (1, 2, 3):
        send(A("XX0"), A("XX%d" % t), t, "xx%d" % t, 12000.0)
        send(A("VV0"), A("VV%d" % t), t, "vv%d" % t, 8000.0)
    cp(A("D1", Z, Z + 512), A("ND", 0, 512))
    cp(A("D1", Z + 512, Z + 1024), A("ND", 512, 1024))
    ms(A("D1", Z + 1024, Z + 1152), 0.0)
    ms(A("RST8"), 0.0)
    fill(A("MONE"), -1)
    sel(A("ID3"), A("ONE", 0, 256), [[0, 2], [-1, 128]], ALU.is_equal, 0, 1)
    ms(A("RST8", 0, 512, 8), 8192.0)
    sel(A("TRI"), A("BO"), [[1, 128]], ALU.is_ge, 0, -1)
    sel(A("T63"), A("TRI"), [[-1, 128]], ALU.not_equal, 0, 1, -63.0)
    aff(A("NBO"), A("BO"), -1.0)
    for n, v, d in (("TN", 16384.0, -31.0), ("TQ", -32768.0, -64.0)):
        aff(A(n), A("TRI"), v)
        sel(A(n), A(n), [[-1, 128]], ALU.not_equal, 0, 1, d * v)
    sel(A("DG"), A("ONE", 0, 160), [[-1, 160]], ALU.is_equal, 16, 1)
    for t in (0, 8, 2, 10):
        sel(A("SL%d" % t), A("DG"), [[0, 10], [1, 16]], ALU.is_equal, -t, 0)
    for j in range(4):
        sel(A("BJ", 512 * j, 512 * j + 512), A("ONE"), [[-1, 4], [-16, 8], [0, 16]], ALU.is_equal, -4 * j, 1)
    off = [0, 64, 192, 384, 640]
    fill(A("NBIG", 0, 256, 1, 0, 16), -int(BIG))
    ts(A("COL", 11, 12), A("PI", 0, 1), -16.0, ALU.add)
    for c in range(4):
        w = 16 * c + 16
        ts(A("MASK", off[c], off[c + 1], 1, 0, 32), A("ONE", 0, 4 * w, 1, 0, 32), A("COL", 11, 12, 1, 0, 32), ALU.mult, 16.0 * c, ALU.add)
        ts(A("CSEL", 128 * c, 128 * c + 2 * w), A("ONE", 0, 2 * w), A("BSEL", c, c + 1), ALU.mult, 8192.0, ALU.mult)
        sel(A("MASK", off[c], off[c + 1], 1, 0, 16), A("NBIG", 0, 4 * w, 1, 0, 16), [[0, 4], [-1, w]], ALU.is_ge, 16 * c - 1, 1, BIG)
        x = A("MASK", off[c], off[c] + w, 1, 0, 16)
        sel(x, x, [[1, w]], ALU.not_equal, -16 * c, -1, 0.0)
        sel(A("ASR", off[c], off[c + 1]), A("ONE", 0, 4 * w), [[0, 4], [-1, w]], ALU.is_equal, 0, 1)
    fill(A("AB", 24, 32), 0)
    for j in (0, 1):
        cp(A("R16B", 128 * j, 128 * j + 128), A("R16"))
    for n, at in (("SEA", 0), ("SEB", 8)):
        fill(A(n), 0)
        sel(A(n), A(n), [[-1, 8], [0, 16]], ALU.not_equal, -at, 1, -8192.0)
        sel(A(n), A(n), [[-1, 8], [0, 16]], ALU.not_equal, -16, 1, BIG)
    fill(A("BSB"), 0)
    for c in (4, 12, 16, 20):
        cp(A("BSB", c, c + 4), A("BO", 0, 64, 16))
    iota(A("NV"), [[1, 128]], 2048 + 1024 + 16384, 0)
    aff(A("KEEP"), A("R16", 0, 16), -1.0, 1.0)
    for t in (0, 2):
        n = "ADD%d" % t
        fill(A(n, 0, 8), Z)
        iota(A(n, 8, 12), [[16, 4]], Z + 1024 + 32 * t, 0)
        iota(A(n, 12, 24), [[2048, 3], [0, 4]], Z, 0)
        iota(A(n, 24, 32), [[2048, 2], [16, 4]], Z + 1024 + 32 * t, 0)
        ts(A(n, 8, 12), A(n, 8, 12), A("COL", 1, 2), ALU.add)
        ts(A(n, 24, 32), A(n, 24, 32), A("COL", 1, 2), ALU.add)
    nx = [0]

    def xbank(h):
        nx[0] += 1
        return ("pX%d" if nx[0] % 2 else "pM%d") % h

    def nodes(t):
        return A("D%d" % t, Z, Z + 1152) if t else A("ND")

    def recs(t, c0=Z):
        return A("R%d" % ((t + 1) // 2), c0)

    def whole(t, h):
        return h == 0 and t % 2 == 0

    def gather(t, h, s):
        H = str(h)
        vo = A("VS16", 16 * t + 8 * h, 16 * t + 8 * h + 8) if s == 2 else A("SU%d%d" % (t, h), 8 - 8 * s, 16 - 8 * s)
        if s == 2 or (s == 0 and whole(t, h)):
            cp(A("EU" + H), IND(nodes(t), vo))
        else:
            ts(A("EU" + H), IND(nodes(t), vo), 4095.0 if s else 2048.0, ALU.min)
        mode = how(t, h, s)
        heads = [j for j, e in enumerate(mode) if j == 0 or e.isupper() or mode[j - 1] == "F"] + [4]
        for j, j2 in zip(heads, heads[1:]):
            rec = IND(recs(t), A("EU" + H, 32 * j, 32 * j2))
            if mode[j] == "F":
                tt(A("RD" + H, 512 * j, 512 * j2), rec, A("XR%d%d" % (t % 2, h), 512 * j, 512 * j2), ALU.subtract)
            else:
                cp(A("RG" + H, 512 * j, 512 * j2), rec, "S" if mode[j] in "STst" else "V")

    def how(t, h, s):
        mode = O["mode"][t % 2][h][2 - s]
        return mode if t else mode.replace("F", O["f0"][h])

    def spread(t, h):
        f = [j for j in range(4) if any(how(t, h, s)[j] == "F" for s in range(3))]
        for i in range(16 if f else 0):
            x = A("XX%d" % t, 256 + 128 * h + 32 * f[0], 288 + 128 * h + 32 * f[-1])
            sel(A("XR%d%d" % (t % 2, h), 512 * f[0] + i, 512 * f[-1] + 512, 16), x, [[0, _n(x)]], ALU.is_ge, 0, 0)

    def runs(t, h, s):
        f, out = [e == "F" for e in how(t, h, s)], []
        for j in range(4):
            if j and f[j] == f[j - 1] and (out[-1][0] == 0 or (out[-1][0] == 2 and j == 3)):
                out[-1][1] = j + 1
            else:
                out.append([j, j + 1, "RD" if f[j] else "RG"])
        return out

    def compare(e, cm, rg, px, xt, rep):
        if e in "SVsv":
            mm([acc(px, xt, rep, True, True)])
            tt(cm, rg, px, ALU.is_le)
        else:
            mm([acc(px, xt, rep, True)])
            mm([acc(px, A("NID"), rg, False, True)])
            comp("S", "activation", [cm, px, ACT.Sigmoid], {"scale": 64.0, "bias": A("COL", 8, 9)})

    def level(t, h, s):
        n = s + 1
        H = str(h)
        EU, RG, CM, pV, SC, NW = [x + H for x in ("EU", "RG", "CM", "pV", "SC", "NW")]
        xt, cc, bk = A("XX%d" % t, 128 * h, 128 * h + 128), A("CC", COFF[s], COFF[s] + 144 * n), "BK%d" % t
        lst = [acc(A(pV, 0, 144 * n), A("L1"), cc, True)]
        if s < 2:
            lst += [acc(A(pV, 0, 144 * n, W), A("ID32"), A(SC, W - 1, 144 * n, W)), acc(A(pV, 0, 144 * n, W), A("ID2K"), A(NW, 16 - 16 * s, 16 - 16 * s + 8 * n))]
        if s == 1:
            lst += [acc(A(pV, 145, 288, W), A("ID32"), A("SG%d%d" % (t, h), 16, 24))]
        if s == 2:
            lst += [acc(A(pV, 289, 432, W), A("NID32"), A("VV%d" % t, 16 * t + 8 * h, 16 * t + 8 * h + 8))]
        mm(lst)
        if s or whole(t, h):
            ts(A("U" + H), A(EU), 2048.0, ALU.is_ge)
            mm([acc(A(pV, 0, 288 if s else 144), A("U" + H), A("UW", 0, 288 if s else 144))])
        if s == 2:
            ts(A("W" + H), A(EU), 4096.0, ALU.is_ge)
            mm([acc(A(pV, 144, 432), A("W" + H), A("UW"))])
        ts(A("E0" + H), A(EU), -1.0, ALU.mult, 1024.0, ALU.add)
        if s:
            ts(A("E1" + H), A(EU), -1.0, ALU.mult, 3072.0, ALU.add)
        for j, e in enumerate(how(t, h, s)):
            if e == "F":
                ts(A(CM, 512 * j, 512 * j + 512), A("RD" + H, 512 * j, 512 * j + 512), 0.0, ALU.is_le)
            else:
                compare(e, A(CM, 512 * j, 512 * j + 512), A(RG, 512 * j, 512 * j + 512), A(xbank(h)), xt, A("REP", 512 * j, 512 * j + 512))
        if s == 2 and t:
            rg, cm, gm, px = "RGG" + H, "CMG" + H, "GM%d%d" % (t, h), xbank(h)
            mm([acc(A(px, 0, 256), xt, A("ID3", 0, 256), True, True)])
            for ks, c0, c1 in (((2, 1), 0, 256), ((0,), 256, 384)):
                cp(A(rg, c0, c1), IND(recs(t), A("GU%d%d" % (t, h), c0 // 16, c1 // 16)), "S" if c0 == 0 else "E")
                tt(A(cm, c0, c1), A(rg, c0, c1), A(px, 0, c1 - c0), ALU.is_le)
                out, n8 = A(pV, 144 * ks[-1], 144 * ks[0] + 144, W), 8 * len(ks)
                mm([acc(out, A("L1"), A("CT", 144, 144 + n8))] +
                   [acc(A(pV, 144 * k, 144 * k + 144, W), A(cm, 256 - 128 * k, 384 - 128 * k), A(bk, 0, 8)) for k in ks] + [acc(out, A("L2"), A("CT", 144, 144 + n8))] +
                   [acc(A(pV, 144 * k, 144 * k + 144, W), A(rg, 256 - 128 * k, 384 - 128 * k), A("BO4K", 0, 8)) for k in ks])
            out = A(pV, 0, 432, W)
            mm([acc(out, A("ID32"), A(gm, 0, 24)), acc(out, A("NID32"), A(gm, 24, 48)), acc(out, A("L1"), A("CG", 0, 24))])

    def choose(t, h, s):
        n = s + 1
        H = str(h)
        RG, CM, pV, SC, NW = [x + H for x in ("RG", "CM", "pV", "SC", "NW")]
        mm([acc(A(pV, 2 + i, 144 * n, W), A(CM, i, 2048, 16), A("BK%d" % t, 0, 8 * n)) for i in range(16)] +
           [acc(A(pV, 0, 144 * n), A("L2"), A("CC", COFF[s], COFF[s] + 144 * n)), acc(A(pV, 0, 144), A("E0" + H), A("IW", 0, 144))] +
           [acc(A(pV, 144, 144 * n), A("E1" + H), A("IW", 0, 144 * s))] * (s > 0) +
           [acc(A(pV, 2 + i, 144 * n, W, 32 * a, 32 * b), A(x + H, 512 * a + i, 512 * b, 16), A("BO4K", 0, 8 * n), False, i == 15)
            for i in range(16) for a, b, x in runs(t, h, s)])
        for c0, c1 in ((144 * s, 144 * n), (0, 144 * s)) if s and O["split"] else ((0, 144 * n),):
            comp("V", "tensor_tensor_scan", [A(SC, c0, c1), A("RST", c0, c1), A(pV, c0, c1), -4 * B, ALU.add, ALU.max])
        k = 1 - t % 2
        sg, out, su = "SG%d%d" % (t, h), A(pV, 448, 456), A("SU%d%d" % (t, h), 16 - 8 * s, 24 - 8 * s)
        if s or t < 3:
            tt(A("KE" + H), IND(A(SC, 144 * s, 144 * n), A("EXK", 0, 8)), A("R16"), ALU.mult)
            mm([acc(out, A("KE" + H), A("BSEL", 0, 8), True), acc(out, A("L1"), A("CT", 0, 8)), acc(out, A("L2"), A("CT", 0, 8)),
                acc(out, A("KE" + H), A("BSEL", 8, 16), False, True)])
            ts(su, out, 1024.0, ALU.add)
        k0 = 0 if (h, s, k) == (0, 1, 0) else s
        keys, hi = A(SC, 144 * k0 + W - 1, 144 * n, W), A("HI" + H, 8 * k0, 8 * n)
        ts(hi, keys, R2K, ALU.add, R2K, ALU.subtract)
        tt(A(sg, 8 * k0, 8 * n), keys, hi, ALU.subtract)
        m = (8, 16 if whole(t, h) else 8, 16)[s]
        if s:
            tt(A(NW, 32 - 16 * s, 32 - 16 * s + m), A(SC, W - 1, W * m, W), A(SC, 1, W * m, W), ALU.is_gt)
        if h == 0 and s:
            source(t, s)

    def source(t, s):
        k, NW, sg = 1 - t % 2, "NW0", "SG%d0" % t
        nw = A(NW, 32 - 16 * s + 8 * k, 40 - 16 * s + 8 * k)
        if s == 2:
            tt(A("HM", 0, 8), A("VV%d" % t, 16 * t, 16 * t + 8), nw, ALU.mult)
            if k:
                tt(A("HM", 0, 8), A("pA", 16, 24), A("HM", 0, 8), ALU.min)
            aff(A("HM", 8, 16), A(sg, 16, 24), -1.0, 1024.0)
            if not k:
                tt(A("DV", 0, 8), A("HM", 8, 16), A("HM", 0, 8), ALU.subtract)
        else:
            tt(A("DV", 8, 16), A("DV", 0, 8), nw, ALU.mult)
            tt(A("AB", 16, 24), A("HM", 0, 8), A("DV", 8, 16), ALU.add)
            aff(A("AB", 8 * k, 16), A(sg, 8 * k, 16), -1.0, 1024.0)

    def roomy(t, s):
        ts(A("FS"), A("EU0"), 0.0, ALU.is_equal)
        mm([acc(A("pA", 16, 24), A("FS"), A("BO4K", 0, 8), True, True)])
        if s == 1:
            tt(A("HM", 8, 16), A("pA", 16, 24), A("HM", 8, 16), ALU.min)
            tt(A("DV", 0, 8), A("HM", 8, 16), A("HM", 0, 8), ALU.subtract)

    def handon(t, h):
        H = str(h)
        keys, low, pV = A("SC" + H, W - 1, 432, W), "SG%d%d" % (t, h), "pV" + H
        if t < 3:
            ts(A(low, 24, 48), keys, THR, ALU.is_lt, B, ALU.mult)
            either(ACT.Relu, keys, {"scale": -8192.0, "bias": A("COL", 9, 10)})
            send(A("SU%d%d" % (t, h), 0, 16), A("GU%d%d" % (t + 1, h), 0, 16), 1, "gw%d%d" % (t + 1, h))
            send(A("SU%d%d" % (t, h), 16, 24), A("GU%d%d" % (t + 1, h), 16, 24), 1, "gu%d%d" % (t + 1, h))
            send(A(low), A("GM%d%d" % (t + 1, h)), 1, "gm%d%d" % (t + 1, h))
        else:
            aff(A("NM" + H, 0, 24), A(low, 0, 24), -1.0, 1024.0)
            ts(A("NZ" + H, 0, 24), keys, THR, ALU.is_ge)
            tt(A("GN" + H, 0, 24), A("NM" + H, 0, 24), A("NZ" + H, 0, 24), ALU.mult)
            mm([acc(A(pV, 0, 128, 1, 0, 24), A("GN" + H, 0, 24), A("ID32"), True, True)])
            cp(A("YO", 128 * h, 128 * h + 128, 1, 0, 24), A(pV, 0, 128, 1, 0, 24))
            for k in range(3):
                dma("Y", ("hbm", "yg", (256 * k + 128 * h, 256 * k + 128 * h + 128)), A("YO", 128 * h, 128 * h + 128, 1, 8 * k, 8 * k + 8), "out", 2000)

    def ask(t):
        even = t % 2 == 0
        X, m, low = A("XX%d" % t, 256, 320), 32 if even else 16, (1, 0, 64)
        old, new = A("D%d" % max(t, 1), Z, Z + 1152), A("D%d" % (t + 1))
        pxt, ptt, pc0, pc1, pct, pg, pz0, pz1 = [{"A": "pA", "B": "pB", "X": "pX0", "M": "pM0"}[x] for x in O["banks"][t % 2]]

        def room(e):
            ts(A("FR"), A(e), 0.0, ALU.is_equal)
            either(ACT.Relu, A(e), {"scale": -1.0, "bias": 1.0})
            if not even:
                mm([acc(A("pA", 16, 24, *low), A("FR"), A("BO1", 0, 8), True, True)])
                tt(A("Q2", 0, 8, *low), A("pA", 16, 24, *low), A("AB", 16, 24, *low), ALU.min)
            first = A(pg, 128, 192)
            mm([acc(first, A("L1"), A("CT", 176, 240), True), acc(first, A("TQ"), A("FR"), False, True)])
            if even:
                aff(A("PL"), first, 0.5, -16384.0)
                tt(A("P0"), first, A("NV", 32 * t, 32 * t + 64), ALU.min)
            else:
                ts(A("P0"), first, 0.0, ALU.is_gt)

        cp(A("EB"), IND(old, A("SU%d0" % t, 8, 12)))
        if not even:
            room("EB")
        tt(A("Q1", 0, 8), A("AB", 8, 16), A("AB", 16, 24), ALU.not_equal)
        tt(A("AB", 24, 32, *low), A("AB", 16, 24, *low) if even else A("Q2", 0, 8, *low), A("Q1", 0, 8, *low), ALU.min)
        rows = (1, 0, 24 if even else 16)
        mm([acc(A(ptt, 64, 128, *rows), A("AB", 8, 8 + rows[2], *low), A("ID32", 0, 64, *low), True, True)])
        cp(A("TT", 0, 64, *rows), A(ptt, 64, 128, *rows))
        tt(A("OWN"), IND(A("AB", 8, 24), A("EX")), A("R16B"), ALU.mult)
        mm([acc(A(pxt, 32, 64), A("OWN", 0, 128, *low), A("BSB", 0, 32, *low), True), acc(A(pxt, 32, 36), A("OWN", 128, 256, *low), A("BSB", 4, 8, *low), False, True)])
        cp(A("AO", 0, 4), A(pxt, 32, 36))
        tt(A("XT", 0, m), A(pxt, 32, 32 + m), A("ADD%d" % (t & 2), 0, m), ALU.add)
        cp(A("EA"), IND(old, A("AO", 0, 4)))
        if even:
            room("EA")
        else:
            cp(A("G0X"), IND(A("AB", 0, 8), A("EX", 0, 8)))
            mm([acc(A(pg, 0, 64), A("G0X", 0, 128, *low), A("ID", 0, 64, *low), True, True)])
            tt(A("NE"), A("EA"), A(pg, 0, 64), ALU.not_equal)
            tt(A("P0"), A("P0"), A(pg, 0, 64), ALU.mult)
            aff(A("AX0"), IND(A("AB", 24, 32), A("EX", 0, 8)), BIG)
        for cs, ps in zip(((0, 1, 2), (3,)), (pc0, pc1)):
            o0 = off[cs[0]]
            lst = [acc(A(ps, 0, off[cs[-1] + 1] - o0), A("R16B", 0, 128, 1, 0, 32), A("MASK", o0, off[cs[-1] + 1], 1, 0, 32), True)]
            for c in cs:
                w, at = 16 * c + 16, off[c] - o0
                lst += [acc(A(ps, at + 2 * w * j, at + 2 * w * j + 2 * w), A("OWN", 128 * j, 128 * j + 128, *low), A("CSEL", 128 * c, 128 * c + 2 * w, *low)) for j in (0, 1)]
            mm(lst)
            for c in cs:
                w, at = 16 * c + 16, off[c] - o0
                mm([acc(A(ps, at + b * w, at + b * w + w), A(o, 0, 128, *rows), A("TT", 0, w, *rows), False, even and c == cs[-1] and b == 3)
                    for b, o in enumerate(("SEA", "SEB", "SEB", "SEA"))])
            if even:
                least(cs, ps)
        if even:
            act(t)

    def least(cs, ps):
        for c in cs:
            comp("V", "tensor_reduce", [A("MN", c, c + 1), A(ps, off[c] - off[cs[0]], off[c + 1] - off[cs[0]]), AxisListType.X, ALU.min],
                 {"apply_absolute_value": True})

    def act(t):
        even = t % 2 == 0
        X, m, low, new = A("XX%d" % t, 256, 320), 32 if even else 16, (1, 0, 64), A("D%d" % (t + 1))
        pxt, ptt, pc0, pc1, pct, pg, pz0, pz1 = [{"A": "pA", "B": "pB", "X": "pX0", "M": "pM0"}[x] for x in O["banks"][t % 2]]
        if not even:
            tt(A("NN", 0, 8), A("SC0", W - 1, 144, W), A("SC0", 1, 144, W), ALU.is_le)
            tt(A("AX1"), IND(A("NN", 0, 8), A("EX", 0, 8)), A("AX0"), ALU.mult)
            for cs, ps in zip(((0, 1, 2), (3,)), (pc0, pc1)):
                mm([acc(A(ps, 0, off[cs[-1] + 1] - off[cs[0]]), A("AX1", 0, 128, *low), A("ASR", off[cs[0]], off[cs[-1] + 1], *low), False, True)])
                least(cs, ps)
        tt(A("OF", 0, m), IND(A("MN"), A("RA", 0, m // 16)), A("XT", 0, m), ALU.min)
        cp(A("OU", 0, m), A("OF", 0, m))
        if t < 3:
            ts(A("ACB", 0, 4), A("MN", 0, 4), 4096.0, ALU.is_gt)
            out = A(pct, 0, 1)
            mm([acc(out, A("L1"), A("CT", 168, 169), True)] + [acc(out, A("ONE", 0, 128), A("ACB", c, c + 1)) for c in range(4)] +
               [acc(out, A("L1"), A("CT", 169, 170)), acc(out, A("L1"), A("CT", 170, 171))] +
               [acc(out, A("MONE"), A("ACB", c, c + 1), False, c == 3) for c in range(4)])
            ts(A("SK%d" % t, 0, 24), A("BOS", 0, 24), out, ALU.mult)
            send(A("SK%d" % t, 0, 24), A("BK%d" % (t + 1), 0, 24), 1, "ka%d" % (t + 1))
        if not even:
            tt(IND(new, A("OU", 0, 4)), A("EA"), A("NE"), ALU.mult)
            tt(IND(new, A("OU", 4, 8)), A("EB"), A("P0"), ALU.add)
            return
        for o, x, r in (("RC", "XC", 8 + t), ("RH", "XH", t)):
            aff(A(o), IND(recs(t), A("SU%d0" % t, 8, 12)), A("KEEP", r, r + 1))
            aff(A(x), X, A("R16", r, r + 1))
        for j in range(5):
            o, x = ("RC", "XC") if j < 3 else ("RH", "XH")
            tt(IND(recs(t + 1, 0), A("OU", 12 + 4 * j, 16 + 4 * j)), A(o), A(x), ALU.add)
        for b, r in ((0, t), (1, 8 + t)):
            out = A("pB", 64 * b, 64 * b + 64)
            mm([acc(out, A("BJ", 128 * (r ^ 8), 128 * (r ^ 8) + 128), X, True)] +
               [acc(out, A("SL%d" % r, r + 16 - i, r + 144 - i), A("RG0", i, 1024, 16), False, i == 15) for i in range(16)])
        ts(A("NGS"), A("pB", 0, 128), 0.0, ALU.is_lt)
        either(ACT.Sigmoid, A("pB", 0, 128), {"scale": -64.0, "bias": A("COL", 10, 11)})
        tt(A("STR"), A("NGS", 0, 64), A("NGS", 64, 128), ALU.mult)
        aff(A("GON"), A("NGS", 0, 64), -1.0, 1.0)
        ts(A("EHI"), A("EB"), R1K, ALU.add, R1K, ALU.subtract)
        tt(A("ELO"), A("EHI"), A("EB"), ALU.subtract)
        mm([acc(A("pB", 0, 64), A("L1"), A("CT", 80, 144), True), acc(A("pB", 0, 64), A("TN"), A("STR"), False, True)])
        tt(A("NBE"), A("pB", 0, 64), A("EHI"), ALU.subtract)
        mm([acc(A("pB", 64, 128), A("NBO"), A("FR"), True), acc(A("pB", 64, 128), A("T63"), A("STR")), acc(A("pB", 64, 128), A("ID2K"), A("NGS", 0, 64), False, True)])
        ts(A("KP"), A("pB", 64, 128), 1984.0, ALU.is_ge)
        for b, ps in enumerate((pz0, pz1)):
            for q in (0, 4):
                lst = []
                for j in range(q, q + 4):
                    out, bj = A(ps, j, 512, 8), A("BJ", 128 * (8 * b + j), 128 * (8 * b + j) + 128)
                    lst += [acc(out, A("ID"), A("PL"), True), acc(out, bj, A("NBE")), acc(out, bj, A("ELO"), False, True)]
                mm(lst)
            comp("S", "activation", [A("ZA", 512 * b, 512 * b + 512), A(ps), ACT.Abs])
            comp("V", "tensor_tensor_scan", [A("ZS", 512 * b, 512 * b + 512), A("RST8"), A("ZA", 512 * b, 512 * b + 512), 0.0, ALU.max, ALU.min])
        aff(A("NE"), A("EA"), 1.0, 16384.0)
        tt(A("P0"), A("P0"), A("NE"), ALU.max)
        tt(IND(new, A("OU", 4, 8)), A("EB"), A("KP"), ALU.mult)
        tt(IND(new, A("OU", 8, 12)), A("EB"), A("GON"), ALU.mult)
        tt(A("P0"), A("P0"), A("ZS", 7, 512, 8), ALU.subtract)
        tt(IND(new, A("OU", 0, 4)), A("P0"), A("ZS", 519, 1024, 8), ALU.subtract)

    def copies(t):
        last = max(i for i, o in enumerate(ops) if o["calls"] and o["calls"][0][0] == "tensor_tensor_scan")
        if t % 2 == 0:
            dma("Y", recs(t + 1), recs(t), "cr%d" % (t // 2 + 1), 7000)
            ops[-1]["also"] = last
        if t:
            dma("Y", nodes(t + 1), nodes(t), "cd%d" % (t + 1), 4000)
            ops[-1]["also"] = last
        if t == 3:
            dma("Y", ("hbm", "yr", (0, 2)), A("R2", Z + 4096, Z + 4098), "out", 3000)
            ops[-1]["also"] = last
            dma("Y", ("hbm", "yr", (2, 1152)), A("R2", Z + 2050, Z + 3200), "out", 3000)
            ops[-1]["also"] = last

    for t in range(NT):
        even = t % 2 == 0
        cp(A("VS16", 16 * t, 16 * t + 16), A("VV%d" % t, 64 + 16 * t, 80 + 16 * t) if t else A("VS", 0, 16))
        for h in (0, 1):
            part[0] = (t, h, "walk", 2)
            spread(t, h)
            for s in (2, 1, 0):
                part[0] = (t, h, "walk", s)
                gather(t, h, s)
                if s and whole(t, h):
                    roomy(t, s)
                level(t, h, s)
                if s == 0 and h == 0:
                    part[0] = (t, h, "act", s)
                    ask(t)
                    part[0] = (t, h, "walk", s)
                choose(t, h, s)
                if (h, s) == (0, 2):
                    copies(t)
            if h == 0 and not even:
                part[0] = (t, h, "act", 0)
                act(t)
            part[0] = (t, h, "hand", 0)
            handon(t, h)
    dma("Y", ("hbm", "yn", None), nodes(4), "out", 4000)
    return ops


def inorder(ops, deps, i, j):
    return ops[i]["eng"] == ops[j]["eng"] and "sem" not in ops[j] and (ops[i]["eng"] == "P" or deps[i].get(j, True) is None or
                                                                               (not OPT["war"] and ops[i]["eng"] in "VS" and "sem" not in ops[i] and not deps[i].get(j, True)))


def order(ops):
    C = COST
    seen, deps = {}, []
    for i, o in enumerate(ops):
        if "alt" in o:
            o.update(eng="V", calls=o["alt"]["V"][0], cost=o["alt"]["V"][1])
        d = {o["also"]: True} if "also" in o else {}
        for x, wr in [(x, False) for x in o["r"]] + [(x, True) for x in o["w"]]:
            ps = TILE[x[1]][0] == "psum"
            lo, hi = (0, 512) if ps else (x[2], x[3])
            lst = seen.setdefault(x[1], [])
            for a, b, j, w2, y in lst:
                apart = not ps and ((x[4] == y[4] and (a - lo) % x[4]) or x[6] <= y[5] or y[6] <= x[5])
                if j != i and a < hi and lo < b and (wr or w2 or ps) and not apart:
                    d[j] = (d.get(j) or (w2 and not wr)) if wr or w2 else d.get(j)
            if (wr and x[4] == 1 and x[6] - x[5] == 128) or ps:
                lst[:] = [e for e in lst if not (lo <= e[0] and e[1] <= hi)]
            lst.append((lo, hi, i, wr, x))
        deps.append(d)
    n = len(ops)
    pre = [list(deps[i]) + ([ops[i]["after"]] if "after" in ops[i] else []) for i in range(n)]
    suc = [[] for _ in ops]
    for i in range(n):
        for j in pre[i]:
            suc[j].append(i)
    late = [o["lat"] if "lat" in o and o["eng"] != "R" else 0.0 for o in ops]
    loose = set(x for i in range(n) for j, v in deps[i].items() if v is None or not (v or OPT["war"] or ops[i]["eng"] not in "VS" or "sem" in ops[i] or "sem" in ops[j]) for x in ((i, j), (j, i)))
    alt, links, base, ind = [o.get("alt") for o in ops], (pre, suc), [o["cost"] for o in ops], [o["ind"] for o in ops]

    def lay(rank, back=None):
        pre, suc = (links[1], links[0]) if back else links
        left, eng = [len(p) for p in pre], back or [o["eng"] for o in ops]
        cost = [alt[i][eng[i]][1] if alt[i] else ops[i]["cost"] for i in range(n)]
        ready = {i: late[i] if back else 0.0 for i in range(n) if not left[i]}
        free, seq, t0, t1 = dict.fromkeys("VSPGYR", 0.0), [], [0.0] * n, [0.0] * n
        while ready:
            st, first = {}, None
            for i, r in ready.items():
                if alt[i] and not back:
                    eng[i] = "V" if max(r, free["V"]) + alt[i]["V"][1] + C["lean"] * (ops[i]["part"][2] == "act") <= max(r, free["S"]) + alt[i]["S"][1] else "S"
                    cost[i] = alt[i][eng[i]][1]
                st[i] = max(r, free[eng[i]])
                if first is None or (st[i], -rank[i]) < (st[first], -rank[first]):
                    first = i
            till = st[first] + min(C["look"], cost[first])
            i = max((j for j in st if eng[j] == eng[first] and st[j] <= till), key=lambda j: rank[j] - C["beta"] * st[j])
            del ready[i]
            if eng[i] != "R":
                free[eng[i]] = st[i] + cost[i]
            t0[i], t1[i] = st[i], st[i] + cost[i] + (0.0 if back else late[i])
            seq.append(i)
            for j in suc[i]:
                left[j] -= 1
                if not left[j]:
                    ready[j] = max(t1[k] + (0.0 if eng[k] == eng[j] and (eng[k] == "P" or (k, j) in loose) else C["lat"]) for k in pre[j]) + (late[j] if back else 0.0)
        return max(t1), seq, eng, t0, t1

    def replay(seq, eng, lat, gather):
        free, last, t1, why = dict.fromkeys("VSPGYR", 0.0), dict.fromkeys("VSPGYR", -1), [0.0] * n, [-1] * n
        for i in seq:
            e = eng[i]
            st, w = free[e], last[e]
            for k in pre[i]:
                v = t1[k] if e == eng[k] and (e == "P" or (k, i) in loose) else t1[k] + lat
                if v > st:
                    st, w = v, k
            c = alt[i][e][1] if alt[i] else base[i]
            if ind[i]:
                c *= gather
            if e != "R":
                free[e], last[e] = st + c, i
            t1[i], why[i] = st + c + late[i], w
        return t1, why

    def worth(rank):
        end, seq, eng, t0, t1 = lay(rank)
        return sum(max(replay(seq, eng, C["lat"] + a, b)[0]) for a, b in CASES)

    rank = [0.0] * n
    for i in range(n - 1, -1, -1):
        rank[i] = ops[i]["cost"] + late[i] + max([rank[j] + C["lat"] for j in suc[i]], default=0.0)
    rank = [rank[i] - 1000 * OPT["lag"][o["part"][0]][2 - o["part"][3]] * o["part"][1] for i, o in enumerate(ops)]
    best, seed, other = worth(rank), [OPT["seed"]], rank
    for _ in range(OPT["turns"]):
        end, seq, eng, t0, t1 = lay(other)
        other = lay(t1, eng)[4]
        v = worth(other)
        if v < best:
            rank, best = other, v

    def draw(m):
        seed[0] = (seed[0] * 1103515245 + 12345) % 2 ** 31
        return (seed[0] >> 8) % m

    def ends(seq, eng):
        runs = [replay(seq, eng, C["lat"] + a, b) for a, b in CASES]
        return sum(max(r[0]) for r in runs), runs[draw(len(runs))]

    end, seq, eng, t0, t1 = lay(rank)
    seq.sort(key=lambda i: t0[i])
    now, (t1, why) = ends(seq, eng)
    best = (now, seq, eng)
    for step in range(OPT["tries"]):
        chain = [max(range(n), key=lambda i: t1[i])]
        while why[chain[-1]] >= 0:
            chain.append(why[chain[-1]])
        pairs = [(a, b) for b, a in zip(chain, chain[1:]) if eng[a] == eng[b] and a not in pre[b]]
        both, seq2, eng2 = [i for i in chain if alt[i]], seq, eng
        if both and draw(7) == 0:
            i = both[draw(len(both))]
            eng2 = eng[:i] + ["S" if eng[i] == "V" else "V"] + eng[i + 1:]
        else:
            a, b = pairs[draw(len(pairs))]
            lo, hi, ahead = seq.index(a), seq.index(b), draw(2)
            for _ in range((0, 0, 1, 2, 4)[draw(5)]):
                more = [q for q in (range(lo - 1, max(lo - 40, -1), -1) if ahead else range(hi + 1, min(hi + 40, n))) if eng[seq[q]] == eng[a]]
                lo, hi = (more[0] if more and ahead else lo), (more[0] if more and not ahead else hi)
            mid, tied = seq[lo:hi + 1], {b if ahead else a}
            for i in reversed(mid) if ahead else mid:
                if i in tied:
                    tied.update(pre[i] if ahead else suc[i])
            seq2 = seq[:lo] + [i for i in mid if (i in tied) == bool(ahead)] + [i for i in mid if (i in tied) != bool(ahead)] + seq[hi + 1:]
        v, run = ends(seq2, eng2)
        if v <= now + draw(1000) ** 2 * C["heat"] * (1 - step / OPT["tries"]) ** 2:
            now, seq, eng, (t1, why) = v, seq2, eng2, run
            if now < best[0]:
                best = (now, seq, eng)
    _, seq, eng = best
    t1 = replay(seq, eng, C["lat"], 1.0)[0]
    for i, o in enumerate(ops):
        if alt[i]:
            o.update(eng=eng[i], calls=alt[i][eng[i]][0], cost=alt[i][eng[i]][1])
        o.update(t0=t1[i] - late[i] - o["cost"], t1=t1[i])
    return seq, deps, max(t1)


def waits(ops, seq, deps):
    pos, known, clock, need, cnt = {}, {}, {}, {}, {}
    for i in seq:
        o = ops[i]
        key = o.get("sem") or o["eng"]
        pos[i] = (key, cnt.get(key, 0))
        cnt[key] = cnt.get(key, 0) + 1
        kn = known.setdefault(o["eng"], {})
        need[i] = []
        if o["eng"] != "R":
            for j in sorted(deps[i], key=lambda j: -ops[j]["t1"]):
                if inorder(ops, deps, i, j):
                    continue
                k, p = pos[j]
                if kn.get(k, -1) < p:
                    need[i].append(j)
                    for k2, p2 in clock[j].items():
                        kn[k2] = max(kn.get(k2, -1), p2)
        clock[i] = dict(kn) if o["eng"] != "R" else {}
        clock[i][key] = pos[i][1]
    return need


PLAN = {}


def rank_program(g, core, T, topo):
    rank = T.rank_of(core)
    if rank is None:
        return
    if not PLAN:
        ops = program()
        seq, deps, _ = order(ops)
        PLAN.update(ops=ops, seq=seq, need=waits(ops, seq, deps))
    ops, seq, need = PLAN["ops"], PLAN["seq"], PLAN["need"]
    queue = {"V": g.vector, "S": g.scalar, "P": g.tensor, "G": g, "Y": g.sync}
    call = {"V": {"tensor_scalar": g.vector.tensor_scalar, "tensor_tensor": g.vector.tensor_tensor, "tensor_copy": g.vector.tensor_copy,
                  "memset": g.vector.memset, "tensor_tensor_scan": g.vector.tensor_tensor_scan, "tensor_reduce": g.vector.tensor_reduce},
            "S": {"activation": g.scalar.activation, "dma_start": g.scalar.dma_start}, "P": {"matmul": g.tensor.matmul},
            "G": {"iota": g.iota, "affine_select": g.affine_select}, "Y": {"dma_start": g.sync.dma_start}}

    def view(x):
        if not isinstance(x, tuple):
            return x
        if x[0] == "ind":
            return view(x[1]).indirect(view(x[2]))
        if x[0] == "hbm":
            return T[x[1]][:] if x[2] is None else T[x[1]][:, x[2][0]:x[2][1]]
        buf, at = PLACE[x[1]]
        return T[buf][x[5]:x[6], at + x[2]:at + x[3]] if x[4] == 1 else T[buf][x[5]:x[6], at + x[2]:at + x[3]:x[4]]

    def lanes(a, b):
        return topo.engines(a, b)[:OPT["eng"]]

    marked = set(j for i in seq for j in need[i])
    total, value = {}, {}
    for i in seq:
        o = ops[i]
        if o["eng"] == "R":
            hop = ops[o["after"]]["calls"][0][1][2]
            value[i] = (o["sem"], len(lanes(T.cores[(rank - hop) % NR], core)))
            total[o["sem"]] = value[i][1]
            continue
        for j in need[i]:
            queue[o["eng"]].wait_ge(T.sem[value[j][0]], value[j][1])
        for meth, args, kw in o["calls"]:
            if meth == "remote":
                to = T.cores[(rank + args[2]) % NR]
                rid, pid = topo.addr(to, core)
                use = lanes(core, to)
                g.remote_dma(view(args[0]), view(args[1]), T.sem[args[3]], T.sem["sent"], pid, rid, sum(1 << e for e in use))
                total["sent"] = total.get("sent", 0) + len(use)
            else:
                ins = call[o["eng"]][meth](*[view(x) for x in args], **{k: view(x) for k, x in kw.items()})
        if o.get("sem") == "sent":
            continue
        if "sem" in o or i in marked:
            sem, n = (o["sem"], 16) if "sem" in o else ("e" + o["eng"], 1)
            ins.then_inc(T.sem[sem], n)
            total[sem] = total.get(sem, 0) + n
            value[i] = (sem, total[sem])
    for sem, n in total.items():
        g.wait_ge(T.sem[sem], n)
